import numpy as np
import ml_dtypes


def mxq(x, axis, fmt="e4m3"):
    dtype, down = {"e4m3": (ml_dtypes.float8_e4m3fn, 7), "e5m2": (ml_dtypes.float8_e5m2, 14)}[fmt]
    v = np.moveaxis(np.asarray(x, np.float32).astype(ml_dtypes.bfloat16).astype(np.float64), axis, -1)
    blocks = v.reshape(v.shape[:-1] + (-1, 32))
    amax = np.abs(blocks).max(-1, keepdims=True)
    byte = np.maximum(np.where(amax > 0, np.frexp(amax)[1] - 1 + 127, 0) - down, 1)
    scale = np.exp2(byte - 127.0)
    codes = (blocks / scale).astype(np.float32).astype(dtype).astype(np.float64)
    return np.moveaxis((codes * scale).reshape(v.shape), -1, axis)


WIDE = False


def mx_kscale(k):
    if not WIDE:
        return np.ones(k)
    levels = np.array([10, -10, 5, -5, 0])
    if k % 512:
        return np.exp2(np.random.permutation(np.resize(levels, k // 32))).repeat(32)
    a = np.empty((k // 512, 16))
    for p in range(k // 512):
        a[p, :8] = np.random.permutation(np.resize(levels, 8))
        for g in range(8):
            far = levels[np.abs(levels - a[p, g]) >= 10]
            a[p, g + 8] = far[np.random.randint(len(far))]
    return np.exp2(a.ravel()).repeat(32)


def f64(x):
    return np.asarray(x).astype(np.float64)


def striped(idx):
    return np.tile(idx.reshape(-1, 16).T, (8, 1)).astype(np.uint16)


def unstriped(offs):
    return offs[:16].T.reshape(-1).astype(np.int64)


E2M1 = np.array([0.0, 0.5, 1.0, 1.5, 2.0, 3.0, 4.0, 6.0, -0.0, -0.5, -1.0, -1.5, -2.0, -3.0, -4.0, -6.0])


def pack_weight(w, fmt):
    k, n = w.shape
    w = f64(np.asarray(w, np.float32).astype(ml_dtypes.bfloat16)).reshape(k // 32, 32, n)
    amax = np.abs(w).max(1)
    if fmt == "e4m3":
        byte = np.frexp(amax)[1] - 1 + 127 - 7
    else:
        mant, ex = np.frexp(amax / 6.0)
        byte = np.where(mant > 0.5, ex, ex - 1) + 127
    byte = np.clip(np.where(amax > 0, byte, 1), 1, 254)
    scaled = (w * np.exp2(127.0 - byte)[:, None, :]).reshape(k, n).astype(np.float32)
    by_word = np.ascontiguousarray(scaled.reshape(k // 512, 128, 4, n).transpose(0, 1, 3, 2))
    if fmt == "e4m3":
        words = by_word.astype(ml_dtypes.float8_e4m3fn).view(np.uint8)
    else:
        c = by_word.astype(ml_dtypes.float4_e2m1fn).view(np.uint8) & 0xF
        words = (c[..., 0::2] | (c[..., 1::2] << 4)).reshape(k // 512, 128, 2 * n)
    return np.ascontiguousarray(words), np.ascontiguousarray(byte.astype(np.uint8).reshape(k // 512, 16, n))


def unpack_weight(words, scales, fmt):
    g, _, n = scales.shape
    words = np.ascontiguousarray(words).reshape(g, 128, n, -1)
    if fmt == "e4m3":
        vals = words.view(ml_dtypes.float8_e4m3fn).astype(np.float64)
    else:
        nib = np.empty((g, 128, n, 4), np.uint8)
        nib[..., 0::2] = words & 0xF
        nib[..., 1::2] = words >> 4
        vals = E2M1[nib]
    vals = vals * np.repeat(np.exp2(scales.astype(np.float64) - 127.0), 8, axis=1)[..., None]
    return vals.transpose(0, 1, 3, 2).reshape(g * 512, n)


def gelu(v):
    return 0.5 * v * (1.0 + np.tanh(np.sqrt(2.0 / np.pi) * (v + 0.044715 * v**3)))


K, H, N, T, S = 1024, 1024, 384, 4096, 1024


def setup_inputs():
    n = np.random.standard_normal
    s = mx_kscale(K)[:, None]
    u = mx_kscale(H)[:, None]
    tab_words, tab_scales = pack_weight(n((K, T)) * s, "e4m3")
    wc_words, wc_scales = pack_weight(n((K, H)) / np.sqrt(K) / s, "e2m1")
    wr_words, wr_scales = pack_weight(1.5 * n((H, N)) / np.sqrt(H) / u, "e4m3")
    return {
        "tab_words": tab_words, "tab_scales": tab_scales,
        "offs": striped(np.random.permutation(T)[:S]),
        "wd": (n((K, H)) / np.sqrt(K) / s).astype(np.float32),
        "wc_words": wc_words, "wc_scales": wc_scales,
        "gain": (np.exp(0.2 * n(H)) * u[:, 0]).astype(np.float32),
        "wr_words": wr_words, "wr_scales": wr_scales,
    }


def reference(tab_words, tab_scales, offs, wd, wc_words, wc_scales, gain, wr_words, wr_scales):
    v = unpack_weight(tab_words, tab_scales, "e4m3")[:, unstriped(offs)]
    wdq = mxq(f64(wd), 0, "e4m3")
    wc = unpack_weight(wc_words, wc_scales, "e2m1")
    wr = unpack_weight(wr_words, wr_scales, "e4m3")
    d = wdq.T @ v
    c = wc.T @ v
    density = np.log1p(np.exp(d))
    colour = np.tanh(c) * f64(gain)[:, None]
    h = mxq(density * colour, 0, "e4m3")
    return wr.T @ h

@@ -1,0 +1,247 @@
+from contextlib import ExitStack
+
+import concourse.mybir as mybir
+
+K, H, N, T, S = 1024, 1024, 384, 4096, 1024
+FLOPS = 2 * (2 * K * H * S + H * N * S)
+
+F32 = mybir.dt.float32
+BF16 = mybir.dt.bfloat16
+I32 = mybir.dt.int32
+U32 = mybir.dt.uint32
+U16 = mybir.dt.uint16
+U8 = mybir.dt.uint8
+FP8X4 = mybir.dt.float8_e4m3fn_x4
+FP4X4 = mybir.dt.float4_e2m1fn_x4
+ACT = mybir.ActivationFunctionType
+ALU = mybir.AluOpType
+
+P = 128
+PACK = 4
+GROUP = P * PACK
+HALF = 512
+CHUNK = 128
+PIECE = 256
+LINEAR_FROM = 30.0
+
+
+def tile_list_voxel_radiance_field_kernel(
+    tc, tab_words, tab_scales, offs, wd, wc_words, wc_scales, gain, wr_words, wr_scales, out
+):
+    nc = tc.nc
+    with ExitStack() as ctx:
+        keep = ctx.enter_context(tc.tile_pool(name="keep", bufs=1))
+        stage = ctx.enter_context(tc.tile_pool(name="stage", bufs=2))
+        ring = ctx.enter_context(tc.tile_pool(name="ring", bufs=3))
+        psum = ctx.enter_context(tc.psum_pool(name="psum", bufs=1))
+
+        offsets = keep.tile([P, S // 16], U16, name="offsets")
+        nc.sync.dma_start(offsets[:], offs)
+
+        banks = [psum.tile([P, HALF], F32, name=f"bank{i}") for i in range(8)]
+
+        warm = keep.tile([P, 1], F32, name="warm", tag="tab_w0", align_bytes=64)
+        warm_out = keep.tile([P, 1], F32, name="warm_out", tag="tab_w1", align_bytes=64)
+        tab_s = keep.tile([P, 2, T // 4], I32, name="tab_s", align_bytes=64)
+        wc_s_raw = keep.tile([P, 2, H // 4], I32, name="wc_s_raw", align_bytes=64)
+        nc.vector.memset(tab_s[:], 0)
+        nc.vector.memset(wc_s_raw[:], 0)
+        nc.vector.memset(warm[:], 0.0)
+        nc.scalar.activation(warm_out[:], warm[:], ACT.Tanh)
+        wc_raw = []
+        for a in range(2):
+            raw = stage.tile([P, H // 2], I32, name="stage", align_bytes=64)
+            nc.sync.dma_start(raw[:], wc_words[a].bitcast(I32))
+            wc_raw.append(raw)
+        for q in range(4):
+            nc.sync.dma_start(
+                tab_s[32 * q : 32 * q + 4, :, :],
+                tab_scales[:, 4 * q : 4 * q + 4, :].rearrange("a r t -> r a t").bitcast(I32),
+            )
+        for q in range(4):
+            nc.sync.dma_start(
+                wc_s_raw[32 * q : 32 * q + 4, :, :],
+                wc_scales[:, 4 * q : 4 * q + 4, :].rearrange("a r e -> r a e").bitcast(I32),
+            )
+        gains = keep.tile([P, 2, PACK], F32, name="gains")
+        nc.sync.dma_start(gains[:], gain.rearrange("(b p t) -> p b t", b=2, t=PACK))
+        tab_w = []
+        for a in range(2):
+            words = keep.tile([P, T], I32, name=f"tab_w{a}", tag=f"tab_w{a}", align_bytes=64)
+            nc.sync.dma_start(words[:], tab_words[a].rearrange("p t i -> p (t i)").bitcast(I32))
+            tab_w.append(words)
+
+        wc_q = keep.tile([P, 2, 2 * H], U8, name="wc_q", align_bytes=64)
+        wc_s = keep.tile([P, 2, H], U8, name="wc_s", align_bytes=64)
+        for a in range(2):
+            nc.vector.tensor_copy(
+                out=wc_q[:, a, :].bitcast(U16).rearrange("p (b t m) -> p b m t", b=2, t=PACK),
+                in_=wc_raw[a][:].bitcast(U16).rearrange("p (b m t) -> p b m t", b=2, t=PACK),
+            )
+
+        v_w = [keep.tile([P, S], U32, name=f"v_w{a}", align_bytes=64) for a in range(2)]
+        v_s = keep.tile([P, 2, S], U8, name="v_s", align_bytes=64)
+
+        def gather(jh):
+            cols = slice(jh * HALF, (jh + 1) * HALF)
+            lst = offsets[:, jh * HALF // 16 : (jh + 1) * HALF // 16]
+            for a in range(2):
+                nc.vector.tensor_copy(v_s[:, a, cols], tab_s[:, a, :].bitcast(U8).indirect(lst))
+            for a in range(2):
+                nc.vector.tensor_copy(v_w[a][:, cols], tab_w[a][:].bitcast(U32).indirect(lst))
+
+        gather(0)
+        for a in range(2):
+            nc.vector.tensor_copy(
+                out=wc_s[:, a, :].rearrange("p (b t m) -> p b m t", b=2, t=PACK),
+                in_=wc_s_raw[:, a, :].bitcast(U8).rearrange("p (b m t) -> p b m t", b=2, t=PACK),
+            )
+        gather(1)
+
+        wd_q = keep.tile([P, 2, H], U32, name="wd_q", align_bytes=64)
+        wd_s = keep.tile([P, 2, H], U8, name="wd_s", align_bytes=64)
+
+        def quantise_wd(b):
+            grouped = []
+            for a in range(2):
+                raw = stage.tile([P, PACK, GROUP], F32, name="stage", align_bytes=64)
+                nc.sync.dma_start(
+                    raw[:],
+                    wd[a * GROUP : (a + 1) * GROUP, b * GROUP : (b + 1) * GROUP].rearrange("(p i) e -> p i e", i=PACK),
+                )
+                g = ring.tile([P, PACK * GROUP], BF16, name="bf", align_bytes=64)
+                nc.vector.tensor_copy(
+                    out=g[:].rearrange("p (t m i) -> p m i t", t=PACK, i=PACK),
+                    in_=raw[:].rearrange("p i (m t) -> p m i t", t=PACK),
+                )
+                grouped.append(g)
+            for a in range(2):
+                cols = slice(b * GROUP, (b + 1) * GROUP)
+                nc.vector.quantize_mx(out=wd_q[:, a, cols].bitcast(FP8X4), scales=wd_s[:, a, cols], in_=grouped[a][:])
+
+        def product(dst, b, t, js, colour):
+            c0 = b * GROUP + t * P
+            for a in range(2):
+                if colour:
+                    lhs = wc_q[:, a, 2 * c0 : 2 * (c0 + P)].bitcast(FP4X4)
+                    lhs_s = wc_s[:, a, c0 : c0 + P]
+                else:
+                    lhs = wd_q[:, a, c0 : c0 + P].bitcast(FP8X4)
+                    lhs_s = wd_s[:, a, c0 : c0 + P]
+                nc.tensor.matmul_mx(
+                    out=dst, lhsT=lhs, lhsT_scale=lhs_s,
+                    rhs=v_w[a][:, js].bitcast(FP8X4), rhs_scale=v_s[:, a, js],
+                    start=(a == 0), stop=(a == 1),
+                )
+
+        tiles = [(jh, t) for jh in range(2) for t in range(PACK)]
+        dens = [keep.tile([P, 2, PACK, HALF], F32, name=f"dens{b}") for b in range(2)]
+        ones = [keep.tile([P, 1], F32, name=f"one{b}") for b in range(2)]
+        col0 = keep.tile([P, 2, PACK, HALF], F32, name="col0")
+        h_q = keep.tile([P, 2, S], U32, name="h_q", align_bytes=64)
+        h_s = keep.tile([P, 2, S], U8, name="h_s", align_bytes=64)
+
+        def exponentials(b):
+            for i, (jh, t) in enumerate(tiles):
+                product(banks[i][:], b, t, slice(jh * HALF, (jh + 1) * HALF), False)
+                nc.scalar.activation(dens[b][:, jh, t, :], banks[i][:], ACT.Exp)
+            nc.scalar.activation(ones[b][:], dens[b][:, 1, PACK - 1, 0:1], ACT.Sign, bias=1.0)
+
+        def softplus(b):
+            for i, (jh, t) in enumerate(tiles):
+                x = dens[b][:, jh, t, :]
+                nc.scalar.activation(x, x, ACT.Ln, bias=ones[b][:])
+                nc.vector.scalar_tensor_tensor(
+                    out=x, in0=x, scalar=LINEAR_FROM, in1=banks[i][:], op0=ALU.min, op1=ALU.max
+                )
+
+        def quantise_h(b, js, g):
+            nc.vector.quantize_mx(out=h_q[:, b, js].bitcast(FP8X4), scales=h_s[:, b, js], in_=g)
+
+        quantise_wd(0)
+        for i, (jh, t) in enumerate(tiles):
+            product(banks[i][:], 0, t, slice(jh * HALF, (jh + 1) * HALF), True)
+            nc.scalar.activation(col0[:, jh, t, :], banks[i][:], ACT.Tanh)
+        exponentials(0)
+        quantise_wd(1)
+        for jh, t in tiles:
+            x = col0[:, jh, t, :]
+            nc.vector.tensor_scalar(out=x, in0=x, scalar1=gains[:, 0, t : t + 1], scalar2=None, op0=ALU.mult)
+
+        wr_q = keep.tile([P, 2, N], I32, name="wr_q", tag="tab_w0", align_bytes=64)
+        wr_s = keep.tile([P, 2, N // 4], I32, name="wr_s", tag="tab_w1", align_bytes=64)
+        nc.sync.dma_start(wr_q[:], wr_words.rearrange("a p n i -> p a (n i)").bitcast(I32))
+        nc.vector.memset(wr_s[:], 0)
+        for q in range(4):
+            nc.sync.dma_start(
+                wr_s[32 * q : 32 * q + 4, :, :],
+                wr_scales[:, 4 * q : 4 * q + 4, :].rearrange("a r n -> r a n").bitcast(I32),
+            )
+
+        softplus(0)
+        pending = None
+        for j0 in range(0, S, PIECE):
+            jh, lo = divmod(j0, HALF)
+            g = ring.tile([P, PACK * PIECE], BF16, name="bf", align_bytes=64)
+            nc.vector.tensor_tensor(
+                out=g[:].rearrange("p (c i t) -> p c t i", i=4, t=PACK),
+                in0=dens[0][:, jh, :, lo : lo + PIECE].rearrange("p t (c i) -> p c t i", i=4),
+                in1=col0[:, jh, :, lo : lo + PIECE].rearrange("p t (c i) -> p c t i", i=4),
+                op=ALU.mult,
+            )
+            if pending is not None:
+                quantise_h(0, pending[0], pending[1][:])
+            pending = (slice(j0, j0 + PIECE), g)
+        quantise_h(0, pending[0], pending[1][:])
+
+        exponentials(1)
+        softplus(1)
+        for jh, t in tiles:
+            x = dens[1][:, jh, t, :]
+            nc.vector.tensor_scalar(out=x, in0=x, scalar1=gains[:, 1, t : t + 1], scalar2=None, op0=ALU.mult)
+
+        chunks = S // CHUNK
+        col1 = keep.tile([P, chunks, CHUNK, PACK], F32, name="col1")
+        result = keep.tile([P, N // P, S], F32, name="result")
+        out_v = out.rearrange("(n p) j -> p n j", p=P)
+        grouped = {}
+
+        def colour_chunk(q):
+            for t in range(PACK):
+                product(banks[q][:, t * CHUNK : (t + 1) * CHUNK], 1, t, slice(q * CHUNK, (q + 1) * CHUNK), True)
+            nc.scalar.activation(col1[:, q, :, :], banks[q][:].rearrange("p (t j) -> p j t", t=PACK), ACT.Tanh)
+
+        def hidden_chunk(q):
+            jh, lo = divmod(q * CHUNK, HALF)
+            g = ring.tile([P, PACK * CHUNK], BF16, name="bf", align_bytes=64)
+            nc.vector.tensor_tensor(
+                out=g[:].rearrange("p (j t) -> p j t", t=PACK),
+                in0=col1[:, q, :, :],
+                in1=dens[1][:, jh, :, lo : lo + CHUNK].rearrange("p t j -> p j t"),
+                op=ALU.mult,
+            )
+            grouped[q] = g
+
+        def radiance_chunk(q):
+            js = slice(q * CHUNK, (q + 1) * CHUNK)
+            quantise_h(1, js, grouped[q][:])
+            for n in range(N // P):
+                ns = slice(n * P, (n + 1) * P)
+                for b in range(2):
+                    nc.tensor.matmul_mx(
+                        out=banks[q][:, ns],
+                        lhsT=wr_q[:, b, ns].bitcast(FP8X4),
+                        lhsT_scale=wr_s[:, b, :].bitcast(U8)[:, ns],
+                        rhs=h_q[:, b, js].bitcast(FP8X4), rhs_scale=h_s[:, b, js],
+                        start=(b == 0), stop=(b == 1),
+                    )
+            nc.scalar.copy(result[:, :, js], banks[q][:, 0:N].rearrange("p (n j) -> p n j", j=CHUNK))
+            nc.sync.dma_start(out_v[:, :, js], result[:, :, js])
+
+        for step in range(chunks + 3):
+            if step < chunks:
+                colour_chunk(step)
+            if 0 <= step - 2 < chunks:
+                hidden_chunk(step - 2)
+            if 0 <= step - 3 < chunks:
+                radiance_chunk(step - 3)

@@ -22,7 +22,8 @@ GROUP = P * PACK
 HALF = 512
 CHUNK = 128
 PIECE = 256
-LINEAR_FROM = 30.0
+LINEAR_FROM = 32.0
+WIDTHS = (128, 256, 256, 256, 128)
 
 
 def tile_list_voxel_radiance_field_kernel(
@@ -31,7 +32,6 @@ def tile_list_voxel_radiance_field_kernel(
     nc = tc.nc
     with ExitStack() as ctx:
         keep = ctx.enter_context(tc.tile_pool(name="keep", bufs=1))
-        stage = ctx.enter_context(tc.tile_pool(name="stage", bufs=2))
         ring = ctx.enter_context(tc.tile_pool(name="ring", bufs=3))
         psum = ctx.enter_context(tc.psum_pool(name="psum", bufs=1))
 
@@ -42,29 +42,26 @@ def tile_list_voxel_radiance_field_kernel(
 
         warm = keep.tile([P, 1], F32, name="warm", tag="tab_w0", align_bytes=64)
         warm_out = keep.tile([P, 1], F32, name="warm_out", tag="tab_w1", align_bytes=64)
-        tab_s = keep.tile([P, 2, T // 4], I32, name="tab_s", align_bytes=64)
-        wc_s_raw = keep.tile([P, 2, H // 4], I32, name="wc_s_raw", align_bytes=64)
+        tab_s = keep.tile([P, 2, T // 4], I32, name="tab_s", tag="wd10", align_bytes=64)
+        wc_s_raw = keep.tile([P, 2, H // 4], I32, name="wc_s_raw", tag="wd01", align_bytes=64)
         nc.vector.memset(tab_s[:], 0)
-        nc.vector.memset(wc_s_raw[:], 0)
         nc.vector.memset(warm[:], 0.0)
+        nc.vector.memset(wc_s_raw[:], 0)
         nc.scalar.activation(warm_out[:], warm[:], ACT.Tanh)
-        wc_raw = []
-        for a in range(2):
-            raw = stage.tile([P, H // 2], I32, name="stage", align_bytes=64)
-            nc.sync.dma_start(raw[:], wc_words[a].bitcast(I32))
-            wc_raw.append(raw)
+        wc_raw = keep.tile([P, 2, H // 2], I32, name="wc_raw", tag="wd00", align_bytes=64)
+        nc.sync.dma_start(wc_raw[:], wc_words.rearrange("a p e -> p a e").bitcast(I32))
         for q in range(4):
             nc.sync.dma_start(
                 tab_s[32 * q : 32 * q + 4, :, :],
                 tab_scales[:, 4 * q : 4 * q + 4, :].rearrange("a r t -> r a t").bitcast(I32),
             )
         for q in range(4):
-            nc.sync.dma_start(
+            nc.scalar.dma_start(
                 wc_s_raw[32 * q : 32 * q + 4, :, :],
                 wc_scales[:, 4 * q : 4 * q + 4, :].rearrange("a r e -> r a e").bitcast(I32),
             )
         gains = keep.tile([P, 2, PACK], F32, name="gains")
-        nc.sync.dma_start(gains[:], gain.rearrange("(b p t) -> p b t", b=2, t=PACK))
+        nc.scalar.dma_start(gains[:], gain.rearrange("(b p t) -> p b t", b=2, t=PACK))
         tab_w = []
         for a in range(2):
             words = keep.tile([P, T], I32, name=f"tab_w{a}", tag=f"tab_w{a}", align_bytes=64)
@@ -76,7 +73,7 @@ def tile_list_voxel_radiance_field_kernel(
         for a in range(2):
             nc.vector.tensor_copy(
                 out=wc_q[:, a, :].bitcast(U16).rearrange("p (b t m) -> p b m t", b=2, t=PACK),
-                in_=wc_raw[a][:].bitcast(U16).rearrange("p (b m t) -> p b m t", b=2, t=PACK),
+                in_=wc_raw[:, a, :].bitcast(U16).rearrange("p (b m t) -> p b m t", b=2, t=PACK),
             )
 
         v_w = [keep.tile([P, S], U32, name=f"v_w{a}", align_bytes=64) for a in range(2)]
@@ -90,13 +87,17 @@ def tile_list_voxel_radiance_field_kernel(
             for a in range(2):
                 nc.vector.tensor_copy(v_w[a][:, cols], tab_w[a][:].bitcast(U32).indirect(lst))
 
-        gather(0)
-        for a in range(2):
+        def reorder_wc_scales(b):
+            cols = slice(b * GROUP, (b + 1) * GROUP)
             nc.vector.tensor_copy(
-                out=wc_s[:, a, :].rearrange("p (b t m) -> p b m t", b=2, t=PACK),
-                in_=wc_s_raw[:, a, :].bitcast(U8).rearrange("p (b m t) -> p b m t", b=2, t=PACK),
+                out=wc_s[:, :, cols].rearrange("p a (t m) -> p a m t", t=PACK),
+                in_=wc_s_raw[:].bitcast(U8)[:, :, cols].rearrange("p a (m t) -> p a m t", t=PACK),
             )
+
+        reorder_wc_scales(0)
+        gather(0)
         gather(1)
+        reorder_wc_scales(1)
 
         wd_q = keep.tile([P, 2, H], U32, name="wd_q", align_bytes=64)
         wd_s = keep.tile([P, 2, H], U8, name="wd_s", align_bytes=64)
@@ -104,7 +105,7 @@ def tile_list_voxel_radiance_field_kernel(
         def quantise_wd(b):
             grouped = []
             for a in range(2):
-                raw = stage.tile([P, PACK, GROUP], F32, name="stage", align_bytes=64)
+                raw = keep.tile([P, PACK, GROUP], F32, name="wd_raw", tag=("wd00", "wd10", "wd01", "tab_w0")[2 * b + a], align_bytes=64)
                 nc.sync.dma_start(
                     raw[:],
                     wd[a * GROUP : (a + 1) * GROUP, b * GROUP : (b + 1) * GROUP].rearrange("(p i) e -> p i e", i=PACK),
@@ -134,42 +135,35 @@ def tile_list_voxel_radiance_field_kernel(
                     start=(a == 0), stop=(a == 1),
                 )
 
-        tiles = [(jh, t) for jh in range(2) for t in range(PACK)]
-        dens = [keep.tile([P, 2, PACK, HALF], F32, name=f"dens{b}") for b in range(2)]
-        ones = [keep.tile([P, 1], F32, name=f"one{b}") for b in range(2)]
-        col0 = keep.tile([P, 2, PACK, HALF], F32, name="col0")
+        tiles = [(b, jh, t) for b in range(2) for jh in range(2) for t in range(PACK)]
+        dens = keep.tile([P, 2, PACK, S], F32, name="dens")
+        col = keep.tile([P, 2, PACK, S], F32, name="col")
+        one = keep.tile([P, 1], F32, name="one")
         h_q = keep.tile([P, 2, S], U32, name="h_q", align_bytes=64)
         h_s = keep.tile([P, 2, S], U8, name="h_s", align_bytes=64)
 
-        def exponentials(b):
-            for i, (jh, t) in enumerate(tiles):
-                product(banks[i][:], b, t, slice(jh * HALF, (jh + 1) * HALF), False)
-                nc.scalar.activation(dens[b][:, jh, t, :], banks[i][:], ACT.Exp)
-            nc.scalar.activation(ones[b][:], dens[b][:, 1, PACK - 1, 0:1], ACT.Sign, bias=1.0)
-
-        def softplus(b):
-            for i, (jh, t) in enumerate(tiles):
-                x = dens[b][:, jh, t, :]
-                nc.scalar.activation(x, x, ACT.Ln, bias=ones[b][:])
-                nc.vector.scalar_tensor_tensor(
-                    out=x, in0=x, scalar=LINEAR_FROM, in1=banks[i][:], op0=ALU.min, op1=ALU.max
-                )
-
-        def quantise_h(b, js, g):
-            nc.vector.quantize_mx(out=h_q[:, b, js].bitcast(FP8X4), scales=h_s[:, b, js], in_=g)
-
         quantise_wd(0)
-        for i, (jh, t) in enumerate(tiles):
-            product(banks[i][:], 0, t, slice(jh * HALF, (jh + 1) * HALF), True)
-            nc.scalar.activation(col0[:, jh, t, :], banks[i][:], ACT.Tanh)
-        exponentials(0)
         quantise_wd(1)
-        for jh, t in tiles:
-            x = col0[:, jh, t, :]
-            nc.vector.tensor_scalar(out=x, in0=x, scalar1=gains[:, 0, t : t + 1], scalar2=None, op0=ALU.mult)
+        for i, (b, jh, t) in enumerate(tiles):
+            js = slice(jh * HALF, (jh + 1) * HALF)
+            product(banks[i % 8][:], b, t, js, True)
+            nc.scalar.activation(col[:, b, t, js], banks[i % 8][:], ACT.Tanh)
+            nc.vector.tensor_scalar(
+                out=col[:, b, t, js], in0=col[:, b, t, js], scalar1=gains[:, b, t : t + 1],
+                scalar2=1.0 / LINEAR_FROM, op0=ALU.mult, op1=ALU.mult,
+            )
+        for i, (b, jh, t) in enumerate(tiles):
+            js = slice(jh * HALF, (jh + 1) * HALF)
+            product(banks[i % 8][:], b, t, js, False)
+            nc.scalar.activation(dens[:, b, t, js], banks[i % 8][:], ACT.Exp)
+            nc.vector.scalar_tensor_tensor(
+                out=col[:, b, t, js], in0=banks[i % 8][:], scalar=LINEAR_FROM, in1=col[:, b, t, js],
+                op0=ALU.max, op1=ALU.mult,
+            )
+        nc.scalar.activation(one[:], dens[:, 1, PACK - 1, S - 1 : S], ACT.Sign, bias=1.0)
 
-        wr_q = keep.tile([P, 2, N], I32, name="wr_q", tag="tab_w0", align_bytes=64)
-        wr_s = keep.tile([P, 2, N // 4], I32, name="wr_s", tag="tab_w1", align_bytes=64)
+        wr_q = keep.tile([P, 2, N], I32, name="wr_q", tag="tab_w1", align_bytes=64)
+        wr_s = keep.tile([P, 2, N // 4], I32, name="wr_s", tag="wd00", align_bytes=64)
         nc.sync.dma_start(wr_q[:], wr_words.rearrange("a p n i -> p a (n i)").bitcast(I32))
         nc.vector.memset(wr_s[:], 0)
         for q in range(4):
@@ -178,70 +172,58 @@ def tile_list_voxel_radiance_field_kernel(
                 wr_scales[:, 4 * q : 4 * q + 4, :].rearrange("a r n -> r a n").bitcast(I32),
             )
 
-        softplus(0)
-        pending = None
-        for j0 in range(0, S, PIECE):
-            jh, lo = divmod(j0, HALF)
-            g = ring.tile([P, PACK * PIECE], BF16, name="bf", align_bytes=64)
-            nc.vector.tensor_tensor(
-                out=g[:].rearrange("p (c i t) -> p c t i", i=4, t=PACK),
-                in0=dens[0][:, jh, :, lo : lo + PIECE].rearrange("p t (c i) -> p c t i", i=4),
-                in1=col0[:, jh, :, lo : lo + PIECE].rearrange("p t (c i) -> p c t i", i=4),
-                op=ALU.mult,
-            )
-            if pending is not None:
-                quantise_h(0, pending[0], pending[1][:])
-            pending = (slice(j0, j0 + PIECE), g)
-        quantise_h(0, pending[0], pending[1][:])
+        spans = []
+        for w in WIDTHS:
+            lo = spans[-1].stop if spans else 0
+            spans.append(slice(lo, lo + w))
+        for js in spans:
+            for b in range(2):
+                nc.scalar.activation(dens[:, b, :, js], dens[:, b, :, js], ACT.Ln, bias=one[:])
 
-        exponentials(1)
-        softplus(1)
-        for jh, t in tiles:
-            x = dens[1][:, jh, t, :]
-            nc.vector.tensor_scalar(out=x, in0=x, scalar1=gains[:, 1, t : t + 1], scalar2=None, op0=ALU.mult)
-
-        chunks = S // CHUNK
-        col1 = keep.tile([P, chunks, CHUNK, PACK], F32, name="col1")
         result = keep.tile([P, N // P, S], F32, name="result")
         out_v = out.rearrange("(n p) j -> p n j", p=P)
-        grouped = {}
 
-        def colour_chunk(q):
-            for t in range(PACK):
-                product(banks[q][:, t * CHUNK : (t + 1) * CHUNK], 1, t, slice(q * CHUNK, (q + 1) * CHUNK), True)
-            nc.scalar.activation(col1[:, q, :, :], banks[q][:].rearrange("p (t j) -> p j t", t=PACK), ACT.Tanh)
-
-        def hidden_chunk(q):
-            jh, lo = divmod(q * CHUNK, HALF)
-            g = ring.tile([P, PACK * CHUNK], BF16, name="bf", align_bytes=64)
-            nc.vector.tensor_tensor(
+        def hidden(b, js):
+            g = ring.tile([P, PACK * (js.stop - js.start)], BF16, name="bf", align_bytes=64)
+            nc.vector.scalar_tensor_tensor(
                 out=g[:].rearrange("p (j t) -> p j t", t=PACK),
-                in0=col1[:, q, :, :],
-                in1=dens[1][:, jh, :, lo : lo + CHUNK].rearrange("p t j -> p j t"),
-                op=ALU.mult,
+                in0=dens[:, b, :, js].rearrange("p t j -> p j t"),
+                scalar=LINEAR_FROM,
+                in1=col[:, b, :, js].rearrange("p t j -> p j t"),
+                op0=ALU.min, op1=ALU.mult,
             )
-            grouped[q] = g
+            return g
 
-        def radiance_chunk(q):
-            js = slice(q * CHUNK, (q + 1) * CHUNK)
-            quantise_h(1, js, grouped[q][:])
-            for n in range(N // P):
-                ns = slice(n * P, (n + 1) * P)
-                for b in range(2):
-                    nc.tensor.matmul_mx(
-                        out=banks[q][:, ns],
-                        lhsT=wr_q[:, b, ns].bitcast(FP8X4),
-                        lhsT_scale=wr_s[:, b, :].bitcast(U8)[:, ns],
-                        rhs=h_q[:, b, js].bitcast(FP8X4), rhs_scale=h_s[:, b, js],
-                        start=(b == 0), stop=(b == 1),
-                    )
-            nc.scalar.copy(result[:, :, js], banks[q][:, 0:N].rearrange("p (n j) -> p n j", j=CHUNK))
+        def finish(c, b, g):
+            js = spans[c]
+            w = js.stop - js.start
+            nc.vector.quantize_mx(out=h_q[:, b, js].bitcast(FP8X4), scales=h_s[:, b, js], in_=g[:])
+            if b == 0:
+                return
+            per_bank = HALF // w
+            for n0 in range(0, N // P, per_bank):
+                count = min(per_bank, N // P - n0)
+                bank = banks[(2 * c + n0 // per_bank) % 8]
+                for n in range(n0, n0 + count):
+                    ns = slice(n * P, (n + 1) * P)
+                    for a in range(2):
+                        nc.tensor.matmul_mx(
+                            out=bank[:, (n - n0) * w : (n - n0 + 1) * w],
+                            lhsT=wr_q[:, a, ns].bitcast(FP8X4),
+                            lhsT_scale=wr_s[:, a, :].bitcast(U8)[:, ns],
+                            rhs=h_q[:, a, js].bitcast(FP8X4), rhs_scale=h_s[:, a, js],
+                            start=(a == 0), stop=(a == 1),
+                        )
+                nc.scalar.copy(
+                    result[:, n0 : n0 + count, js], bank[:, 0 : count * w].rearrange("p (n j) -> p n j", j=w)
+                )
             nc.sync.dma_start(out_v[:, :, js], result[:, :, js])
 
-        for step in range(chunks + 3):
-            if step < chunks:
-                colour_chunk(step)
-            if 0 <= step - 2 < chunks:
-                hidden_chunk(step - 2)
-            if 0 <= step - 3 < chunks:
-                radiance_chunk(step - 3)
+        pending = None
+        for c in range(len(spans)):
+            for b in range(2):
+                g = hidden(b, spans[c])
+                if pending is not None:
+                    finish(*pending)
+                pending = (c, b, g)
+        finish(*pending)

@@ -22,6 +22,7 @@ GROUP = P * PACK
 HALF = 512
 CHUNK = 128
 PIECE = 256
+RUN = 4
 LINEAR_FROM = 32.0
 WIDTHS = (128, 256, 256, 256, 128)
 
@@ -136,31 +137,36 @@ def tile_list_voxel_radiance_field_kernel(
                 )
 
         tiles = [(b, jh, t) for b in range(2) for jh in range(2) for t in range(PACK)]
-        dens = keep.tile([P, 2, PACK, S], F32, name="dens")
-        col = keep.tile([P, 2, PACK, S], F32, name="col")
+        dens = keep.tile([P, 2, S // RUN, PACK, RUN], F32, name="dens", align_bytes=64)
+        col = keep.tile([P, 2, S // RUN, PACK, RUN], F32, name="col", align_bytes=64)
         one = keep.tile([P, 1], F32, name="one")
         h_q = keep.tile([P, 2, S], U32, name="h_q", align_bytes=64)
         h_s = keep.tile([P, 2, S], U8, name="h_s", align_bytes=64)
 
         quantise_wd(0)
         quantise_wd(1)
+        def rows(tile, b, jh, t):
+            return tile[:, b, jh * HALF // RUN : (jh + 1) * HALF // RUN, t, :]
+
         for i, (b, jh, t) in enumerate(tiles):
-            js = slice(jh * HALF, (jh + 1) * HALF)
-            product(banks[i % 8][:], b, t, js, True)
-            nc.scalar.activation(col[:, b, t, js], banks[i % 8][:], ACT.Tanh)
+            bank = banks[i % 8]
+            product(bank[:], b, t, slice(jh * HALF, (jh + 1) * HALF), True)
+            x = rows(col, b, jh, t)
+            nc.scalar.activation(x, bank[:].rearrange("p (c i) -> p c i", i=RUN), ACT.Tanh)
             nc.vector.tensor_scalar(
-                out=col[:, b, t, js], in0=col[:, b, t, js], scalar1=gains[:, b, t : t + 1],
+                out=x, in0=x, scalar1=gains[:, b, t : t + 1],
                 scalar2=1.0 / LINEAR_FROM, op0=ALU.mult, op1=ALU.mult,
             )
         for i, (b, jh, t) in enumerate(tiles):
-            js = slice(jh * HALF, (jh + 1) * HALF)
-            product(banks[i % 8][:], b, t, js, False)
-            nc.scalar.activation(dens[:, b, t, js], banks[i % 8][:], ACT.Exp)
+            bank = banks[i % 8]
+            product(bank[:], b, t, slice(jh * HALF, (jh + 1) * HALF), False)
+            logits = bank[:].rearrange("p (c i) -> p c i", i=RUN)
+            nc.scalar.activation(rows(dens, b, jh, t), logits, ACT.Exp)
+            x = rows(col, b, jh, t)
             nc.vector.scalar_tensor_tensor(
-                out=col[:, b, t, js], in0=banks[i % 8][:], scalar=LINEAR_FROM, in1=col[:, b, t, js],
-                op0=ALU.max, op1=ALU.mult,
+                out=x, in0=logits, scalar=LINEAR_FROM, in1=x, op0=ALU.max, op1=ALU.mult,
             )
-        nc.scalar.activation(one[:], dens[:, 1, PACK - 1, S - 1 : S], ACT.Sign, bias=1.0)
+        nc.scalar.activation(one[:], dens[:, 1, S // RUN - 1, PACK - 1, 0:1], ACT.Sign, bias=1.0)
 
         wr_q = keep.tile([P, 2, N], I32, name="wr_q", tag="tab_w1", align_bytes=64)
         wr_s = keep.tile([P, 2, N // 4], I32, name="wr_s", tag="wd00", align_bytes=64)
@@ -172,13 +178,17 @@ def tile_list_voxel_radiance_field_kernel(
                 wr_scales[:, 4 * q : 4 * q + 4, :].rearrange("a r n -> r a n").bitcast(I32),
             )
 
+        def flat(tile, b, js):
+            return tile[:, b, js.start // RUN : js.stop // RUN, :, :].rearrange("p c t i -> p (c t) i")
+
         spans = []
         for w in WIDTHS:
             lo = spans[-1].stop if spans else 0
             spans.append(slice(lo, lo + w))
         for js in spans:
             for b in range(2):
-                nc.scalar.activation(dens[:, b, :, js], dens[:, b, :, js], ACT.Ln, bias=one[:])
+                x = flat(dens, b, js)
+                nc.scalar.activation(x, x, ACT.Ln, bias=one[:])
 
         result = keep.tile([P, N // P, S], F32, name="result")
         out_v = out.rearrange("(n p) j -> p n j", p=P)
@@ -186,10 +196,10 @@ def tile_list_voxel_radiance_field_kernel(
         def hidden(b, js):
             g = ring.tile([P, PACK * (js.stop - js.start)], BF16, name="bf", align_bytes=64)
             nc.vector.scalar_tensor_tensor(
-                out=g[:].rearrange("p (j t) -> p j t", t=PACK),
-                in0=dens[:, b, :, js].rearrange("p t j -> p j t"),
+                out=g[:].rearrange("p (i x) -> p x i", i=RUN),
+                in0=flat(dens, b, js),
                 scalar=LINEAR_FROM,
-                in1=col[:, b, :, js].rearrange("p t j -> p j t"),
+                in1=flat(col, b, js),
                 op0=ALU.min, op1=ALU.mult,
             )
             return g
@@ -215,7 +225,8 @@ def tile_list_voxel_radiance_field_kernel(
                             start=(a == 0), stop=(a == 1),
                         )
                 nc.scalar.copy(
-                    result[:, n0 : n0 + count, js], bank[:, 0 : count * w].rearrange("p (n j) -> p n j", j=w)
+                    result[:, n0 : n0 + count, js].rearrange("p n (c i) -> p n c i", i=RUN),
+                    bank[:, 0 : count * w].rearrange("p (n i c) -> p n c i", n=count, i=RUN),
                 )
             nc.sync.dma_start(out_v[:, :, js], result[:, :, js])
 

@@ -43,87 +43,85 @@ def tile_list_voxel_radiance_field_kernel(
 
         warm = keep.tile([P, 1], F32, name="warm", tag="tab_w0", align_bytes=64)
         warm_out = keep.tile([P, 1], F32, name="warm_out", tag="tab_w1", align_bytes=64)
-        tab_s = keep.tile([P, 2, T // 4], I32, name="tab_s", tag="wd10", align_bytes=64)
-        wc_s_raw = keep.tile([P, 2, H // 4], I32, name="wc_s_raw", tag="wd01", align_bytes=64)
+        tab_s = keep.tile([P, T // 4], I32, name="tab_s", tag="gains", align_bytes=64)
+        wc_s_raw = keep.tile([P, 2, H // 4], I32, name="wc_s_raw", align_bytes=64)
+        v_s = keep.tile([P, 2, S // 4], I32, name="v_s", align_bytes=64)
         nc.vector.memset(tab_s[:], 0)
-        nc.vector.memset(warm[:], 0.0)
         nc.vector.memset(wc_s_raw[:], 0)
+        nc.vector.memset(warm[:], 0.0)
+        nc.vector.memset(v_s[:], 0)
         nc.scalar.activation(warm_out[:], warm[:], ACT.Tanh)
-        wc_raw = keep.tile([P, 2, H // 2], I32, name="wc_raw", tag="wd00", align_bytes=64)
+        wc_raw = keep.tile([P, 2, H // 2], I32, name="wc_raw", align_bytes=64)
         nc.sync.dma_start(wc_raw[:], wc_words.rearrange("a p e -> p a e").bitcast(I32))
+        nc.sync.dma_start(tab_s[0:32, :], tab_scales.rearrange("a q t -> (a q) t").bitcast(I32))
         for q in range(4):
             nc.sync.dma_start(
-                tab_s[32 * q : 32 * q + 4, :, :],
-                tab_scales[:, 4 * q : 4 * q + 4, :].rearrange("a r t -> r a t").bitcast(I32),
-            )
-        for q in range(4):
-            nc.scalar.dma_start(
                 wc_s_raw[32 * q : 32 * q + 4, :, :],
                 wc_scales[:, 4 * q : 4 * q + 4, :].rearrange("a r e -> r a e").bitcast(I32),
             )
-        gains = keep.tile([P, 2, PACK], F32, name="gains")
-        nc.scalar.dma_start(gains[:], gain.rearrange("(b p t) -> p b t", b=2, t=PACK))
         tab_w = []
         for a in range(2):
             words = keep.tile([P, T], I32, name=f"tab_w{a}", tag=f"tab_w{a}", align_bytes=64)
             nc.sync.dma_start(words[:], tab_words[a].rearrange("p t i -> p (t i)").bitcast(I32))
             tab_w.append(words)
 
+        picked_s = keep.tile([P, S], U8, name="picked_s", align_bytes=64)
+        nc.vector.tensor_copy(picked_s[:], tab_s[:].bitcast(U8).indirect(offsets[:]))
+        for a in range(2):
+            for q in range(4):
+                queue = nc.gpsimd if (a, q) == (1, 3) else nc.scalar
+                row = 16 * a + 4 * q
+                queue.dma_start(v_s[32 * q : 32 * q + 4, a, :], picked_s[row : row + 4, :].bitcast(I32))
+        gains = keep.tile([P, 2, PACK], F32, name="gains", tag="gains", align_bytes=64)
+        nc.scalar.dma_start(gains[:], gain.rearrange("(b p t) -> p b t", b=2, t=PACK))
+
         wc_q = keep.tile([P, 2, 2 * H], U8, name="wc_q", align_bytes=64)
         wc_s = keep.tile([P, 2, H], U8, name="wc_s", align_bytes=64)
-        for a in range(2):
+        for u in range(2):
+            pair = slice(2 * u, 2 * u + 2)
             nc.vector.tensor_copy(
-                out=wc_q[:, a, :].bitcast(U16).rearrange("p (b t m) -> p b m t", b=2, t=PACK),
-                in_=wc_raw[:, a, :].bitcast(U16).rearrange("p (b m t) -> p b m t", b=2, t=PACK),
+                out=wc_q[:].bitcast(U16).rearrange("p a (b t m) -> p (a b) m t", b=2, t=PACK)[:, :, :, pair],
+                in_=wc_raw[:].bitcast(U16).rearrange("p a (b m t) -> p (a b) m t", b=2, t=PACK)[:, :, :, pair],
+            )
+        for u in range(2):
+            pair = slice(2 * u, 2 * u + 2)
+            nc.vector.tensor_copy(
+                out=wc_s[:].rearrange("p a (b t m) -> p (a b) m t", b=2, t=PACK)[:, :, :, pair],
+                in_=wc_s_raw[:].bitcast(U8).rearrange("p a (b m t) -> p (a b) m t", b=2, t=PACK)[:, :, :, pair],
             )
 
         v_w = [keep.tile([P, S], U32, name=f"v_w{a}", align_bytes=64) for a in range(2)]
-        v_s = keep.tile([P, 2, S], U8, name="v_s", align_bytes=64)
-
-        def gather(jh):
+        for jh in range(2):
             cols = slice(jh * HALF, (jh + 1) * HALF)
             lst = offsets[:, jh * HALF // 16 : (jh + 1) * HALF // 16]
             for a in range(2):
-                nc.vector.tensor_copy(v_s[:, a, cols], tab_s[:, a, :].bitcast(U8).indirect(lst))
-            for a in range(2):
                 nc.vector.tensor_copy(v_w[a][:, cols], tab_w[a][:].bitcast(U32).indirect(lst))
-
-        def reorder_wc_scales(b):
-            cols = slice(b * GROUP, (b + 1) * GROUP)
-            nc.vector.tensor_copy(
-                out=wc_s[:, :, cols].rearrange("p a (t m) -> p a m t", t=PACK),
-                in_=wc_s_raw[:].bitcast(U8)[:, :, cols].rearrange("p a (m t) -> p a m t", t=PACK),
-            )
-
-        reorder_wc_scales(0)
-        gather(0)
-        gather(1)
-        reorder_wc_scales(1)
 
         wd_q = keep.tile([P, 2, H], U32, name="wd_q", align_bytes=64)
         wd_s = keep.tile([P, 2, H], U8, name="wd_s", align_bytes=64)
 
         def quantise_wd(b):
-            grouped = []
+            grouped = keep.tile([P, 2, PACK * GROUP], BF16, name=f"wd_bf{b}", tag=f"wd_bf{b}", align_bytes=64)
+            both = keep.tile([P, 2, PACK, GROUP], F32, name="wd_raw", tag=f"tab_w{b}", align_bytes=64)
             for a in range(2):
-                raw = keep.tile([P, PACK, GROUP], F32, name="wd_raw", tag=("wd00", "wd10", "wd01", "tab_w0")[2 * b + a], align_bytes=64)
+                raw = both[:, a, :, :]
                 nc.sync.dma_start(
-                    raw[:],
+                    raw,
                     wd[a * GROUP : (a + 1) * GROUP, b * GROUP : (b + 1) * GROUP].rearrange("(p i) e -> p i e", i=PACK),
                 )
-                g = ring.tile([P, PACK * GROUP], BF16, name="bf", align_bytes=64)
-                nc.vector.tensor_copy(
-                    out=g[:].rearrange("p (t m i) -> p m i t", t=PACK, i=PACK),
-                    in_=raw[:].rearrange("p i (m t) -> p m i t", t=PACK),
-                )
-                grouped.append(g)
+                for u in range(2):
+                    pair = slice(2 * u, 2 * u + 2)
+                    nc.vector.tensor_copy(
+                        out=grouped[:, a, :].rearrange("p (t m i) -> p m i t", t=PACK, i=PACK)[:, :, :, pair],
+                        in_=raw.rearrange("p i (m t) -> p m i t", t=PACK)[:, :, :, pair],
+                    )
             for a in range(2):
                 cols = slice(b * GROUP, (b + 1) * GROUP)
-                nc.vector.quantize_mx(out=wd_q[:, a, cols].bitcast(FP8X4), scales=wd_s[:, a, cols], in_=grouped[a][:])
+                nc.vector.quantize_mx(out=wd_q[:, a, cols].bitcast(FP8X4), scales=wd_s[:, a, cols], in_=grouped[:, a, :])
 
-        def product(dst, b, t, js, colour):
+        def product(dst, b, t, js, colour, passes=(0, 1)):
             c0 = b * GROUP + t * P
-            for a in range(2):
+            for a in passes:
                 if colour:
                     lhs = wc_q[:, a, 2 * c0 : 2 * (c0 + P)].bitcast(FP4X4)
                     lhs_s = wc_s[:, a, c0 : c0 + P]
@@ -132,7 +130,7 @@ def tile_list_voxel_radiance_field_kernel(
                     lhs_s = wd_s[:, a, c0 : c0 + P]
                 nc.tensor.matmul_mx(
                     out=dst, lhsT=lhs, lhsT_scale=lhs_s,
-                    rhs=v_w[a][:, js].bitcast(FP8X4), rhs_scale=v_s[:, a, js],
+                    rhs=v_w[a][:, js].bitcast(FP8X4), rhs_scale=v_s[:, a, :].bitcast(U8)[:, js],
                     start=(a == 0), stop=(a == 1),
                 )
 
@@ -148,9 +146,11 @@ def tile_list_voxel_radiance_field_kernel(
         def rows(tile, b, jh, t):
             return tile[:, b, jh * HALF // RUN : (jh + 1) * HALF // RUN, t, :]
 
+        for i, (b, jh, t) in enumerate(tiles[:8]):
+            product(banks[i][:], b, t, slice(jh * HALF, (jh + 1) * HALF), True, (0,))
         for i, (b, jh, t) in enumerate(tiles):
             bank = banks[i % 8]
-            product(bank[:], b, t, slice(jh * HALF, (jh + 1) * HALF), True)
+            product(bank[:], b, t, slice(jh * HALF, (jh + 1) * HALF), True, (1,) if i < 8 else (0, 1))
             x = rows(col, b, jh, t)
             nc.scalar.activation(x, bank[:].rearrange("p (c i) -> p c i", i=RUN), ACT.Tanh)
             nc.vector.tensor_scalar(
@@ -168,8 +168,8 @@ def tile_list_voxel_radiance_field_kernel(
             )
         nc.scalar.activation(one[:], dens[:, 1, S // RUN - 1, PACK - 1, 0:1], ACT.Sign, bias=1.0)
 
-        wr_q = keep.tile([P, 2, N], I32, name="wr_q", tag="tab_w1", align_bytes=64)
-        wr_s = keep.tile([P, 2, N // 4], I32, name="wr_s", tag="wd00", align_bytes=64)
+        wr_q = keep.tile([P, 2, N], I32, name="wr_q", tag="wd_bf0", align_bytes=64)
+        wr_s = keep.tile([P, 2, N // 4], I32, name="wr_s", tag="tab_w0", align_bytes=64)
         nc.sync.dma_start(wr_q[:], wr_words.rearrange("a p n i -> p a (n i)").bitcast(I32))
         nc.vector.memset(wr_s[:], 0)
         for q in range(4):
@@ -195,13 +195,15 @@ def tile_list_voxel_radiance_field_kernel(
 
         def hidden(b, js):
             g = ring.tile([P, PACK * (js.stop - js.start)], BF16, name="bf", align_bytes=64)
-            nc.vector.scalar_tensor_tensor(
-                out=g[:].rearrange("p (i x) -> p x i", i=RUN),
-                in0=flat(dens, b, js),
-                scalar=LINEAR_FROM,
-                in1=flat(col, b, js),
-                op0=ALU.min, op1=ALU.mult,
-            )
+            for u in range(2):
+                pair = slice(2 * u, 2 * u + 2)
+                nc.vector.scalar_tensor_tensor(
+                    out=g[:].rearrange("p (i x) -> p x i", i=RUN)[:, :, pair],
+                    in0=flat(dens, b, js)[:, :, pair],
+                    scalar=LINEAR_FROM,
+                    in1=flat(col, b, js)[:, :, pair],
+                    op0=ALU.min, op1=ALU.mult,
+                )
             return g
 
         def finish(c, b, g):

@@ -23,7 +23,9 @@ HALF = 512
 CHUNK = 128
 PIECE = 256
 RUN = 4
-LINEAR_FROM = 32.0
+LINEAR_FROM = 16.0
+LOG_FLOOR = 2.0**-60
+GPSIMD_TILES = 12
 WIDTHS = (128, 256, 256, 256, 128)
 
 
@@ -41,24 +43,25 @@ def tile_list_voxel_radiance_field_kernel(
 
         banks = [psum.tile([P, HALF], F32, name=f"bank{i}") for i in range(8)]
 
-        warm = keep.tile([P, 1], F32, name="warm", tag="tab_w0", align_bytes=64)
+        warm = keep.tile([P, 1], F32, name="warm", align_bytes=64)
         warm_out = keep.tile([P, 1], F32, name="warm_out", tag="tab_w1", align_bytes=64)
         tab_s = keep.tile([P, T // 4], I32, name="tab_s", tag="gains", align_bytes=64)
         wc_s_raw = keep.tile([P, 2, H // 4], I32, name="wc_s_raw", align_bytes=64)
         v_s = keep.tile([P, 2, S // 4], I32, name="v_s", align_bytes=64)
-        nc.vector.memset(tab_s[:], 0)
         nc.vector.memset(wc_s_raw[:], 0)
         nc.vector.memset(warm[:], 0.0)
+        nc.vector.memset(tab_s[32:64, :], 0)
+        nc.vector.memset(tab_s[64:128, :], 0)
         nc.vector.memset(v_s[:], 0)
-        nc.scalar.activation(warm_out[:], warm[:], ACT.Tanh)
         wc_raw = keep.tile([P, 2, H // 2], I32, name="wc_raw", align_bytes=64)
-        nc.sync.dma_start(wc_raw[:], wc_words.rearrange("a p e -> p a e").bitcast(I32))
         nc.sync.dma_start(tab_s[0:32, :], tab_scales.rearrange("a q t -> (a q) t").bitcast(I32))
+        nc.sync.dma_start(wc_raw[:], wc_words.rearrange("a p e -> p a e").bitcast(I32))
         for q in range(4):
-            nc.sync.dma_start(
+            nc.scalar.dma_start(
                 wc_s_raw[32 * q : 32 * q + 4, :, :],
                 wc_scales[:, 4 * q : 4 * q + 4, :].rearrange("a r e -> r a e").bitcast(I32),
             )
+        nc.scalar.activation(warm_out[:], warm[:], ACT.Sigmoid)
         tab_w = []
         for a in range(2):
             words = keep.tile([P, T], I32, name=f"tab_w{a}", tag=f"tab_w{a}", align_bytes=64)
@@ -74,6 +77,10 @@ def tile_list_voxel_radiance_field_kernel(
                 queue.dma_start(v_s[32 * q : 32 * q + 4, a, :], picked_s[row : row + 4, :].bitcast(I32))
         gains = keep.tile([P, 2, PACK], F32, name="gains", tag="gains", align_bytes=64)
         nc.scalar.dma_start(gains[:], gain.rearrange("(b p t) -> p b t", b=2, t=PACK))
+        factor = keep.tile([P, 2, PACK], F32, name="factor", align_bytes=64)
+        nc.gpsimd.tensor_scalar(
+            out=factor[:], in0=gains[:], scalar1=-1.0 / LINEAR_FROM, scalar2=0.0, op0=ALU.mult, op1=ALU.add,
+        )
 
         wc_q = keep.tile([P, 2, 2 * H], U8, name="wc_q", align_bytes=64)
         wc_s = keep.tile([P, 2, H], U8, name="wc_s", align_bytes=64)
@@ -136,7 +143,7 @@ def tile_list_voxel_radiance_field_kernel(
 
         tiles = [(b, jh, t) for b in range(2) for jh in range(2) for t in range(PACK)]
         dens = keep.tile([P, 2, S // RUN, PACK, RUN], F32, name="dens", align_bytes=64)
-        col = keep.tile([P, 2, S // RUN, PACK, RUN], F32, name="col", align_bytes=64)
+        col = keep.tile([P, 2, S // RUN, PACK, 2 * RUN], F32, name="col", align_bytes=64)
         one = keep.tile([P, 1], F32, name="one")
         h_q = keep.tile([P, 2, S], U32, name="h_q", align_bytes=64)
         h_s = keep.tile([P, 2, S], U8, name="h_s", align_bytes=64)
@@ -144,7 +151,7 @@ def tile_list_voxel_radiance_field_kernel(
         quantise_wd(0)
         quantise_wd(1)
         def rows(tile, b, jh, t):
-            return tile[:, b, jh * HALF // RUN : (jh + 1) * HALF // RUN, t, :]
+            return tile[:, b, jh * HALF // RUN : (jh + 1) * HALF // RUN, t, 0:RUN]
 
         for i, (b, jh, t) in enumerate(tiles[:8]):
             product(banks[i][:], b, t, slice(jh * HALF, (jh + 1) * HALF), True, (0,))
@@ -153,20 +160,20 @@ def tile_list_voxel_radiance_field_kernel(
             product(bank[:], b, t, slice(jh * HALF, (jh + 1) * HALF), True, (1,) if i < 8 else (0, 1))
             x = rows(col, b, jh, t)
             nc.scalar.activation(x, bank[:].rearrange("p (c i) -> p c i", i=RUN), ACT.Tanh)
-            nc.vector.tensor_scalar(
-                out=x, in0=x, scalar1=gains[:, b, t : t + 1],
-                scalar2=1.0 / LINEAR_FROM, op0=ALU.mult, op1=ALU.mult,
-            )
         for i, (b, jh, t) in enumerate(tiles):
             bank = banks[i % 8]
             product(bank[:], b, t, slice(jh * HALF, (jh + 1) * HALF), False)
             logits = bank[:].rearrange("p (c i) -> p c i", i=RUN)
-            nc.scalar.activation(rows(dens, b, jh, t), logits, ACT.Exp)
+            nc.scalar.activation(rows(dens, b, jh, t), logits, ACT.Sigmoid, scale=-1.0)
             x = rows(col, b, jh, t)
             nc.vector.scalar_tensor_tensor(
                 out=x, in0=logits, scalar=LINEAR_FROM, in1=x, op0=ALU.max, op1=ALU.mult,
             )
-        nc.scalar.activation(one[:], dens[:, 1, S // RUN - 1, PACK - 1, 0:1], ACT.Sign, bias=1.0)
+            engine = nc.gpsimd if i < GPSIMD_TILES else nc.vector
+            engine.tensor_scalar(
+                out=x, in0=x, scalar1=factor[:, b, t : t + 1], scalar2=0.0, op0=ALU.mult, op1=ALU.add,
+            )
+        nc.scalar.activation(one[:], dens[:, 1, S // RUN - 1, PACK - 1, 0:1], ACT.Copy, scale=0.0, bias=LOG_FLOOR)
 
         wr_q = keep.tile([P, 2, N], I32, name="wr_q", tag="wd_bf0", align_bytes=64)
         wr_s = keep.tile([P, 2, N // 4], I32, name="wr_s", tag="tab_w0", align_bytes=64)
@@ -200,9 +207,9 @@ def tile_list_voxel_radiance_field_kernel(
                 nc.vector.scalar_tensor_tensor(
                     out=g[:].rearrange("p (i x) -> p x i", i=RUN)[:, :, pair],
                     in0=flat(dens, b, js)[:, :, pair],
-                    scalar=LINEAR_FROM,
+                    scalar=-LINEAR_FROM,
                     in1=flat(col, b, js)[:, :, pair],
-                    op0=ALU.min, op1=ALU.mult,
+                    op0=ALU.max, op1=ALU.mult,
                 )
             return g
 

@@ -25,7 +25,6 @@ PIECE = 256
 RUN = 4
 LINEAR_FROM = 16.0
 LOG_FLOOR = 2.0**-60
-GPSIMD_TILES = 12
 WIDTHS = (128, 256, 256, 256, 128)
 
 
@@ -44,11 +43,11 @@ def tile_list_voxel_radiance_field_kernel(
         banks = [psum.tile([P, HALF], F32, name=f"bank{i}") for i in range(8)]
 
         warm = keep.tile([P, 1], F32, name="warm", align_bytes=64)
-        warm_out = keep.tile([P, 1], F32, name="warm_out", tag="tab_w1", align_bytes=64)
+        warm_out = keep.tile([P, 1], F32, name="warm_out", align_bytes=64)
         tab_s = keep.tile([P, T // 4], I32, name="tab_s", tag="gains", align_bytes=64)
         wc_s_raw = keep.tile([P, 2, H // 4], I32, name="wc_s_raw", align_bytes=64)
         v_s = keep.tile([P, 2, S // 4], I32, name="v_s", align_bytes=64)
-        nc.vector.memset(wc_s_raw[:], 0)
+        nc.gpsimd.memset(wc_s_raw[:], 0)
         nc.vector.memset(warm[:], 0.0)
         nc.vector.memset(tab_s[32:64, :], 0)
         nc.vector.memset(tab_s[64:128, :], 0)
@@ -57,7 +56,7 @@ def tile_list_voxel_radiance_field_kernel(
         nc.sync.dma_start(tab_s[0:32, :], tab_scales.rearrange("a q t -> (a q) t").bitcast(I32))
         nc.sync.dma_start(wc_raw[:], wc_words.rearrange("a p e -> p a e").bitcast(I32))
         for q in range(4):
-            nc.scalar.dma_start(
+            nc.gpsimd.dma_start(
                 wc_s_raw[32 * q : 32 * q + 4, :, :],
                 wc_scales[:, 4 * q : 4 * q + 4, :].rearrange("a r e -> r a e").bitcast(I32),
             )
@@ -77,10 +76,6 @@ def tile_list_voxel_radiance_field_kernel(
                 queue.dma_start(v_s[32 * q : 32 * q + 4, a, :], picked_s[row : row + 4, :].bitcast(I32))
         gains = keep.tile([P, 2, PACK], F32, name="gains", tag="gains", align_bytes=64)
         nc.scalar.dma_start(gains[:], gain.rearrange("(b p t) -> p b t", b=2, t=PACK))
-        factor = keep.tile([P, 2, PACK], F32, name="factor", align_bytes=64)
-        nc.gpsimd.tensor_scalar(
-            out=factor[:], in0=gains[:], scalar1=-1.0 / LINEAR_FROM, scalar2=0.0, op0=ALU.mult, op1=ALU.add,
-        )
 
         wc_q = keep.tile([P, 2, 2 * H], U8, name="wc_q", align_bytes=64)
         wc_s = keep.tile([P, 2, H], U8, name="wc_s", align_bytes=64)
@@ -143,7 +138,9 @@ def tile_list_voxel_radiance_field_kernel(
 
         tiles = [(b, jh, t) for b in range(2) for jh in range(2) for t in range(PACK)]
         dens = keep.tile([P, 2, S // RUN, PACK, RUN], F32, name="dens", align_bytes=64)
-        col = keep.tile([P, 2, S // RUN, PACK, 2 * RUN], F32, name="col", align_bytes=64)
+        col = [
+            keep.tile([P, 1, S // RUN, PACK, (b + 1) * RUN], F32, name=f"col{b}", align_bytes=64) for b in range(2)
+        ]
         one = keep.tile([P, 1], F32, name="one")
         h_q = keep.tile([P, 2, S], U32, name="h_q", align_bytes=64)
         h_s = keep.tile([P, 2, S], U8, name="h_s", align_bytes=64)
@@ -158,20 +155,30 @@ def tile_list_voxel_radiance_field_kernel(
         for i, (b, jh, t) in enumerate(tiles):
             bank = banks[i % 8]
             product(bank[:], b, t, slice(jh * HALF, (jh + 1) * HALF), True, (1,) if i < 8 else (0, 1))
-            x = rows(col, b, jh, t)
+            x = rows(col[b], 0, jh, t)
             nc.scalar.activation(x, bank[:].rearrange("p (c i) -> p c i", i=RUN), ACT.Tanh)
+            if b == 0:
+                nc.vector.tensor_scalar(
+                    out=x, in0=x, scalar1=gains[:, b, t : t + 1],
+                    scalar2=-1.0 / LINEAR_FROM, op0=ALU.mult, op1=ALU.mult,
+                )
+        factor = keep.tile([P, PACK], F32, name="factor", tag="wd_bf1", align_bytes=64)
+        nc.gpsimd.tensor_scalar(
+            out=factor[:], in0=gains[:, 1, :], scalar1=-1.0 / LINEAR_FROM, scalar2=0.0, op0=ALU.mult, op1=ALU.add,
+        )
+        for b, jh, t in tiles[8:]:
+            x = rows(col[b], 0, jh, t)
+            nc.gpsimd.tensor_scalar(
+                out=x, in0=x, scalar1=factor[:, t : t + 1], scalar2=0.0, op0=ALU.mult, op1=ALU.add,
+            )
         for i, (b, jh, t) in enumerate(tiles):
             bank = banks[i % 8]
             product(bank[:], b, t, slice(jh * HALF, (jh + 1) * HALF), False)
             logits = bank[:].rearrange("p (c i) -> p c i", i=RUN)
             nc.scalar.activation(rows(dens, b, jh, t), logits, ACT.Sigmoid, scale=-1.0)
-            x = rows(col, b, jh, t)
+            x = rows(col[b], 0, jh, t)
             nc.vector.scalar_tensor_tensor(
                 out=x, in0=logits, scalar=LINEAR_FROM, in1=x, op0=ALU.max, op1=ALU.mult,
-            )
-            engine = nc.gpsimd if i < GPSIMD_TILES else nc.vector
-            engine.tensor_scalar(
-                out=x, in0=x, scalar1=factor[:, b, t : t + 1], scalar2=0.0, op0=ALU.mult, op1=ALU.add,
             )
         nc.scalar.activation(one[:], dens[:, 1, S // RUN - 1, PACK - 1, 0:1], ACT.Copy, scale=0.0, bias=LOG_FLOOR)
 
@@ -208,7 +215,7 @@ def tile_list_voxel_radiance_field_kernel(
                     out=g[:].rearrange("p (i x) -> p x i", i=RUN)[:, :, pair],
                     in0=flat(dens, b, js)[:, :, pair],
                     scalar=-LINEAR_FROM,
-                    in1=flat(col, b, js)[:, :, pair],
+                    in1=flat(col[b], 0, js)[:, :, pair],
                     op0=ALU.max, op1=ALU.mult,
                 )
             return g
@@ -217,6 +224,26 @@ def tile_list_voxel_radiance_field_kernel(
             js = spans[c]
             w = js.stop - js.start
             nc.vector.quantize_mx(out=h_q[:, b, js].bitcast(FP8X4), scales=h_s[:, b, js], in_=g[:])
+            if c == len(spans) - 1:
+                for n in range(N // P):
+                    ns = slice(n * P, (n + 1) * P)
+                    nc.tensor.matmul_mx(
+                        out=banks[n][:, 0:w],
+                        lhsT=wr_q[:, b, ns].bitcast(FP8X4),
+                        lhsT_scale=wr_s[:, b, :].bitcast(U8)[:, ns],
+                        rhs=h_q[:, b, js].bitcast(FP8X4), rhs_scale=h_s[:, b, js],
+                        start=(b == 0), stop=(b == 1),
+                    )
+                    if b == 1:
+                        dst = result[:, n, js].rearrange("p (c i) -> p c i", i=RUN)
+                        src = banks[n][:, 0:w].rearrange("p (i c) -> p c i", i=RUN)
+                        if n == 1:
+                            nc.vector.tensor_copy(dst, src)
+                        else:
+                            nc.scalar.copy(dst, src)
+                if b == 1:
+                    nc.sync.dma_start(out_v[:, :, js], result[:, :, js])
+                return
             if b == 0:
                 return
             per_bank = HALF // w

@@ -23,6 +23,7 @@ HALF = 512
 CHUNK = 128
 PIECE = 256
 RUN = 4
+PIECE_BYTES = 4 * PACK * GROUP
 LINEAR_FROM = 16.0
 LOG_FLOOR = 2.0**-60
 WIDTHS = (128, 256, 256, 256, 128)
@@ -35,6 +36,7 @@ def tile_list_voxel_radiance_field_kernel(
     with ExitStack() as ctx:
         keep = ctx.enter_context(tc.tile_pool(name="keep", bufs=1))
         ring = ctx.enter_context(tc.tile_pool(name="ring", bufs=3))
+        stage = ctx.enter_context(tc.tile_pool(name="stage", bufs=1))
         psum = ctx.enter_context(tc.psum_pool(name="psum", bufs=1))
 
         offsets = keep.tile([P, S // 16], U16, name="offsets")
@@ -63,7 +65,10 @@ def tile_list_voxel_radiance_field_kernel(
         nc.scalar.activation(warm_out[:], warm[:], ACT.Sigmoid)
         tab_w = []
         for a in range(2):
-            words = keep.tile([P, T], I32, name=f"tab_w{a}", tag=f"tab_w{a}", align_bytes=64)
+            if a == 0:
+                words = stage.tile([P, T], I32, name="tab_w0", offset=PIECE_BYTES - 64, align_bytes=64)
+            else:
+                words = keep.tile([P, T], I32, name="tab_w1", tag="tab_w1", align_bytes=64)
             nc.sync.dma_start(words[:], tab_words[a].rearrange("p t i -> p (t i)").bitcast(I32))
             tab_w.append(words)
 
@@ -93,10 +98,10 @@ def tile_list_voxel_radiance_field_kernel(
             )
 
         v_w = [keep.tile([P, S], U32, name=f"v_w{a}", align_bytes=64) for a in range(2)]
-        for jh in range(2):
-            cols = slice(jh * HALF, (jh + 1) * HALF)
-            lst = offsets[:, jh * HALF // 16 : (jh + 1) * HALF // 16]
-            for a in range(2):
+        for a in range(2):
+            for jh in range(2):
+                cols = slice(jh * HALF, (jh + 1) * HALF)
+                lst = offsets[:, jh * HALF // 16 : (jh + 1) * HALF // 16]
                 nc.vector.tensor_copy(v_w[a][:, cols], tab_w[a][:].bitcast(U32).indirect(lst))
 
         wd_q = keep.tile([P, 2, H], U32, name="wd_q", align_bytes=64)
@@ -104,9 +109,15 @@ def tile_list_voxel_radiance_field_kernel(
 
         def quantise_wd(b):
             grouped = keep.tile([P, 2, PACK * GROUP], BF16, name=f"wd_bf{b}", tag=f"wd_bf{b}", align_bytes=64)
-            both = keep.tile([P, 2, PACK, GROUP], F32, name="wd_raw", tag=f"tab_w{b}", align_bytes=64)
             for a in range(2):
-                raw = both[:, a, :, :]
+                piece = 2 * b + a
+                if piece < 3:
+                    whole = stage.tile(
+                        [P, PACK, GROUP], F32, name=f"wd_raw{piece}", offset=piece * PIECE_BYTES, align_bytes=64
+                    )
+                else:
+                    whole = keep.tile([P, PACK, GROUP], F32, name="wd_raw3", tag="tab_w1", align_bytes=64)
+                raw = whole[:]
                 nc.sync.dma_start(
                     raw,
                     wd[a * GROUP : (a + 1) * GROUP, b * GROUP : (b + 1) * GROUP].rearrange("(p i) e -> p i e", i=PACK),
@@ -162,10 +173,11 @@ def tile_list_voxel_radiance_field_kernel(
                     out=x, in0=x, scalar1=gains[:, b, t : t + 1],
                     scalar2=-1.0 / LINEAR_FROM, op0=ALU.mult, op1=ALU.mult,
                 )
-        factor = keep.tile([P, PACK], F32, name="factor", tag="wd_bf1", align_bytes=64)
-        nc.gpsimd.tensor_scalar(
-            out=factor[:], in0=gains[:, 1, :], scalar1=-1.0 / LINEAR_FROM, scalar2=0.0, op0=ALU.mult, op1=ALU.add,
+        factor = keep.tile([P, PACK + 1], F32, name="factor", tag="wd_bf1", align_bytes=64)
+        nc.vector.tensor_scalar(
+            out=factor[:, 0:PACK], in0=gains[:, 1, :], scalar1=-1.0 / LINEAR_FROM, scalar2=None, op0=ALU.mult,
         )
+        nc.vector.memset(factor[:, PACK : PACK + 1], LINEAR_FROM)
         for b, jh, t in tiles[8:]:
             x = rows(col[b], 0, jh, t)
             nc.gpsimd.tensor_scalar(
@@ -178,12 +190,12 @@ def tile_list_voxel_radiance_field_kernel(
             nc.scalar.activation(rows(dens, b, jh, t), logits, ACT.Sigmoid, scale=-1.0)
             x = rows(col[b], 0, jh, t)
             nc.vector.scalar_tensor_tensor(
-                out=x, in0=logits, scalar=LINEAR_FROM, in1=x, op0=ALU.max, op1=ALU.mult,
+                out=x, in0=logits, scalar=factor[:, PACK : PACK + 1], in1=x, op0=ALU.max, op1=ALU.mult,
             )
-        nc.scalar.activation(one[:], dens[:, 1, S // RUN - 1, PACK - 1, 0:1], ACT.Copy, scale=0.0, bias=LOG_FLOOR)
+        nc.scalar.activation(one[:], dens[:, 1, S // RUN - 1, PACK - 3, 0:1], ACT.Copy, scale=0.0, bias=LOG_FLOOR)
 
         wr_q = keep.tile([P, 2, N], I32, name="wr_q", tag="wd_bf0", align_bytes=64)
-        wr_s = keep.tile([P, 2, N // 4], I32, name="wr_s", tag="tab_w0", align_bytes=64)
+        wr_s = stage.tile([P, 2, N // 4], I32, name="wr_s", offset=0, align_bytes=64)
         nc.sync.dma_start(wr_q[:], wr_words.rearrange("a p n i -> p a (n i)").bitcast(I32))
         nc.vector.memset(wr_s[:], 0)
         for q in range(4):

@@ -26,7 +26,8 @@ RUN = 4
 PIECE_BYTES = 4 * PACK * GROUP
 LINEAR_FROM = 16.0
 LOG_FLOOR = 2.0**-60
-WIDTHS = (128, 256, 256, 256, 128)
+WIDTHS = (128, 256, 256, 128, 128, 128)
+FIRST = 64
 
 
 def tile_list_voxel_radiance_field_kernel(
@@ -46,11 +47,11 @@ def tile_list_voxel_radiance_field_kernel(
 
         warm = keep.tile([P, 1], F32, name="warm", align_bytes=64)
         warm_out = keep.tile([P, 1], F32, name="warm_out", align_bytes=64)
-        tab_s = keep.tile([P, T // 4], I32, name="tab_s", tag="gains", align_bytes=64)
+        tab_s = keep.tile([P, T // 4], I32, name="tab_s", tag="tab_w1", align_bytes=64)
         wc_s_raw = keep.tile([P, 2, H // 4], I32, name="wc_s_raw", align_bytes=64)
         v_s = keep.tile([P, 2, S // 4], I32, name="v_s", align_bytes=64)
         nc.gpsimd.memset(wc_s_raw[:], 0)
-        nc.vector.memset(warm[:], 0.0)
+        nc.gpsimd.memset(warm[:], 0.0)
         nc.vector.memset(tab_s[32:64, :], 0)
         nc.vector.memset(tab_s[64:128, :], 0)
         nc.vector.memset(v_s[:], 0)
@@ -58,29 +59,31 @@ def tile_list_voxel_radiance_field_kernel(
         nc.sync.dma_start(tab_s[0:32, :], tab_scales.rearrange("a q t -> (a q) t").bitcast(I32))
         nc.sync.dma_start(wc_raw[:], wc_words.rearrange("a p e -> p a e").bitcast(I32))
         for q in range(4):
-            nc.gpsimd.dma_start(
+            nc.sync.dma_start(
                 wc_s_raw[32 * q : 32 * q + 4, :, :],
                 wc_scales[:, 4 * q : 4 * q + 4, :].rearrange("a r e -> r a e").bitcast(I32),
             )
         nc.scalar.activation(warm_out[:], warm[:], ACT.Sigmoid)
-        tab_w = []
-        for a in range(2):
-            if a == 0:
-                words = stage.tile([P, T], I32, name="tab_w0", offset=PIECE_BYTES - 64, align_bytes=64)
-            else:
-                words = keep.tile([P, T], I32, name="tab_w1", tag="tab_w1", align_bytes=64)
-            nc.sync.dma_start(words[:], tab_words[a].rearrange("p t i -> p (t i)").bitcast(I32))
-            tab_w.append(words)
+        tab_w = [stage.tile([P, T], I32, name="tab_w0", offset=PIECE_BYTES - 64, align_bytes=64)]
+        nc.sync.dma_start(tab_w[0][:], tab_words[0].rearrange("p t i -> p (t i)").bitcast(I32))
 
         picked_s = keep.tile([P, S], U8, name="picked_s", align_bytes=64)
         nc.vector.tensor_copy(picked_s[:], tab_s[:].bitcast(U8).indirect(offsets[:]))
-        for a in range(2):
-            for q in range(4):
-                queue = nc.gpsimd if (a, q) == (1, 3) else nc.scalar
-                row = 16 * a + 4 * q
-                queue.dma_start(v_s[32 * q : 32 * q + 4, a, :], picked_s[row : row + 4, :].bitcast(I32))
-        gains = keep.tile([P, 2, PACK], F32, name="gains", tag="gains", align_bytes=64)
-        nc.scalar.dma_start(gains[:], gain.rearrange("(b p t) -> p b t", b=2, t=PACK))
+        tab_w.append(keep.tile([P, T], I32, name="tab_w1", tag="tab_w1", align_bytes=64))
+        second = tab_words[1].rearrange("p t i -> p (t i)").bitcast(I32)
+
+        def move_rows(a, q):
+            row = 16 * a + 4 * q
+            nc.scalar.dma_start(v_s[32 * q : 32 * q + 4, a, :], picked_s[row : row + 4, :].bitcast(I32))
+
+        for q in range(4):
+            move_rows(0, q)
+        nc.scalar.dma_start(tab_w[1][:, 0 : T // 2], second[:, 0 : T // 2])
+        for q in range(4):
+            move_rows(1, q)
+        nc.scalar.dma_start(tab_w[1][:, T // 2 : T], second[:, T // 2 : T])
+        gains = keep.tile([P, 2, PACK], F32, name="gains", align_bytes=64)
+        nc.gpsimd.dma_start(gains[:], gain.rearrange("(b p t) -> p b t", b=2, t=PACK))
 
         wc_q = keep.tile([P, 2, 2 * H], U8, name="wc_q", align_bytes=64)
         wc_s = keep.tile([P, 2, H], U8, name="wc_s", align_bytes=64)
@@ -150,7 +153,7 @@ def tile_list_voxel_radiance_field_kernel(
         tiles = [(b, jh, t) for b in range(2) for jh in range(2) for t in range(PACK)]
         dens = keep.tile([P, 2, S // RUN, PACK, RUN], F32, name="dens", align_bytes=64)
         col = [
-            keep.tile([P, 1, S // RUN, PACK, (b + 1) * RUN], F32, name=f"col{b}", align_bytes=64) for b in range(2)
+            keep.tile([P, 1, S // RUN, PACK, 2 * RUN], F32, name=f"col{b}", align_bytes=64) for b in range(2)
         ]
         one = keep.tile([P, 1], F32, name="one")
         h_q = keep.tile([P, 2, S], U32, name="h_q", align_bytes=64)
@@ -168,21 +171,25 @@ def tile_list_voxel_radiance_field_kernel(
             product(bank[:], b, t, slice(jh * HALF, (jh + 1) * HALF), True, (1,) if i < 8 else (0, 1))
             x = rows(col[b], 0, jh, t)
             nc.scalar.activation(x, bank[:].rearrange("p (c i) -> p c i", i=RUN), ACT.Tanh)
-            if b == 0:
+            if b == 0 and jh == 0:
                 nc.vector.tensor_scalar(
                     out=x, in0=x, scalar1=gains[:, b, t : t + 1],
                     scalar2=-1.0 / LINEAR_FROM, op0=ALU.mult, op1=ALU.mult,
                 )
-        factor = keep.tile([P, PACK + 1], F32, name="factor", tag="wd_bf1", align_bytes=64)
+        factor = keep.tile([P, 2 * PACK + 1], F32, name="factor", tag="wd_bf1", align_bytes=64)
         nc.vector.tensor_scalar(
-            out=factor[:, 0:PACK], in0=gains[:, 1, :], scalar1=-1.0 / LINEAR_FROM, scalar2=None, op0=ALU.mult,
+            out=factor[:, 0 : 2 * PACK], in0=gains[:].rearrange("p b t -> p (b t)"), scalar1=-1.0 / LINEAR_FROM, scalar2=None, op0=ALU.mult,
         )
-        nc.vector.memset(factor[:, PACK : PACK + 1], LINEAR_FROM)
-        for b, jh, t in tiles[8:]:
-            x = rows(col[b], 0, jh, t)
+        nc.vector.memset(factor[:, 2 * PACK : 2 * PACK + 1], LINEAR_FROM)
+
+        def apply_gain(x, b, t):
+            at = b * PACK + t
             nc.gpsimd.tensor_scalar(
-                out=x, in0=x, scalar1=factor[:, t : t + 1], scalar2=0.0, op0=ALU.mult, op1=ALU.add,
+                out=x, in0=x, scalar1=factor[:, at : at + 1], scalar2=0.0, op0=ALU.mult, op1=ALU.add,
             )
+
+        for t in range(PACK):
+            apply_gain(col[1][:, 0, :, t, 0:RUN], 1, t)
         for i, (b, jh, t) in enumerate(tiles):
             bank = banks[i % 8]
             product(bank[:], b, t, slice(jh * HALF, (jh + 1) * HALF), False)
@@ -190,8 +197,10 @@ def tile_list_voxel_radiance_field_kernel(
             nc.scalar.activation(rows(dens, b, jh, t), logits, ACT.Sigmoid, scale=-1.0)
             x = rows(col[b], 0, jh, t)
             nc.vector.scalar_tensor_tensor(
-                out=x, in0=logits, scalar=factor[:, PACK : PACK + 1], in1=x, op0=ALU.max, op1=ALU.mult,
+                out=x, in0=logits, scalar=factor[:, 2 * PACK : 2 * PACK + 1], in1=x, op0=ALU.max, op1=ALU.mult,
             )
+            if b == 0 and jh == 1:
+                apply_gain(x, b, t)
         nc.scalar.activation(one[:], dens[:, 1, S // RUN - 1, PACK - 3, 0:1], ACT.Copy, scale=0.0, bias=LOG_FLOOR)
 
         wr_q = keep.tile([P, 2, N], I32, name="wr_q", tag="wd_bf0", align_bytes=64)
@@ -211,25 +220,34 @@ def tile_list_voxel_radiance_field_kernel(
         for w in WIDTHS:
             lo = spans[-1].stop if spans else 0
             spans.append(slice(lo, lo + w))
+
+        def parts(b, js):
+            if b == 0 and js.start == 0:
+                return [slice(0, FIRST), slice(FIRST, js.stop)]
+            return [js]
+
         for js in spans:
             for b in range(2):
-                x = flat(dens, b, js)
-                nc.scalar.activation(x, x, ACT.Ln, bias=one[:])
+                for part in parts(b, js):
+                    x = flat(dens, b, part)
+                    nc.scalar.activation(x, x, ACT.Ln, bias=one[:])
 
         result = keep.tile([P, N // P, S], F32, name="result")
         out_v = out.rearrange("(n p) j -> p n j", p=P)
 
         def hidden(b, js):
             g = ring.tile([P, PACK * (js.stop - js.start)], BF16, name="bf", align_bytes=64)
-            for u in range(2):
-                pair = slice(2 * u, 2 * u + 2)
-                nc.vector.scalar_tensor_tensor(
-                    out=g[:].rearrange("p (i x) -> p x i", i=RUN)[:, :, pair],
-                    in0=flat(dens, b, js)[:, :, pair],
-                    scalar=-LINEAR_FROM,
-                    in1=flat(col[b], 0, js)[:, :, pair],
-                    op0=ALU.max, op1=ALU.mult,
-                )
+            for part in parts(b, js):
+                xs = slice(part.start - js.start, part.stop - js.start)
+                for u in range(2):
+                    pair = slice(2 * u, 2 * u + 2)
+                    nc.vector.scalar_tensor_tensor(
+                        out=g[:].rearrange("p (i x) -> p x i", i=RUN)[:, xs, pair],
+                        in0=flat(dens, b, part)[:, :, pair],
+                        scalar=-LINEAR_FROM,
+                        in1=flat(col[b], 0, part)[:, :, pair],
+                        op0=ALU.max, op1=ALU.mult,
+                    )
             return g
 
         def finish(c, b, g):
@@ -261,7 +279,7 @@ def tile_list_voxel_radiance_field_kernel(
             per_bank = HALF // w
             for n0 in range(0, N // P, per_bank):
                 count = min(per_bank, N // P - n0)
-                bank = banks[(2 * c + n0 // per_bank) % 8]
+                bank = banks[3 + (2 * c + n0 // per_bank) % 5]
                 for n in range(n0, n0 + count):
                     ns = slice(n * P, (n + 1) * P)
                     for a in range(2):

@@ -156,8 +156,8 @@ def tile_list_voxel_radiance_field_kernel(
             keep.tile([P, 1, S // RUN, PACK, 2 * RUN], F32, name=f"col{b}", align_bytes=64) for b in range(2)
         ]
         one = keep.tile([P, 1], F32, name="one")
-        h_q = keep.tile([P, 2, S], U32, name="h_q", align_bytes=64)
-        h_s = keep.tile([P, 2, S], U8, name="h_s", align_bytes=64)
+        h_q = keep.tile([P, 2 * S], U32, name="h_q", align_bytes=64)
+        h_s = keep.tile([P, 2 * S], U8, name="h_s", align_bytes=64)
 
         quantise_wd(0)
         quantise_wd(1)
@@ -166,16 +166,23 @@ def tile_list_voxel_radiance_field_kernel(
 
         for i, (b, jh, t) in enumerate(tiles[:8]):
             product(banks[i][:], b, t, slice(jh * HALF, (jh + 1) * HALF), True, (0,))
-        for i, (b, jh, t) in enumerate(tiles):
-            bank = banks[i % 8]
-            product(bank[:], b, t, slice(jh * HALF, (jh + 1) * HALF), True, (1,) if i < 8 else (0, 1))
-            x = rows(col[b], 0, jh, t)
-            nc.scalar.activation(x, bank[:].rearrange("p (c i) -> p c i", i=RUN), ACT.Tanh)
-            if b == 0 and jh == 0:
-                nc.vector.tensor_scalar(
-                    out=x, in0=x, scalar1=gains[:, b, t : t + 1],
-                    scalar2=-1.0 / LINEAR_FROM, op0=ALU.mult, op1=ALU.mult,
+        for first in range(0, len(tiles), 2):
+            for i in (first, first + 1):
+                b, jh, t = tiles[i]
+                product(banks[i % 8][:], b, t, slice(jh * HALF, (jh + 1) * HALF), True, (1,) if i < 8 else (0, 1))
+            for i in (first, first + 1) if first == 0 else (first + 1, first):
+                b, jh, t = tiles[i]
+                nc.scalar.activation(
+                    rows(col[b], 0, jh, t), banks[i % 8][:].rearrange("p (c i) -> p c i", i=RUN), ACT.Tanh
                 )
+            for i in (first, first + 1):
+                b, jh, t = tiles[i]
+                if b == 0 and jh == 0:
+                    x = rows(col[b], 0, jh, t)
+                    nc.vector.tensor_scalar(
+                        out=x, in0=x, scalar1=gains[:, b, t : t + 1],
+                        scalar2=-1.0 / LINEAR_FROM, op0=ALU.mult, op1=ALU.mult,
+                    )
         factor = keep.tile([P, 2 * PACK + 1], F32, name="factor", tag="wd_bf1", align_bytes=64)
         nc.vector.tensor_scalar(
             out=factor[:, 0 : 2 * PACK], in0=gains[:].rearrange("p b t -> p (b t)"), scalar1=-1.0 / LINEAR_FROM, scalar2=None, op0=ALU.mult,
@@ -190,18 +197,24 @@ def tile_list_voxel_radiance_field_kernel(
 
         for t in range(PACK):
             apply_gain(col[1][:, 0, :, t, 0:RUN], 1, t)
-        for i, (b, jh, t) in enumerate(tiles):
-            bank = banks[i % 8]
-            product(bank[:], b, t, slice(jh * HALF, (jh + 1) * HALF), False)
-            logits = bank[:].rearrange("p (c i) -> p c i", i=RUN)
-            nc.scalar.activation(rows(dens, b, jh, t), logits, ACT.Sigmoid, scale=-1.0)
-            x = rows(col[b], 0, jh, t)
-            nc.vector.scalar_tensor_tensor(
-                out=x, in0=logits, scalar=factor[:, 2 * PACK : 2 * PACK + 1], in1=x, op0=ALU.max, op1=ALU.mult,
-            )
-            if b == 0 and jh == 1:
-                apply_gain(x, b, t)
-        nc.scalar.activation(one[:], dens[:, 1, S // RUN - 1, PACK - 3, 0:1], ACT.Copy, scale=0.0, bias=LOG_FLOOR)
+        for first in range(0, len(tiles), 2):
+            for i in (first, first + 1):
+                b, jh, t = tiles[i]
+                product(banks[i % 8][:], b, t, slice(jh * HALF, (jh + 1) * HALF), False)
+            for i in (first + 1, first):
+                b, jh, t = tiles[i]
+                logits = banks[i % 8][:].rearrange("p (c i) -> p c i", i=RUN)
+                nc.scalar.activation(rows(dens, b, jh, t), logits, ACT.Sigmoid, scale=-1.0)
+            for i in (first, first + 1):
+                b, jh, t = tiles[i]
+                logits = banks[i % 8][:].rearrange("p (c i) -> p c i", i=RUN)
+                x = rows(col[b], 0, jh, t)
+                nc.vector.scalar_tensor_tensor(
+                    out=x, in0=logits, scalar=factor[:, 2 * PACK : 2 * PACK + 1], in1=x, op0=ALU.max, op1=ALU.mult,
+                )
+                if b == 0 and jh == 1:
+                    apply_gain(x, b, t)
+        nc.scalar.activation(one[:], dens[:, 1, S // RUN - 1, PACK - 4, 0:1], ACT.Copy, scale=0.0, bias=LOG_FLOOR)
 
         wr_q = keep.tile([P, 2, N], I32, name="wr_q", tag="wd_bf0", align_bytes=64)
         wr_s = stage.tile([P, 2, N // 4], I32, name="wr_s", offset=0, align_bytes=64)
@@ -226,7 +239,7 @@ def tile_list_voxel_radiance_field_kernel(
                 return [slice(0, FIRST), slice(FIRST, js.stop)]
             return [js]
 
-        for js in spans:
+        for js in spans[:-2] + [slice(spans[-2].start, S)]:
             for b in range(2):
                 for part in parts(b, js):
                     x = flat(dens, b, part)
@@ -235,72 +248,76 @@ def tile_list_voxel_radiance_field_kernel(
         result = keep.tile([P, N // P, S], F32, name="result")
         out_v = out.rearrange("(n p) j -> p n j", p=P)
 
-        def hidden(b, js):
-            g = ring.tile([P, PACK * (js.stop - js.start)], BF16, name="bf", align_bytes=64)
+        def hidden(g, b, js):
             for part in parts(b, js):
                 xs = slice(part.start - js.start, part.stop - js.start)
                 for u in range(2):
                     pair = slice(2 * u, 2 * u + 2)
                     nc.vector.scalar_tensor_tensor(
-                        out=g[:].rearrange("p (i x) -> p x i", i=RUN)[:, xs, pair],
+                        out=g[:, b, :].rearrange("p (i x) -> p x i", i=RUN)[:, xs, pair],
                         in0=flat(dens, b, part)[:, :, pair],
                         scalar=-LINEAR_FROM,
                         in1=flat(col[b], 0, part)[:, :, pair],
                         op0=ALU.max, op1=ALU.mult,
                     )
-            return g
 
-        def finish(c, b, g):
+        def words(js, b):
+            w = js.stop - js.start
+            return slice(2 * js.start + b * w, 2 * js.start + (b + 1) * w)
+
+        def radiance(dst, n, b, js):
+            ns = slice(n * P, (n + 1) * P)
+            nc.tensor.matmul_mx(
+                out=dst,
+                lhsT=wr_q[:, b, ns].bitcast(FP8X4),
+                lhsT_scale=wr_s[:, b, :].bitcast(U8)[:, ns],
+                rhs=h_q[:, words(js, b)].bitcast(FP8X4), rhs_scale=h_s[:, words(js, b)],
+                start=(b == 0), stop=(b == 1),
+            )
+
+        def finish(c, g):
             js = spans[c]
             w = js.stop - js.start
-            nc.vector.quantize_mx(out=h_q[:, b, js].bitcast(FP8X4), scales=h_s[:, b, js], in_=g[:])
-            if c == len(spans) - 1:
-                for n in range(N // P):
-                    ns = slice(n * P, (n + 1) * P)
-                    nc.tensor.matmul_mx(
-                        out=banks[n][:, 0:w],
-                        lhsT=wr_q[:, b, ns].bitcast(FP8X4),
-                        lhsT_scale=wr_s[:, b, :].bitcast(U8)[:, ns],
-                        rhs=h_q[:, b, js].bitcast(FP8X4), rhs_scale=h_s[:, b, js],
-                        start=(b == 0), stop=(b == 1),
-                    )
-                    if b == 1:
-                        dst = result[:, n, js].rearrange("p (c i) -> p c i", i=RUN)
-                        src = banks[n][:, 0:w].rearrange("p (i c) -> p c i", i=RUN)
-                        if n == 1:
-                            nc.vector.tensor_copy(dst, src)
-                        else:
-                            nc.scalar.copy(dst, src)
-                if b == 1:
-                    nc.sync.dma_start(out_v[:, :, js], result[:, :, js])
-                return
-            if b == 0:
-                return
+            both = slice(2 * js.start, 2 * js.stop)
+            nc.vector.quantize_mx(
+                out=h_q[:, both].bitcast(FP8X4), scales=h_s[:, both], in_=g[:].rearrange("p b x -> p (b x)")
+            )
             per_bank = HALF // w
             for n0 in range(0, N // P, per_bank):
                 count = min(per_bank, N // P - n0)
                 bank = banks[3 + (2 * c + n0 // per_bank) % 5]
                 for n in range(n0, n0 + count):
-                    ns = slice(n * P, (n + 1) * P)
-                    for a in range(2):
-                        nc.tensor.matmul_mx(
-                            out=bank[:, (n - n0) * w : (n - n0 + 1) * w],
-                            lhsT=wr_q[:, a, ns].bitcast(FP8X4),
-                            lhsT_scale=wr_s[:, a, :].bitcast(U8)[:, ns],
-                            rhs=h_q[:, a, js].bitcast(FP8X4), rhs_scale=h_s[:, a, js],
-                            start=(a == 0), stop=(a == 1),
-                        )
+                    for b in range(2):
+                        radiance(bank[:, (n - n0) * w : (n - n0 + 1) * w], n, b, js)
                 nc.scalar.copy(
                     result[:, n0 : n0 + count, js].rearrange("p n (c i) -> p n c i", i=RUN),
                     bank[:, 0 : count * w].rearrange("p (n i c) -> p n c i", n=count, i=RUN),
                 )
             nc.sync.dma_start(out_v[:, :, js], result[:, :, js])
 
-        pending = None
-        for c in range(len(spans)):
+        def finish_last(js, g):
+            w = js.stop - js.start
             for b in range(2):
-                g = hidden(b, spans[c])
-                if pending is not None:
-                    finish(*pending)
-                pending = (c, b, g)
-        finish(*pending)
+                nc.vector.quantize_mx(
+                    out=h_q[:, words(js, b)].bitcast(FP8X4), scales=h_s[:, words(js, b)], in_=g[:, b, :]
+                )
+                for n in range(N // P):
+                    radiance(banks[n][:, 0:w], n, b, js)
+            for n in range(N // P):
+                dst = result[:, n, js].rearrange("p (c i) -> p c i", i=RUN)
+                src = banks[n][:, 0:w].rearrange("p (i c) -> p c i", i=RUN)
+                if n == 1:
+                    nc.vector.tensor_copy(dst, src)
+                else:
+                    nc.scalar.copy(dst, src)
+            nc.sync.dma_start(out_v[:, :, js], result[:, :, js])
+
+        pending = None
+        for c, js in enumerate(spans):
+            g = ring.tile([P, 2, PACK * (js.stop - js.start)], BF16, name="bf", align_bytes=64)
+            hidden(g, 0, js)
+            if pending is not None:
+                finish(*pending)
+            hidden(g, 1, js)
+            pending = (c, g)
+        finish_last(spans[-1], g)

@@ -20,14 +20,16 @@ P = 128
 PACK = 4
 GROUP = P * PACK
 HALF = 512
-CHUNK = 128
-PIECE = 256
+BANKS = 8
 RUN = 4
-PIECE_BYTES = 4 * PACK * GROUP
+ALIGN = 64
+WC_GROUP_BYTES = 2 * 2 * GROUP
+WD_PIECE_BYTES = 4 * PACK * GROUP
 LINEAR_FROM = 16.0
 LOG_FLOOR = 2.0**-60
-WIDTHS = (128, 256, 256, 128, 128, 128)
-FIRST = 64
+STEPS = (128, 256, 256, 128, 128, 128)
+FIRST_CUT = 64
+LAST_BANKS = N // P
 
 
 def tile_list_voxel_radiance_field_kernel(
@@ -38,186 +40,179 @@ def tile_list_voxel_radiance_field_kernel(
         keep = ctx.enter_context(tc.tile_pool(name="keep", bufs=1))
         ring = ctx.enter_context(tc.tile_pool(name="ring", bufs=3))
         stage = ctx.enter_context(tc.tile_pool(name="stage", bufs=1))
+        late = ctx.enter_context(tc.tile_pool(name="late", bufs=1))
         psum = ctx.enter_context(tc.psum_pool(name="psum", bufs=1))
+
+        banks = [psum.tile([P, HALF], F32, name=f"bank{i}") for i in range(BANKS)]
 
         offsets = keep.tile([P, S // 16], U16, name="offsets")
         nc.sync.dma_start(offsets[:], offs)
+        warm = keep.tile([P, 1], F32, name="warm", align_bytes=ALIGN)
+        warm_out = keep.tile([P, 1], F32, name="warm_out", align_bytes=ALIGN)
+        tab_s = late.tile([P, T // 4], I32, name="tab_s", offset=0, align_bytes=ALIGN)
+        wc_s_raw = keep.tile([P, 2, H // 4], I32, name="wc_s_raw", align_bytes=ALIGN)
+        v_s = keep.tile([P, 2, S // 4], I32, name="v_s", align_bytes=ALIGN)
 
-        banks = [psum.tile([P, HALF], F32, name=f"bank{i}") for i in range(8)]
-
-        warm = keep.tile([P, 1], F32, name="warm", align_bytes=64)
-        warm_out = keep.tile([P, 1], F32, name="warm_out", align_bytes=64)
-        tab_s = keep.tile([P, T // 4], I32, name="tab_s", tag="tab_w1", align_bytes=64)
-        wc_s_raw = keep.tile([P, 2, H // 4], I32, name="wc_s_raw", align_bytes=64)
-        v_s = keep.tile([P, 2, S // 4], I32, name="v_s", align_bytes=64)
         nc.gpsimd.memset(wc_s_raw[:], 0)
         nc.gpsimd.memset(warm[:], 0.0)
         nc.vector.memset(tab_s[32:64, :], 0)
         nc.vector.memset(tab_s[64:128, :], 0)
         nc.vector.memset(v_s[:], 0)
-        wc_raw = keep.tile([P, 2, H // 2], I32, name="wc_raw", align_bytes=64)
+
+        wc_raw = [keep.tile([P, 2, GROUP // 2], I32, name="wc_raw0", align_bytes=ALIGN)]
+        wc_src = wc_words.rearrange("a p e -> p a e").bitcast(I32)
         nc.sync.dma_start(tab_s[0:32, :], tab_scales.rearrange("a q t -> (a q) t").bitcast(I32))
-        nc.sync.dma_start(wc_raw[:], wc_words.rearrange("a p e -> p a e").bitcast(I32))
+        nc.sync.dma_start(wc_raw[0][:], wc_src[:, :, 0 : GROUP // 2])
         for q in range(4):
             nc.sync.dma_start(
                 wc_s_raw[32 * q : 32 * q + 4, :, :],
                 wc_scales[:, 4 * q : 4 * q + 4, :].rearrange("a r e -> r a e").bitcast(I32),
             )
+
         nc.scalar.activation(warm_out[:], warm[:], ACT.Sigmoid)
-        tab_w = [stage.tile([P, T], I32, name="tab_w0", offset=PIECE_BYTES - 64, align_bytes=64)]
+
+        tab_w = [stage.tile([P, T], I32, name="tab_w0", offset=WD_PIECE_BYTES - ALIGN, align_bytes=ALIGN)]
         nc.sync.dma_start(tab_w[0][:], tab_words[0].rearrange("p t i -> p (t i)").bitcast(I32))
 
-        picked_s = keep.tile([P, S], U8, name="picked_s", align_bytes=64)
+        picked_s = keep.tile([P, S], U8, name="picked_s", align_bytes=ALIGN)
         nc.vector.tensor_copy(picked_s[:], tab_s[:].bitcast(U8).indirect(offsets[:]))
-        tab_w.append(keep.tile([P, T], I32, name="tab_w1", tag="tab_w1", align_bytes=64))
-        second = tab_words[1].rearrange("p t i -> p (t i)").bitcast(I32)
 
-        def move_rows(a, q):
-            row = 16 * a + 4 * q
-            nc.scalar.dma_start(v_s[32 * q : 32 * q + 4, a, :], picked_s[row : row + 4, :].bitcast(I32))
+        def move_scale_rows(a):
+            for q in range(4):
+                row = 16 * a + 4 * q
+                nc.scalar.dma_start(v_s[32 * q : 32 * q + 4, a, :], picked_s[row : row + 4, :].bitcast(I32))
 
-        for q in range(4):
-            move_rows(0, q)
-        nc.scalar.dma_start(tab_w[1][:, 0 : T // 2], second[:, 0 : T // 2])
-        for q in range(4):
-            move_rows(1, q)
-        nc.scalar.dma_start(tab_w[1][:, T // 2 : T], second[:, T // 2 : T])
-        gains = keep.tile([P, 2, PACK], F32, name="gains", align_bytes=64)
+        tab_w.append(late.tile([P, T], I32, name="tab_w1", offset=WC_GROUP_BYTES, align_bytes=ALIGN))
+        move_scale_rows(0)
+        nc.scalar.dma_start(tab_w[1][:], tab_words[1].rearrange("p t i -> p (t i)").bitcast(I32))
+        move_scale_rows(1)
+        wc_raw.append(late.tile([P, 2, GROUP // 2], I32, name="wc_raw1", offset=0, align_bytes=ALIGN))
+        nc.scalar.dma_start(wc_raw[1][:], wc_src[:, :, GROUP // 2 : GROUP])
+        gains = keep.tile([P, 2, PACK], F32, name="gains", align_bytes=ALIGN)
         nc.gpsimd.dma_start(gains[:], gain.rearrange("(b p t) -> p b t", b=2, t=PACK))
 
-        wc_q = keep.tile([P, 2, 2 * H], U8, name="wc_q", align_bytes=64)
-        wc_s = keep.tile([P, 2, H], U8, name="wc_s", align_bytes=64)
-        for u in range(2):
-            pair = slice(2 * u, 2 * u + 2)
-            nc.vector.tensor_copy(
-                out=wc_q[:].bitcast(U16).rearrange("p a (b t m) -> p (a b) m t", b=2, t=PACK)[:, :, :, pair],
-                in_=wc_raw[:].bitcast(U16).rearrange("p a (b m t) -> p (a b) m t", b=2, t=PACK)[:, :, :, pair],
-            )
-        for u in range(2):
-            pair = slice(2 * u, 2 * u + 2)
+        pairs = [slice(0, 2), slice(2, 4)]
+
+        wc_q = keep.tile([P, 2, 2 * H], U8, name="wc_q", align_bytes=ALIGN)
+        wc_s = keep.tile([P, 2, H], U8, name="wc_s", align_bytes=ALIGN)
+
+        def deal_wc_words(b):
+            for pair in pairs:
+                nc.vector.tensor_copy(
+                    out=wc_q[:].bitcast(U16).rearrange("p a (b t m) -> p a b m t", b=2, t=PACK)[:, :, b, :, pair],
+                    in_=wc_raw[b][:].bitcast(U16).rearrange("p a (m t) -> p a m t", t=PACK)[:, :, :, pair],
+                )
+
+        deal_wc_words(0)
+        for pair in pairs:
             nc.vector.tensor_copy(
                 out=wc_s[:].rearrange("p a (b t m) -> p (a b) m t", b=2, t=PACK)[:, :, :, pair],
                 in_=wc_s_raw[:].bitcast(U8).rearrange("p a (b m t) -> p (a b) m t", b=2, t=PACK)[:, :, :, pair],
             )
 
-        v_w = [keep.tile([P, S], U32, name=f"v_w{a}", align_bytes=64) for a in range(2)]
+        halves = [slice(0, HALF), slice(HALF, S)]
+        v_w = [keep.tile([P, S], U32, name=f"v_w{a}", align_bytes=ALIGN) for a in range(2)]
         for a in range(2):
-            for jh in range(2):
-                cols = slice(jh * HALF, (jh + 1) * HALF)
-                lst = offsets[:, jh * HALF // 16 : (jh + 1) * HALF // 16]
-                nc.vector.tensor_copy(v_w[a][:, cols], tab_w[a][:].bitcast(U32).indirect(lst))
+            for half in halves:
+                entries = offsets[:, half.start // 16 : half.stop // 16]
+                nc.vector.tensor_copy(v_w[a][:, half], tab_w[a][:].bitcast(U32).indirect(entries))
+        deal_wc_words(1)
 
-        wd_q = keep.tile([P, 2, H], U32, name="wd_q", align_bytes=64)
-        wd_s = keep.tile([P, 2, H], U8, name="wd_s", align_bytes=64)
-
-        def quantise_wd(b):
-            grouped = keep.tile([P, 2, PACK * GROUP], BF16, name=f"wd_bf{b}", tag=f"wd_bf{b}", align_bytes=64)
+        wd_q = keep.tile([P, 2, H], U32, name="wd_q", align_bytes=ALIGN)
+        wd_s = keep.tile([P, 2, H], U8, name="wd_s", align_bytes=ALIGN)
+        wd_places = [(stage, 0), (stage, WD_PIECE_BYTES), (stage, 2 * WD_PIECE_BYTES), (late, WC_GROUP_BYTES)]
+        for b in range(2):
+            cols = slice(b * GROUP, (b + 1) * GROUP)
+            grouped = keep.tile([P, 2, PACK * GROUP], BF16, name=f"wd_bf{b}", tag=f"wd_bf{b}", align_bytes=ALIGN)
             for a in range(2):
-                piece = 2 * b + a
-                if piece < 3:
-                    whole = stage.tile(
-                        [P, PACK, GROUP], F32, name=f"wd_raw{piece}", offset=piece * PIECE_BYTES, align_bytes=64
-                    )
-                else:
-                    whole = keep.tile([P, PACK, GROUP], F32, name="wd_raw3", tag="tab_w1", align_bytes=64)
-                raw = whole[:]
-                nc.sync.dma_start(
-                    raw,
-                    wd[a * GROUP : (a + 1) * GROUP, b * GROUP : (b + 1) * GROUP].rearrange("(p i) e -> p i e", i=PACK),
-                )
-                for u in range(2):
-                    pair = slice(2 * u, 2 * u + 2)
+                pool, place = wd_places[2 * b + a]
+                raw = pool.tile([P, PACK, GROUP], F32, name=f"wd_raw{2 * b + a}", offset=place, align_bytes=ALIGN)
+                nc.sync.dma_start(raw[:], wd[a * GROUP : (a + 1) * GROUP, cols].rearrange("(p i) e -> p i e", i=PACK))
+                for pair in pairs:
                     nc.vector.tensor_copy(
                         out=grouped[:, a, :].rearrange("p (t m i) -> p m i t", t=PACK, i=PACK)[:, :, :, pair],
-                        in_=raw.rearrange("p i (m t) -> p m i t", t=PACK)[:, :, :, pair],
+                        in_=raw[:].rearrange("p i (m t) -> p m i t", t=PACK)[:, :, :, pair],
                     )
             for a in range(2):
-                cols = slice(b * GROUP, (b + 1) * GROUP)
-                nc.vector.quantize_mx(out=wd_q[:, a, cols].bitcast(FP8X4), scales=wd_s[:, a, cols], in_=grouped[:, a, :])
+                nc.vector.quantize_mx(
+                    out=wd_q[:, a, cols].bitcast(FP8X4), scales=wd_s[:, a, cols], in_=grouped[:, a, :]
+                )
 
-        def product(dst, b, t, js, colour, passes=(0, 1)):
+        def first_stage(bank, lhs, lhs_scale, a, half):
+            nc.tensor.matmul_mx(
+                out=bank[:], lhsT=lhs, lhsT_scale=lhs_scale,
+                rhs=v_w[a][:, half].bitcast(FP8X4), rhs_scale=v_s[:, a, :].bitcast(U8)[:, half],
+                start=(a == 0), stop=(a == 1),
+            )
+
+        def colour_pass(bank, b, half, t, a):
             c0 = b * GROUP + t * P
-            for a in passes:
-                if colour:
-                    lhs = wc_q[:, a, 2 * c0 : 2 * (c0 + P)].bitcast(FP4X4)
-                    lhs_s = wc_s[:, a, c0 : c0 + P]
-                else:
-                    lhs = wd_q[:, a, c0 : c0 + P].bitcast(FP8X4)
-                    lhs_s = wd_s[:, a, c0 : c0 + P]
-                nc.tensor.matmul_mx(
-                    out=dst, lhsT=lhs, lhsT_scale=lhs_s,
-                    rhs=v_w[a][:, js].bitcast(FP8X4), rhs_scale=v_s[:, a, :].bitcast(U8)[:, js],
-                    start=(a == 0), stop=(a == 1),
+            first_stage(bank, wc_q[:, a, 2 * c0 : 2 * (c0 + P)].bitcast(FP4X4), wc_s[:, a, c0 : c0 + P], a, half)
+
+        def density_pass(bank, b, half, t, a):
+            c0 = b * GROUP + t * P
+            first_stage(bank, wd_q[:, a, c0 : c0 + P].bitcast(FP8X4), wd_s[:, a, c0 : c0 + P], a, half)
+
+        products = [(b, half, t) for b in range(2) for half in halves for t in range(PACK)]
+        dens = keep.tile([P, 2, S // RUN, PACK, RUN], F32, name="dens", align_bytes=ALIGN)
+        col = [keep.tile([P, S // RUN, PACK, 2 * RUN], F32, name=f"col{b}", align_bytes=ALIGN) for b in range(2)]
+        floor = keep.tile([P, 1], F32, name="floor")
+        h_q = keep.tile([P, 2 * S], U32, name="h_q", align_bytes=ALIGN)
+        h_s = keep.tile([P, 2 * S], U8, name="h_s", align_bytes=ALIGN)
+
+        def runs(tile, voxels, t):
+            return tile[:, voxels.start // RUN : voxels.stop // RUN, t, 0:RUN]
+
+        def in_runs(bank):
+            return bank[:].rearrange("p (c i) -> p c i", i=RUN)
+
+        for i, (b, half, t) in enumerate(products[:BANKS]):
+            colour_pass(banks[i], b, half, t, 0)
+        for i, (b, half, t) in enumerate(products):
+            bank = banks[i % BANKS]
+            for a in (1,) if i < BANKS else (0, 1):
+                colour_pass(bank, b, half, t, a)
+            x = runs(col[b], half, t)
+            nc.scalar.activation(x, in_runs(bank), ACT.Tanh)
+            if b == 0 and half == halves[0]:
+                nc.vector.tensor_scalar(
+                    out=x, in0=x, scalar1=gains[:, b, t : t + 1],
+                    scalar2=-1.0 / LINEAR_FROM, op0=ALU.mult, op1=ALU.mult,
                 )
 
-        tiles = [(b, jh, t) for b in range(2) for jh in range(2) for t in range(PACK)]
-        dens = keep.tile([P, 2, S // RUN, PACK, RUN], F32, name="dens", align_bytes=64)
-        col = [
-            keep.tile([P, 1, S // RUN, PACK, 2 * RUN], F32, name=f"col{b}", align_bytes=64) for b in range(2)
-        ]
-        one = keep.tile([P, 1], F32, name="one")
-        h_q = keep.tile([P, 2 * S], U32, name="h_q", align_bytes=64)
-        h_s = keep.tile([P, 2 * S], U8, name="h_s", align_bytes=64)
-
-        quantise_wd(0)
-        quantise_wd(1)
-        def rows(tile, b, jh, t):
-            return tile[:, b, jh * HALF // RUN : (jh + 1) * HALF // RUN, t, 0:RUN]
-
-        for i, (b, jh, t) in enumerate(tiles[:8]):
-            product(banks[i][:], b, t, slice(jh * HALF, (jh + 1) * HALF), True, (0,))
-        for first in range(0, len(tiles), 2):
-            for i in (first, first + 1):
-                b, jh, t = tiles[i]
-                product(banks[i % 8][:], b, t, slice(jh * HALF, (jh + 1) * HALF), True, (1,) if i < 8 else (0, 1))
-            for i in (first, first + 1) if first == 0 else (first + 1, first):
-                b, jh, t = tiles[i]
-                nc.scalar.activation(
-                    rows(col[b], 0, jh, t), banks[i % 8][:].rearrange("p (c i) -> p c i", i=RUN), ACT.Tanh
-                )
-            for i in (first, first + 1):
-                b, jh, t = tiles[i]
-                if b == 0 and jh == 0:
-                    x = rows(col[b], 0, jh, t)
-                    nc.vector.tensor_scalar(
-                        out=x, in0=x, scalar1=gains[:, b, t : t + 1],
-                        scalar2=-1.0 / LINEAR_FROM, op0=ALU.mult, op1=ALU.mult,
-                    )
-        factor = keep.tile([P, 2 * PACK + 1], F32, name="factor", tag="wd_bf1", align_bytes=64)
+        consts = keep.tile([P, 2 * PACK + 1], F32, name="consts", tag="wd_bf1", align_bytes=ALIGN)
+        threshold = consts[:, 2 * PACK : 2 * PACK + 1]
         nc.vector.tensor_scalar(
-            out=factor[:, 0 : 2 * PACK], in0=gains[:].rearrange("p b t -> p (b t)"), scalar1=-1.0 / LINEAR_FROM, scalar2=None, op0=ALU.mult,
+            out=consts[:, 0 : 2 * PACK], in0=gains[:].rearrange("p b t -> p (b t)"),
+            scalar1=-1.0 / LINEAR_FROM, scalar2=None, op0=ALU.mult,
         )
-        nc.vector.memset(factor[:, 2 * PACK : 2 * PACK + 1], LINEAR_FROM)
+        nc.vector.memset(threshold, LINEAR_FROM)
 
-        def apply_gain(x, b, t):
+        def gain_on_gpsimd(b, voxels, t):
+            x = runs(col[b], voxels, t)
             at = b * PACK + t
             nc.gpsimd.tensor_scalar(
-                out=x, in0=x, scalar1=factor[:, at : at + 1], scalar2=0.0, op0=ALU.mult, op1=ALU.add,
+                out=x, in0=x, scalar1=consts[:, at : at + 1], scalar2=0.0, op0=ALU.mult, op1=ALU.add,
             )
 
         for t in range(PACK):
-            apply_gain(col[1][:, 0, :, t, 0:RUN], 1, t)
-        for first in range(0, len(tiles), 2):
-            for i in (first, first + 1):
-                b, jh, t = tiles[i]
-                product(banks[i % 8][:], b, t, slice(jh * HALF, (jh + 1) * HALF), False)
-            for i in (first + 1, first):
-                b, jh, t = tiles[i]
-                logits = banks[i % 8][:].rearrange("p (c i) -> p c i", i=RUN)
-                nc.scalar.activation(rows(dens, b, jh, t), logits, ACT.Sigmoid, scale=-1.0)
-            for i in (first, first + 1):
-                b, jh, t = tiles[i]
-                logits = banks[i % 8][:].rearrange("p (c i) -> p c i", i=RUN)
-                x = rows(col[b], 0, jh, t)
-                nc.vector.scalar_tensor_tensor(
-                    out=x, in0=logits, scalar=factor[:, 2 * PACK : 2 * PACK + 1], in1=x, op0=ALU.max, op1=ALU.mult,
-                )
-                if b == 0 and jh == 1:
-                    apply_gain(x, b, t)
-        nc.scalar.activation(one[:], dens[:, 1, S // RUN - 1, PACK - 4, 0:1], ACT.Copy, scale=0.0, bias=LOG_FLOOR)
+            gain_on_gpsimd(1, slice(0, S), t)
+        for i, (b, half, t) in enumerate(products):
+            bank = banks[i % BANKS]
+            for a in range(2):
+                density_pass(bank, b, half, t, a)
+            nc.scalar.activation(runs(dens[:, b], half, t), in_runs(bank), ACT.Sigmoid, scale=-1.0)
+            x = runs(col[b], half, t)
+            nc.vector.scalar_tensor_tensor(
+                out=x, in0=in_runs(bank), scalar=threshold, in1=x, op0=ALU.max, op1=ALU.mult,
+            )
+            if b == 0 and half == halves[1]:
+                gain_on_gpsimd(b, half, t)
 
-        wr_q = keep.tile([P, 2, N], I32, name="wr_q", tag="wd_bf0", align_bytes=64)
-        wr_s = stage.tile([P, 2, N // 4], I32, name="wr_s", offset=0, align_bytes=64)
+        nc.scalar.activation(floor[:], dens[:, 1, S // RUN - 1, PACK - 3, 0:1], ACT.Copy, scale=0.0, bias=LOG_FLOOR)
+
+        wr_q = keep.tile([P, 2, N], I32, name="wr_q", tag="wd_bf0", align_bytes=ALIGN)
+        wr_s = stage.tile([P, 2, N // 4], I32, name="wr_s", offset=0, align_bytes=ALIGN)
         nc.sync.dma_start(wr_q[:], wr_words.rearrange("a p n i -> p a (n i)").bitcast(I32))
         nc.vector.memset(wr_s[:], 0)
         for q in range(4):
@@ -226,98 +221,97 @@ def tile_list_voxel_radiance_field_kernel(
                 wr_scales[:, 4 * q : 4 * q + 4, :].rearrange("a r n -> r a n").bitcast(I32),
             )
 
-        def flat(tile, b, js):
-            return tile[:, b, js.start // RUN : js.stop // RUN, :, :].rearrange("p c t i -> p (c t) i")
+        def all_products(tile, voxels):
+            return tile[:, voxels.start // RUN : voxels.stop // RUN, :, :].rearrange("p c t i -> p (c t) i")
 
-        spans = []
-        for w in WIDTHS:
-            lo = spans[-1].stop if spans else 0
-            spans.append(slice(lo, lo + w))
+        steps = []
+        for width in STEPS:
+            first = steps[-1].stop if steps else 0
+            steps.append(slice(first, first + width))
 
-        def parts(b, js):
-            if b == 0 and js.start == 0:
-                return [slice(0, FIRST), slice(FIRST, js.stop)]
-            return [js]
+        def parts(b, voxels):
+            if b == 0 and voxels.start == 0:
+                return [slice(0, FIRST_CUT), slice(FIRST_CUT, voxels.stop)]
+            return [voxels]
 
-        for js in spans[:-2] + [slice(spans[-2].start, S)]:
+        for voxels in steps[:-2] + [slice(steps[-2].start, S)]:
             for b in range(2):
-                for part in parts(b, js):
-                    x = flat(dens, b, part)
-                    nc.scalar.activation(x, x, ACT.Ln, bias=one[:])
+                for part in parts(b, voxels):
+                    x = all_products(dens[:, b], part)
+                    nc.scalar.activation(x, x, ACT.Ln, bias=floor[:])
 
         result = keep.tile([P, N // P, S], F32, name="result")
         out_v = out.rearrange("(n p) j -> p n j", p=P)
 
-        def hidden(g, b, js):
-            for part in parts(b, js):
-                xs = slice(part.start - js.start, part.stop - js.start)
-                for u in range(2):
-                    pair = slice(2 * u, 2 * u + 2)
+        def hidden(h_bf, b, voxels):
+            for part in parts(b, voxels):
+                local = slice(part.start - voxels.start, part.stop - voxels.start)
+                for pair in pairs:
                     nc.vector.scalar_tensor_tensor(
-                        out=g[:, b, :].rearrange("p (i x) -> p x i", i=RUN)[:, xs, pair],
-                        in0=flat(dens, b, part)[:, :, pair],
+                        out=h_bf[:, b, :].rearrange("p (i x) -> p x i", i=RUN)[:, local, pair],
+                        in0=all_products(dens[:, b], part)[:, :, pair],
                         scalar=-LINEAR_FROM,
-                        in1=flat(col[b], 0, part)[:, :, pair],
+                        in1=all_products(col[b], part)[:, :, pair],
                         op0=ALU.max, op1=ALU.mult,
                     )
 
-        def words(js, b):
-            w = js.stop - js.start
-            return slice(2 * js.start + b * w, 2 * js.start + (b + 1) * w)
+        def h_columns(voxels, b):
+            width = voxels.stop - voxels.start
+            return slice(2 * voxels.start + b * width, 2 * voxels.start + (b + 1) * width)
 
-        def radiance(dst, n, b, js):
-            ns = slice(n * P, (n + 1) * P)
+        def radiance_pass(dst, n, b, voxels):
+            rows = slice(n * P, (n + 1) * P)
             nc.tensor.matmul_mx(
                 out=dst,
-                lhsT=wr_q[:, b, ns].bitcast(FP8X4),
-                lhsT_scale=wr_s[:, b, :].bitcast(U8)[:, ns],
-                rhs=h_q[:, words(js, b)].bitcast(FP8X4), rhs_scale=h_s[:, words(js, b)],
+                lhsT=wr_q[:, b, rows].bitcast(FP8X4),
+                lhsT_scale=wr_s[:, b, :].bitcast(U8)[:, rows],
+                rhs=h_q[:, h_columns(voxels, b)].bitcast(FP8X4), rhs_scale=h_s[:, h_columns(voxels, b)],
                 start=(b == 0), stop=(b == 1),
             )
 
-        def finish(c, g):
-            js = spans[c]
-            w = js.stop - js.start
-            both = slice(2 * js.start, 2 * js.stop)
+        def finish(step, h_bf):
+            voxels = steps[step]
+            width = voxels.stop - voxels.start
+            both = slice(2 * voxels.start, 2 * voxels.stop)
             nc.vector.quantize_mx(
-                out=h_q[:, both].bitcast(FP8X4), scales=h_s[:, both], in_=g[:].rearrange("p b x -> p (b x)")
+                out=h_q[:, both].bitcast(FP8X4), scales=h_s[:, both], in_=h_bf[:].rearrange("p b x -> p (b x)")
             )
-            per_bank = HALF // w
+            per_bank = HALF // width
             for n0 in range(0, N // P, per_bank):
                 count = min(per_bank, N // P - n0)
-                bank = banks[3 + (2 * c + n0 // per_bank) % 5]
+                bank = banks[LAST_BANKS + (2 * step + n0 // per_bank) % (BANKS - LAST_BANKS)]
                 for n in range(n0, n0 + count):
                     for b in range(2):
-                        radiance(bank[:, (n - n0) * w : (n - n0 + 1) * w], n, b, js)
+                        radiance_pass(bank[:, (n - n0) * width : (n - n0 + 1) * width], n, b, voxels)
                 nc.scalar.copy(
-                    result[:, n0 : n0 + count, js].rearrange("p n (c i) -> p n c i", i=RUN),
-                    bank[:, 0 : count * w].rearrange("p (n i c) -> p n c i", n=count, i=RUN),
+                    result[:, n0 : n0 + count, voxels].rearrange("p n (c i) -> p n c i", i=RUN),
+                    bank[:, 0 : count * width].rearrange("p (n i c) -> p n c i", n=count, i=RUN),
                 )
-            nc.sync.dma_start(out_v[:, :, js], result[:, :, js])
+            nc.sync.dma_start(out_v[:, :, voxels], result[:, :, voxels])
 
-        def finish_last(js, g):
-            w = js.stop - js.start
+        def finish_last(voxels, h_bf):
+            width = voxels.stop - voxels.start
             for b in range(2):
                 nc.vector.quantize_mx(
-                    out=h_q[:, words(js, b)].bitcast(FP8X4), scales=h_s[:, words(js, b)], in_=g[:, b, :]
+                    out=h_q[:, h_columns(voxels, b)].bitcast(FP8X4),
+                    scales=h_s[:, h_columns(voxels, b)],
+                    in_=h_bf[:, b, :],
                 )
-                for n in range(N // P):
-                    radiance(banks[n][:, 0:w], n, b, js)
-            for n in range(N // P):
-                dst = result[:, n, js].rearrange("p (c i) -> p c i", i=RUN)
-                src = banks[n][:, 0:w].rearrange("p (i c) -> p c i", i=RUN)
-                if n == 1:
-                    nc.vector.tensor_copy(dst, src)
-                else:
-                    nc.scalar.copy(dst, src)
-            nc.sync.dma_start(out_v[:, :, js], result[:, :, js])
+                for n in range(LAST_BANKS):
+                    radiance_pass(banks[n][:, 0:width], n, b, voxels)
+            for n, copy in enumerate((nc.scalar.copy, nc.vector.tensor_copy, nc.scalar.copy)):
+                copy(
+                    result[:, n, voxels].rearrange("p (c i) -> p c i", i=RUN),
+                    banks[n][:, 0:width].rearrange("p (i c) -> p c i", i=RUN),
+                )
+                nc.sync.dma_start(out_v[:, n, voxels], result[:, n, voxels])
 
         pending = None
-        for c, js in enumerate(spans):
-            g = ring.tile([P, 2, PACK * (js.stop - js.start)], BF16, name="bf", align_bytes=64)
-            hidden(g, 0, js)
+        for step, voxels in enumerate(steps):
+            h_bf = ring.tile([P, 2, PACK * (voxels.stop - voxels.start)], BF16, name="h_bf", align_bytes=ALIGN)
+            hidden(h_bf, 0, voxels)
             if pending is not None:
                 finish(*pending)
-            hidden(g, 1, js)
-            pending = (c, g)
-        finish_last(spans[-1], g)
+            hidden(h_bf, 1, voxels)
+            pending = (step, h_bf)
+        finish_last(steps[-1], h_bf)

@@ -20,6 +20,7 @@ P = 128
 PACK = 4
 GROUP = P * PACK
 HALF = 512
+QUARTER = 256
 BANKS = 8
 RUN = 4
 ALIGN = 64
@@ -41,6 +42,7 @@ def tile_list_voxel_radiance_field_kernel(
         ring = ctx.enter_context(tc.tile_pool(name="ring", bufs=3))
         stage = ctx.enter_context(tc.tile_pool(name="stage", bufs=1))
         late = ctx.enter_context(tc.tile_pool(name="late", bufs=1))
+        turn = ctx.enter_context(tc.tile_pool(name="turn", bufs=1))
         psum = ctx.enter_context(tc.psum_pool(name="psum", bufs=1))
 
         banks = [psum.tile([P, HALF], F32, name=f"bank{i}") for i in range(BANKS)]
@@ -82,12 +84,10 @@ def tile_list_voxel_radiance_field_kernel(
                 row = 16 * a + 4 * q
                 nc.scalar.dma_start(v_s[32 * q : 32 * q + 4, a, :], picked_s[row : row + 4, :].bitcast(I32))
 
-        tab_w.append(late.tile([P, T], I32, name="tab_w1", offset=WC_GROUP_BYTES, align_bytes=ALIGN))
+        tab_w.append(late.tile([P, T], I32, name="tab_w1", offset=0, align_bytes=ALIGN))
         move_scale_rows(0)
         nc.scalar.dma_start(tab_w[1][:], tab_words[1].rearrange("p t i -> p (t i)").bitcast(I32))
         move_scale_rows(1)
-        wc_raw.append(late.tile([P, 2, GROUP // 2], I32, name="wc_raw1", offset=0, align_bytes=ALIGN))
-        nc.scalar.dma_start(wc_raw[1][:], wc_src[:, :, GROUP // 2 : GROUP])
         gains = keep.tile([P, 2, PACK], F32, name="gains", align_bytes=ALIGN)
         nc.gpsimd.dma_start(gains[:], gain.rearrange("(b p t) -> p b t", b=2, t=PACK))
 
@@ -112,48 +112,67 @@ def tile_list_voxel_radiance_field_kernel(
 
         halves = [slice(0, HALF), slice(HALF, S)]
         v_w = [keep.tile([P, S], U32, name=f"v_w{a}", align_bytes=ALIGN) for a in range(2)]
-        for a in range(2):
-            for half in halves:
-                entries = offsets[:, half.start // 16 : half.stop // 16]
-                nc.vector.tensor_copy(v_w[a][:, half], tab_w[a][:].bitcast(U32).indirect(entries))
-        deal_wc_words(1)
+        quarters = [slice(0, QUARTER), slice(QUARTER, HALF)]
+        for a, pieces in enumerate((halves, quarters + halves[1:])):
+            for piece in pieces:
+                entries = offsets[:, piece.start // 16 : piece.stop // 16]
+                nc.vector.tensor_copy(v_w[a][:, piece], tab_w[a][:].bitcast(U32).indirect(entries))
 
         wd_q = keep.tile([P, 2, H], U32, name="wd_q", align_bytes=ALIGN)
         wd_s = keep.tile([P, 2, H], U8, name="wd_s", align_bytes=ALIGN)
-        wd_places = [(stage, 0), (stage, WD_PIECE_BYTES), (stage, 2 * WD_PIECE_BYTES), (late, WC_GROUP_BYTES)]
-        for b in range(2):
+        wd_places = [
+            (stage, 0), (stage, WD_PIECE_BYTES + WC_GROUP_BYTES), (stage, 2 * WD_PIECE_BYTES + WC_GROUP_BYTES), (late, 0),
+        ]
+        wd_raw = []
+        for piece, (pool, place) in enumerate(wd_places):
+            b, a = divmod(piece, 2)
+            raw = pool.tile([P, PACK, GROUP], F32, name=f"wd_raw{piece}", offset=place, align_bytes=ALIGN)
+            rows = wd[a * GROUP : (a + 1) * GROUP, b * GROUP : (b + 1) * GROUP]
+            nc.sync.dma_start(raw[:], rows.rearrange("(p i) e -> p i e", i=PACK))
+            wd_raw.append(raw)
+            if piece == 0:
+                wc_raw.append(stage.tile([P, 2, GROUP // 2], I32, name="wc_raw1", offset=WD_PIECE_BYTES, align_bytes=ALIGN))
+                nc.sync.dma_start(wc_raw[1][:], wc_src[:, :, GROUP // 2 : GROUP])
+
+        def quantise_wd(piece, grouped):
+            b, a = divmod(piece, 2)
             cols = slice(b * GROUP, (b + 1) * GROUP)
-            grouped = keep.tile([P, 2, PACK * GROUP], BF16, name=f"wd_bf{b}", tag=f"wd_bf{b}", align_bytes=ALIGN)
-            for a in range(2):
-                pool, place = wd_places[2 * b + a]
-                raw = pool.tile([P, PACK, GROUP], F32, name=f"wd_raw{2 * b + a}", offset=place, align_bytes=ALIGN)
-                nc.sync.dma_start(raw[:], wd[a * GROUP : (a + 1) * GROUP, cols].rearrange("(p i) e -> p i e", i=PACK))
-                for pair in pairs:
-                    nc.vector.tensor_copy(
-                        out=grouped[:, a, :].rearrange("p (t m i) -> p m i t", t=PACK, i=PACK)[:, :, :, pair],
-                        in_=raw[:].rearrange("p i (m t) -> p m i t", t=PACK)[:, :, :, pair],
-                    )
-            for a in range(2):
+            for pair in pairs:
+                nc.vector.tensor_copy(
+                    out=grouped[:].rearrange("p (t m i) -> p m i t", t=PACK, i=PACK)[:, :, :, pair],
+                    in_=wd_raw[piece][:].rearrange("p i (m t) -> p m i t", t=PACK)[:, :, :, pair],
+                )
+            for pair in pairs:
+                part = slice(cols.start + pair.start * P, cols.start + pair.stop * P)
                 nc.vector.quantize_mx(
-                    out=wd_q[:, a, cols].bitcast(FP8X4), scales=wd_s[:, a, cols], in_=grouped[:, a, :]
+                    out=wd_q[:, a, part].bitcast(FP8X4), scales=wd_s[:, a, part],
+                    in_=grouped[:, pair.start * GROUP : pair.stop * GROUP],
                 )
 
-        def first_stage(bank, lhs, lhs_scale, a, half):
-            nc.tensor.matmul_mx(
-                out=bank[:], lhsT=lhs, lhsT_scale=lhs_scale,
-                rhs=v_w[a][:, half].bitcast(FP8X4), rhs_scale=v_s[:, a, :].bitcast(U8)[:, half],
-                start=(a == 0), stop=(a == 1),
-            )
+        wd_bf = [keep.tile([P, PACK * GROUP], BF16, name=f"wd_bf{n}", tag=f"wd_bf{n}", align_bytes=ALIGN) for n in range(3)]
+        quantise_wd(0, wd_bf[0])
+        deal_wc_words(1)
+        quantise_wd(1, wd_bf[1])
+        quantise_wd(2, wd_bf[2])
+        quantise_wd(3, turn.tile([P, PACK * GROUP], BF16, name="wd_bf3", offset=0, align_bytes=ALIGN))
 
-        def colour_pass(bank, b, half, t, a):
-            c0 = b * GROUP + t * P
-            first_stage(bank, wc_q[:, a, 2 * c0 : 2 * (c0 + P)].bitcast(FP4X4), wc_s[:, a, c0 : c0 + P], a, half)
+        def first_stage(bank, is_colour, b, voxels, ts, a):
+            width = voxels.stop - voxels.start
+            for t in ts:
+                c0 = b * GROUP + t * P
+                if is_colour:
+                    lhs, lhs_scale = wc_q[:, a, 2 * c0 : 2 * (c0 + P)].bitcast(FP4X4), wc_s[:, a, c0 : c0 + P]
+                else:
+                    lhs, lhs_scale = wd_q[:, a, c0 : c0 + P].bitcast(FP8X4), wd_s[:, a, c0 : c0 + P]
+                nc.tensor.matmul_mx(
+                    out=bank[:, (t - ts[0]) * width : (t - ts[0] + 1) * width], lhsT=lhs, lhsT_scale=lhs_scale,
+                    rhs=v_w[a][:, voxels].bitcast(FP8X4), rhs_scale=v_s[:, a, :].bitcast(U8)[:, voxels],
+                    start=(a == 0 and t == ts[0]), stop=(a == 1 and t == ts[-1]),
+                )
 
-        def density_pass(bank, b, half, t, a):
-            c0 = b * GROUP + t * P
-            first_stage(bank, wd_q[:, a, c0 : c0 + P].bitcast(FP8X4), wd_s[:, a, c0 : c0 + P], a, half)
-
-        products = [(b, half, t) for b in range(2) for half in halves for t in range(PACK)]
+        whole = [(b, half, (t,)) for b in range(2) for half in halves for t in range(PACK)]
+        colours = [(0, quarter, ts) for quarter in quarters for ts in ((0, 1), (2, 3))] + whole[PACK:]
+        turns = [(True, c) for c in colours] + [(False, d) for d in whole]
         dens = keep.tile([P, 2, S // RUN, PACK, RUN], F32, name="dens", align_bytes=ALIGN)
         col = [keep.tile([P, S // RUN, PACK, 2 * RUN], F32, name=f"col{b}", align_bytes=ALIGN) for b in range(2)]
         floor = keep.tile([P, 1], F32, name="floor")
@@ -166,48 +185,50 @@ def tile_list_voxel_radiance_field_kernel(
         def in_runs(bank):
             return bank[:].rearrange("p (c i) -> p c i", i=RUN)
 
-        for i, (b, half, t) in enumerate(products[:BANKS]):
-            colour_pass(banks[i], b, half, t, 0)
-        for i, (b, half, t) in enumerate(products):
+        def gain(engine, factors, b, t, voxels=slice(0, S)):
+            x = runs(col[b], voxels, t)
+            engine.tensor_scalar(out=x, in0=x, scalar1=factors[0], scalar2=factors[1], op0=ALU.mult, op1=factors[2])
+
+        def gain_factors(b):
+            tile = turn.tile([P, PACK], F32, name=f"factors{b}", offset=ALIGN, align_bytes=ALIGN)
+            nc.gpsimd.tensor_scalar(
+                out=tile[:], in0=gains[:, b, :], scalar1=-1.0 / LINEAR_FROM, scalar2=0.0, op0=ALU.mult, op1=ALU.add,
+            )
+            return tile
+
+        for i, (is_colour, (b, voxels, ts)) in enumerate(turns[:BANKS]):
+            first_stage(banks[i], is_colour, b, voxels, ts, 0)
+        late_threshold = turn.tile([P, 1], F32, name="late_threshold", offset=0, align_bytes=ALIGN)
+        threshold = late_threshold[:]
+        nc.vector.memset(threshold, LINEAR_FROM)
+        factors = gain_factors(1)
+        for i, (is_colour, (b, voxels, ts)) in enumerate(turns):
             bank = banks[i % BANKS]
             for a in (1,) if i < BANKS else (0, 1):
-                colour_pass(bank, b, half, t, a)
-            x = runs(col[b], half, t)
-            nc.scalar.activation(x, in_runs(bank), ACT.Tanh)
-            if b == 0 and half == halves[0]:
-                nc.vector.tensor_scalar(
-                    out=x, in0=x, scalar1=gains[:, b, t : t + 1],
-                    scalar2=-1.0 / LINEAR_FROM, op0=ALU.mult, op1=ALU.mult,
+                first_stage(bank, is_colour, b, voxels, ts, a)
+            t = ts[0]
+            if is_colour:
+                target = col[b][:, voxels.start // RUN : voxels.stop // RUN, t : ts[-1] + 1, 0:RUN]
+                nc.scalar.activation(
+                    target.rearrange("p c t i -> p t c i"),
+                    bank[:].rearrange("p (t c i) -> p t c i", t=len(ts), i=RUN),
+                    ACT.Tanh,
+                )
+                if b == 0 and voxels == quarters[1]:
+                    for t in ts:
+                        gain(nc.vector, (gains[:, b, t : t + 1], -1.0 / LINEAR_FROM, ALU.mult), b, t, halves[0])
+                if b == 1 and voxels == halves[1]:
+                    gain(nc.gpsimd, (factors[:, t : t + 1], 0.0, ALU.add), b, t)
+            else:
+                nc.scalar.activation(runs(dens[:, b], voxels, t), in_runs(bank), ACT.Sigmoid, scale=-1.0)
+                x = runs(col[b], voxels, t)
+                nc.vector.scalar_tensor_tensor(
+                    out=x, in0=in_runs(bank), scalar=threshold, in1=x, op0=ALU.max, op1=ALU.mult,
                 )
 
-        consts = keep.tile([P, 2 * PACK + 1], F32, name="consts", tag="wd_bf1", align_bytes=ALIGN)
-        threshold = consts[:, 2 * PACK : 2 * PACK + 1]
-        nc.vector.tensor_scalar(
-            out=consts[:, 0 : 2 * PACK], in0=gains[:].rearrange("p b t -> p (b t)"),
-            scalar1=-1.0 / LINEAR_FROM, scalar2=None, op0=ALU.mult,
-        )
-        nc.vector.memset(threshold, LINEAR_FROM)
-
-        def gain_on_gpsimd(b, voxels, t):
-            x = runs(col[b], voxels, t)
-            at = b * PACK + t
-            nc.gpsimd.tensor_scalar(
-                out=x, in0=x, scalar1=consts[:, at : at + 1], scalar2=0.0, op0=ALU.mult, op1=ALU.add,
-            )
-
+        factors = gain_factors(0)
         for t in range(PACK):
-            gain_on_gpsimd(1, slice(0, S), t)
-        for i, (b, half, t) in enumerate(products):
-            bank = banks[i % BANKS]
-            for a in range(2):
-                density_pass(bank, b, half, t, a)
-            nc.scalar.activation(runs(dens[:, b], half, t), in_runs(bank), ACT.Sigmoid, scale=-1.0)
-            x = runs(col[b], half, t)
-            nc.vector.scalar_tensor_tensor(
-                out=x, in0=in_runs(bank), scalar=threshold, in1=x, op0=ALU.max, op1=ALU.mult,
-            )
-            if b == 0 and half == halves[1]:
-                gain_on_gpsimd(b, half, t)
+            gain(nc.gpsimd, (factors[:, t : t + 1], 0.0, ALU.add), 0, t, halves[1])
 
         nc.scalar.activation(floor[:], dens[:, 1, S // RUN - 1, PACK - 3, 0:1], ACT.Copy, scale=0.0, bias=LOG_FLOOR)
 

@@ -22,6 +22,8 @@ GROUP = P * PACK
 HALF = 512
 QUARTER = 256
 BANKS = 8
+VECTOR_GAINS = 2
+LOGS_AHEAD = 3
 RUN = 4
 ALIGN = 64
 WC_GROUP_BYTES = 2 * 2 * GROUP
@@ -121,7 +123,7 @@ def tile_list_voxel_radiance_field_kernel(
         wd_q = keep.tile([P, 2, H], U32, name="wd_q", align_bytes=ALIGN)
         wd_s = keep.tile([P, 2, H], U8, name="wd_s", align_bytes=ALIGN)
         wd_places = [
-            (stage, 0), (stage, WD_PIECE_BYTES + WC_GROUP_BYTES), (stage, 2 * WD_PIECE_BYTES + WC_GROUP_BYTES), (late, 0),
+            (stage, 0), (stage, WD_PIECE_BYTES + WC_GROUP_BYTES), (stage, 2 * WD_PIECE_BYTES + WC_GROUP_BYTES),
         ]
         wd_raw = []
         for piece, (pool, place) in enumerate(wd_places):
@@ -133,6 +135,29 @@ def tile_list_voxel_radiance_field_kernel(
             if piece == 0:
                 wc_raw.append(stage.tile([P, 2, GROUP // 2], I32, name="wc_raw1", offset=WD_PIECE_BYTES, align_bytes=ALIGN))
                 nc.sync.dma_start(wc_raw[1][:], wc_src[:, :, GROUP // 2 : GROUP])
+
+        last_raw = []
+        for part in range(2):
+            raw = late.tile(
+                [P, PACK, GROUP // 2], F32, name=f"wd_last{part}", offset=part * WD_PIECE_BYTES // 2, align_bytes=ALIGN
+            )
+            rows = wd[GROUP:, GROUP + part * GROUP // 2 : GROUP + (part + 1) * GROUP // 2]
+            nc.sync.dma_start(raw[:], rows.rearrange("(p i) e -> p i e", i=PACK))
+            last_raw.append(raw)
+
+        def quantise_last(part, grouped):
+            for pair in pairs:
+                nc.vector.tensor_copy(
+                    out=grouped[:].rearrange("p (t m i) -> p m i t", t=PACK, i=PACK)[:, :, :, pair],
+                    in_=last_raw[part][:].rearrange("p i (m t) -> p m i t", t=PACK)[:, :, :, pair],
+                )
+            for t in range(PACK):
+                first = GROUP + t * P + part * P // 2
+                cols = slice(first, first + P // 2)
+                nc.vector.quantize_mx(
+                    out=wd_q[:, 1, cols].bitcast(FP8X4), scales=wd_s[:, 1, cols],
+                    in_=grouped[:, t * GROUP // 2 : (t + 1) * GROUP // 2],
+                )
 
         def quantise_wd(piece, grouped):
             b, a = divmod(piece, 2)
@@ -154,7 +179,8 @@ def tile_list_voxel_radiance_field_kernel(
         deal_wc_words(1)
         quantise_wd(1, wd_bf[1])
         quantise_wd(2, wd_bf[2])
-        quantise_wd(3, turn.tile([P, PACK * GROUP], BF16, name="wd_bf3", offset=0, align_bytes=ALIGN))
+        quantise_last(0, keep.tile([P, PACK * GROUP // 2], BF16, name="wd_bf3", align_bytes=ALIGN))
+        quantise_last(1, turn.tile([P, PACK * GROUP // 2], BF16, name="wd_bf4", offset=0, align_bytes=ALIGN))
 
         def first_stage(bank, is_colour, b, voxels, ts, a):
             width = voxels.stop - voxels.start
@@ -189,19 +215,15 @@ def tile_list_voxel_radiance_field_kernel(
             x = runs(col[b], voxels, t)
             engine.tensor_scalar(out=x, in0=x, scalar1=factors[0], scalar2=factors[1], op0=ALU.mult, op1=factors[2])
 
-        def gain_factors(b):
-            tile = turn.tile([P, PACK], F32, name=f"factors{b}", offset=ALIGN, align_bytes=ALIGN)
-            nc.gpsimd.tensor_scalar(
-                out=tile[:], in0=gains[:, b, :], scalar1=-1.0 / LINEAR_FROM, scalar2=0.0, op0=ALU.mult, op1=ALU.add,
-            )
-            return tile
-
         for i, (is_colour, (b, voxels, ts)) in enumerate(turns[:BANKS]):
             first_stage(banks[i], is_colour, b, voxels, ts, 0)
         late_threshold = turn.tile([P, 1], F32, name="late_threshold", offset=0, align_bytes=ALIGN)
         threshold = late_threshold[:]
         nc.vector.memset(threshold, LINEAR_FROM)
-        factors = gain_factors(1)
+        factors = turn.tile([P, 2, PACK], F32, name="factors", offset=ALIGN, align_bytes=ALIGN)
+        nc.gpsimd.tensor_scalar(
+            out=factors[:], in0=gains[:], scalar1=-1.0 / LINEAR_FROM, scalar2=0.0, op0=ALU.mult, op1=ALU.add,
+        )
         for i, (is_colour, (b, voxels, ts)) in enumerate(turns):
             bank = banks[i % BANKS]
             for a in (1,) if i < BANKS else (0, 1):
@@ -215,10 +237,10 @@ def tile_list_voxel_radiance_field_kernel(
                     ACT.Tanh,
                 )
                 if b == 0 and voxels == quarters[1]:
-                    for t in ts:
+                    for t in range(ts[0], min(ts[-1] + 1, VECTOR_GAINS)):
                         gain(nc.vector, (gains[:, b, t : t + 1], -1.0 / LINEAR_FROM, ALU.mult), b, t, halves[0])
                 if b == 1 and voxels == halves[1]:
-                    gain(nc.gpsimd, (factors[:, t : t + 1], 0.0, ALU.add), b, t)
+                    gain(nc.gpsimd, (factors[:, b, t : t + 1], 0.0, ALU.add), b, t)
             else:
                 nc.scalar.activation(runs(dens[:, b], voxels, t), in_runs(bank), ACT.Sigmoid, scale=-1.0)
                 x = runs(col[b], voxels, t)
@@ -226,9 +248,10 @@ def tile_list_voxel_radiance_field_kernel(
                     out=x, in0=in_runs(bank), scalar=threshold, in1=x, op0=ALU.max, op1=ALU.mult,
                 )
 
-        factors = gain_factors(0)
-        for t in range(PACK):
-            gain(nc.gpsimd, (factors[:, t : t + 1], 0.0, ALU.add), 0, t, halves[1])
+        for t in range(VECTOR_GAINS, PACK):
+            gain(nc.gpsimd, (factors[:, 0, t : t + 1], 0.0, ALU.add), 0, t)
+        for t in range(VECTOR_GAINS):
+            gain(nc.gpsimd, (factors[:, 0, t : t + 1], 0.0, ALU.add), 0, t, halves[1])
 
         nc.scalar.activation(floor[:], dens[:, 1, S // RUN - 1, PACK - 3, 0:1], ACT.Copy, scale=0.0, bias=LOG_FLOOR)
 
@@ -255,11 +278,14 @@ def tile_list_voxel_radiance_field_kernel(
                 return [slice(0, FIRST_CUT), slice(FIRST_CUT, voxels.stop)]
             return [voxels]
 
-        for voxels in steps[:-2] + [slice(steps[-2].start, S)]:
+        def logarithms(voxels):
             for b in range(2):
                 for part in parts(b, voxels):
                     x = all_products(dens[:, b], part)
                     nc.scalar.activation(x, x, ACT.Ln, bias=floor[:])
+
+        for voxels in steps[:LOGS_AHEAD]:
+            logarithms(voxels)
 
         result = keep.tile([P, N // P, S], F32, name="result")
         out_v = out.rearrange("(n p) j -> p n j", p=P)
@@ -333,6 +359,8 @@ def tile_list_voxel_radiance_field_kernel(
             hidden(h_bf, 0, voxels)
             if pending is not None:
                 finish(*pending)
+                for later in steps[step - 1 + LOGS_AHEAD : step + LOGS_AHEAD]:
+                    logarithms(later)
             hidden(h_bf, 1, voxels)
             pending = (step, h_bf)
         finish_last(steps[-1], h_bf)

@@ -31,7 +31,7 @@ WD_PIECE_BYTES = 4 * PACK * GROUP
 LINEAR_FROM = 16.0
 LOG_FLOOR = 2.0**-60
 STEPS = (128, 256, 256, 128, 128, 128)
-FIRST_CUT = 64
+HALVED = 5
 LAST_BANKS = N // P
 
 
@@ -243,6 +243,11 @@ def tile_list_voxel_radiance_field_kernel(
                     gain(nc.gpsimd, (factors[:, b, t : t + 1], 0.0, ALU.add), b, t)
             else:
                 nc.scalar.activation(runs(dens[:, b], voxels, t), in_runs(bank), ACT.Sigmoid, scale=-1.0)
+                if i == len(turns) - 3:
+                    nc.vector.tensor_scalar(
+                        out=floor[:], in0=dens[:, b, S // RUN - 1, t, 0:1],
+                        scalar1=0.0, scalar2=LOG_FLOOR, op0=ALU.mult, op1=ALU.add,
+                    )
                 x = runs(col[b], voxels, t)
                 nc.vector.scalar_tensor_tensor(
                     out=x, in0=in_runs(bank), scalar=threshold, in1=x, op0=ALU.max, op1=ALU.mult,
@@ -253,7 +258,6 @@ def tile_list_voxel_radiance_field_kernel(
         for t in range(VECTOR_GAINS):
             gain(nc.gpsimd, (factors[:, 0, t : t + 1], 0.0, ALU.add), 0, t, halves[1])
 
-        nc.scalar.activation(floor[:], dens[:, 1, S // RUN - 1, PACK - 3, 0:1], ACT.Copy, scale=0.0, bias=LOG_FLOOR)
 
         wr_q = keep.tile([P, 2, N], I32, name="wr_q", tag="wd_bf0", align_bytes=ALIGN)
         wr_s = stage.tile([P, 2, N // 4], I32, name="wr_s", offset=0, align_bytes=ALIGN)
@@ -274,8 +278,9 @@ def tile_list_voxel_radiance_field_kernel(
             steps.append(slice(first, first + width))
 
         def parts(b, voxels):
-            if b == 0 and voxels.start == 0:
-                return [slice(0, FIRST_CUT), slice(FIRST_CUT, voxels.stop)]
+            if 2 * steps.index(voxels) + b < HALVED:
+                middle = (voxels.start + voxels.stop) // 2
+                return [slice(voxels.start, middle), slice(middle, voxels.stop)]
             return [voxels]
 
         def logarithms(voxels):
@@ -293,14 +298,13 @@ def tile_list_voxel_radiance_field_kernel(
         def hidden(h_bf, b, voxels):
             for part in parts(b, voxels):
                 local = slice(part.start - voxels.start, part.stop - voxels.start)
-                for pair in pairs:
-                    nc.vector.scalar_tensor_tensor(
-                        out=h_bf[:, b, :].rearrange("p (i x) -> p x i", i=RUN)[:, local, pair],
-                        in0=all_products(dens[:, b], part)[:, :, pair],
-                        scalar=-LINEAR_FROM,
-                        in1=all_products(col[b], part)[:, :, pair],
-                        op0=ALU.max, op1=ALU.mult,
-                    )
+                nc.vector.scalar_tensor_tensor(
+                    out=h_bf[:, b, :].rearrange("p (i x) -> p x i", i=RUN)[:, local, :],
+                    in0=all_products(dens[:, b], part),
+                    scalar=-LINEAR_FROM,
+                    in1=all_products(col[b], part)[:, :, 0:RUN],
+                    op0=ALU.max, op1=ALU.mult,
+                )
 
         def h_columns(voxels, b):
             width = voxels.stop - voxels.start
@@ -346,7 +350,7 @@ def tile_list_voxel_radiance_field_kernel(
                 )
                 for n in range(LAST_BANKS):
                     radiance_pass(banks[n][:, 0:width], n, b, voxels)
-            for n, copy in enumerate((nc.scalar.copy, nc.vector.tensor_copy, nc.scalar.copy)):
+            for n, copy in enumerate((nc.vector.tensor_copy, nc.vector.tensor_copy, nc.scalar.copy)):
                 copy(
                     result[:, n, voxels].rearrange("p (c i) -> p c i", i=RUN),
                     banks[n][:, 0:width].rearrange("p (i c) -> p c i", i=RUN),
@@ -359,7 +363,7 @@ def tile_list_voxel_radiance_field_kernel(
             hidden(h_bf, 0, voxels)
             if pending is not None:
                 finish(*pending)
-                for later in steps[step - 1 + LOGS_AHEAD : step + LOGS_AHEAD]:
+                for later in {1: steps[3:4], 2: steps[4:]}.get(step, []):
                     logarithms(later)
             hidden(h_bf, 1, voxels)
             pending = (step, h_bf)

@@ -27,6 +27,7 @@ LOGS_AHEAD = 3
 RUN = 4
 ALIGN = 64
 WC_GROUP_BYTES = 2 * 2 * GROUP
+WC_BYTES = 2 * WC_GROUP_BYTES
 WD_PIECE_BYTES = 4 * PACK * GROUP
 LINEAR_FROM = 16.0
 LOG_FLOOR = 2.0**-60
@@ -53,7 +54,7 @@ def tile_list_voxel_radiance_field_kernel(
         nc.sync.dma_start(offsets[:], offs)
         warm = keep.tile([P, 1], F32, name="warm", align_bytes=ALIGN)
         warm_out = keep.tile([P, 1], F32, name="warm_out", align_bytes=ALIGN)
-        tab_s = late.tile([P, T // 4], I32, name="tab_s", offset=0, align_bytes=ALIGN)
+        tab_s = late.tile([P, T // 4], I32, name="tab_s", offset=WC_BYTES - ALIGN, align_bytes=ALIGN)
         wc_s_raw = keep.tile([P, 2, H // 4], I32, name="wc_s_raw", align_bytes=ALIGN)
         v_s = keep.tile([P, 2, S // 4], I32, name="v_s", align_bytes=ALIGN)
 
@@ -66,7 +67,7 @@ def tile_list_voxel_radiance_field_kernel(
         wc_raw = [keep.tile([P, 2, GROUP // 2], I32, name="wc_raw0", align_bytes=ALIGN)]
         wc_src = wc_words.rearrange("a p e -> p a e").bitcast(I32)
         nc.sync.dma_start(tab_s[0:32, :], tab_scales.rearrange("a q t -> (a q) t").bitcast(I32))
-        nc.sync.dma_start(wc_raw[0][:], wc_src[:, :, 0 : GROUP // 2])
+        nc.scalar.dma_start(wc_raw[0][:], wc_src[:, :, 0 : GROUP // 2])
         for q in range(4):
             nc.sync.dma_start(
                 wc_s_raw[32 * q : 32 * q + 4, :, :],
@@ -86,7 +87,7 @@ def tile_list_voxel_radiance_field_kernel(
                 row = 16 * a + 4 * q
                 nc.scalar.dma_start(v_s[32 * q : 32 * q + 4, a, :], picked_s[row : row + 4, :].bitcast(I32))
 
-        tab_w.append(late.tile([P, T], I32, name="tab_w1", offset=0, align_bytes=ALIGN))
+        tab_w.append(late.tile([P, T], I32, name="tab_w1", offset=WC_BYTES, align_bytes=ALIGN))
         move_scale_rows(0)
         nc.scalar.dma_start(tab_w[1][:], tab_words[1].rearrange("p t i -> p (t i)").bitcast(I32))
         move_scale_rows(1)
@@ -95,7 +96,7 @@ def tile_list_voxel_radiance_field_kernel(
 
         pairs = [slice(0, 2), slice(2, 4)]
 
-        wc_q = keep.tile([P, 2, 2 * H], U8, name="wc_q", align_bytes=ALIGN)
+        wc_q = late.tile([P, 2, 2 * H], U8, name="wc_q", offset=0, align_bytes=ALIGN)
         wc_s = keep.tile([P, 2, H], U8, name="wc_s", align_bytes=ALIGN)
 
         def deal_wc_words(b):
@@ -139,7 +140,7 @@ def tile_list_voxel_radiance_field_kernel(
         last_raw = []
         for part in range(2):
             raw = late.tile(
-                [P, PACK, GROUP // 2], F32, name=f"wd_last{part}", offset=part * WD_PIECE_BYTES // 2, align_bytes=ALIGN
+                [P, PACK, GROUP // 2], F32, name=f"wd_last{part}", offset=WC_BYTES + part * WD_PIECE_BYTES // 2, align_bytes=ALIGN
             )
             rows = wd[GROUP:, GROUP + part * GROUP // 2 : GROUP + (part + 1) * GROUP // 2]
             nc.sync.dma_start(raw[:], rows.rearrange("(p i) e -> p i e", i=PACK))

@@ -56,13 +56,14 @@ def tile_list_voxel_radiance_field_kernel(
         warm_out = keep.tile([P, 1], F32, name="warm_out", align_bytes=ALIGN)
         tab_s = late.tile([P, T // 4], I32, name="tab_s", offset=WC_BYTES - ALIGN, align_bytes=ALIGN)
         wc_s_raw = keep.tile([P, 2, H // 4], I32, name="wc_s_raw", align_bytes=ALIGN)
-        v_s = keep.tile([P, 2, S // 4], I32, name="v_s", align_bytes=ALIGN)
+        v_s = [keep.tile([P, S // 4], I32, name=f"v_s{a}", align_bytes=ALIGN) for a in range(2)]
 
         nc.gpsimd.memset(wc_s_raw[:], 0)
         nc.gpsimd.memset(warm[:], 0.0)
         nc.vector.memset(tab_s[32:64, :], 0)
         nc.vector.memset(tab_s[64:128, :], 0)
-        nc.vector.memset(v_s[:], 0)
+        for plane in v_s:
+            nc.vector.memset(plane[:], 0)
 
         wc_raw = [keep.tile([P, 2, GROUP // 2], I32, name="wc_raw0", align_bytes=ALIGN)]
         wc_src = wc_words.rearrange("a p e -> p a e").bitcast(I32)
@@ -70,8 +71,8 @@ def tile_list_voxel_radiance_field_kernel(
         nc.scalar.dma_start(wc_raw[0][:], wc_src[:, :, 0 : GROUP // 2])
         for q in range(4):
             nc.sync.dma_start(
-                wc_s_raw[32 * q : 32 * q + 4, :, :],
-                wc_scales[:, 4 * q : 4 * q + 4, :].rearrange("a r e -> r a e").bitcast(I32),
+                wc_s_raw[q:P:32, :, :],
+                wc_scales[:, q:16:4, :].rearrange("a r e -> r a e").bitcast(I32),
             )
 
         nc.scalar.activation(warm_out[:], warm[:], ACT.Sigmoid)
@@ -84,8 +85,7 @@ def tile_list_voxel_radiance_field_kernel(
 
         def move_scale_rows(a):
             for q in range(4):
-                row = 16 * a + 4 * q
-                nc.scalar.dma_start(v_s[32 * q : 32 * q + 4, a, :], picked_s[row : row + 4, :].bitcast(I32))
+                nc.scalar.dma_start(v_s[a][q:P:32, :], picked_s[16 * a + q : 16 * (a + 1) : 4, :].bitcast(I32))
 
         tab_w.append(late.tile([P, T], I32, name="tab_w1", offset=WC_BYTES, align_bytes=ALIGN))
         move_scale_rows(0)
@@ -193,7 +193,7 @@ def tile_list_voxel_radiance_field_kernel(
                     lhs, lhs_scale = wd_q[:, a, c0 : c0 + P].bitcast(FP8X4), wd_s[:, a, c0 : c0 + P]
                 nc.tensor.matmul_mx(
                     out=bank[:, (t - ts[0]) * width : (t - ts[0] + 1) * width], lhsT=lhs, lhsT_scale=lhs_scale,
-                    rhs=v_w[a][:, voxels].bitcast(FP8X4), rhs_scale=v_s[:, a, :].bitcast(U8)[:, voxels],
+                    rhs=v_w[a][:, voxels].bitcast(FP8X4), rhs_scale=v_s[a][:].bitcast(U8)[:, voxels],
                     start=(a == 0 and t == ts[0]), stop=(a == 1 and t == ts[-1]),
                 )
 
@@ -266,8 +266,8 @@ def tile_list_voxel_radiance_field_kernel(
         nc.vector.memset(wr_s[:], 0)
         for q in range(4):
             nc.sync.dma_start(
-                wr_s[32 * q : 32 * q + 4, :, :],
-                wr_scales[:, 4 * q : 4 * q + 4, :].rearrange("a r n -> r a n").bitcast(I32),
+                wr_s[q:P:32, :, :],
+                wr_scales[:, q:16:4, :].rearrange("a r n -> r a n").bitcast(I32),
             )
 
         def all_products(tile, voxels):

@@ -199,7 +199,11 @@ def tile_list_voxel_radiance_field_kernel(
 
         whole = [(b, half, (t,)) for b in range(2) for half in halves for t in range(PACK)]
         colours = [(0, quarter, ts) for quarter in quarters for ts in ((0, 1), (2, 3))] + whole[PACK:]
-        turns = [(True, c) for c in colours] + [(False, d) for d in whole]
+        last = [(0, halves[1], (t,)) for t in range(VECTOR_GAINS)]
+        densities = [d for d in whole[:BANKS] if d not in last]
+        held = len(densities)
+        densities = densities + [(1, half, (t,)) for t in range(PACK) for half in halves] + last
+        turns = [(True, c) for c in colours] + [(False, d) for d in densities]
         dens = keep.tile([P, 2, S // RUN, PACK, RUN], F32, name="dens", align_bytes=ALIGN)
         col = [keep.tile([P, S // RUN, PACK, 2 * RUN], F32, name=f"col{b}", align_bytes=ALIGN) for b in range(2)]
         floor = keep.tile([P, 1], F32, name="floor")
@@ -244,20 +248,20 @@ def tile_list_voxel_radiance_field_kernel(
                     gain(nc.gpsimd, (factors[:, b, t : t + 1], 0.0, ALU.add), b, t)
             else:
                 nc.scalar.activation(runs(dens[:, b], voxels, t), in_runs(bank), ACT.Sigmoid, scale=-1.0)
-                if i == len(turns) - 3:
+                if i == len(turns) - 6:
                     nc.vector.tensor_scalar(
-                        out=floor[:], in0=dens[:, b, S // RUN - 1, t, 0:1],
+                        out=floor[:], in0=dens[:, b, voxels.start // RUN, t, 0:1],
                         scalar1=0.0, scalar2=LOG_FLOOR, op0=ALU.mult, op1=ALU.add,
                     )
                 x = runs(col[b], voxels, t)
                 nc.vector.scalar_tensor_tensor(
-                    out=x, in0=in_runs(bank), scalar=threshold, in1=x, op0=ALU.max, op1=ALU.mult,
+                    out=x, in0=in_runs(bank), scalar=threshold if i < len(colours) + held else LINEAR_FROM, in1=x, op0=ALU.max, op1=ALU.mult,
                 )
 
         for t in range(VECTOR_GAINS, PACK):
             gain(nc.gpsimd, (factors[:, 0, t : t + 1], 0.0, ALU.add), 0, t)
         for t in range(VECTOR_GAINS):
-            gain(nc.gpsimd, (factors[:, 0, t : t + 1], 0.0, ALU.add), 0, t, halves[1])
+            gain(nc.vector, (gains[:, 0, t : t + 1], -1.0 / LINEAR_FROM, ALU.mult), 0, t, halves[1])
 
 
         wr_q = keep.tile([P, 2, N], I32, name="wr_q", tag="wd_bf0", align_bytes=ALIGN)

@@ -126,6 +126,8 @@ def tile_list_voxel_radiance_field_kernel(
         wd_places = [
             (stage, 0), (stage, WD_PIECE_BYTES + WC_GROUP_BYTES), (stage, 2 * WD_PIECE_BYTES + WC_GROUP_BYTES),
         ]
+        wc_raw.append(stage.tile([P, 2, GROUP // 2], I32, name="wc_raw1", offset=WD_PIECE_BYTES, align_bytes=ALIGN))
+        nc.sync.dma_start(wc_raw[1][:], wc_src[:, :, GROUP // 2 : GROUP])
         wd_raw = []
         for piece, (pool, place) in enumerate(wd_places):
             b, a = divmod(piece, 2)
@@ -133,9 +135,6 @@ def tile_list_voxel_radiance_field_kernel(
             rows = wd[a * GROUP : (a + 1) * GROUP, b * GROUP : (b + 1) * GROUP]
             nc.sync.dma_start(raw[:], rows.rearrange("(p i) e -> p i e", i=PACK))
             wd_raw.append(raw)
-            if piece == 0:
-                wc_raw.append(stage.tile([P, 2, GROUP // 2], I32, name="wc_raw1", offset=WD_PIECE_BYTES, align_bytes=ALIGN))
-                nc.sync.dma_start(wc_raw[1][:], wc_src[:, :, GROUP // 2 : GROUP])
 
         last_raw = []
         for part in range(2):
@@ -176,8 +175,8 @@ def tile_list_voxel_radiance_field_kernel(
                 )
 
         wd_bf = [keep.tile([P, PACK * GROUP], BF16, name=f"wd_bf{n}", tag=f"wd_bf{n}", align_bytes=ALIGN) for n in range(3)]
-        quantise_wd(0, wd_bf[0])
         deal_wc_words(1)
+        quantise_wd(0, wd_bf[0])
         quantise_wd(1, wd_bf[1])
         quantise_wd(2, wd_bf[2])
         quantise_last(0, keep.tile([P, PACK * GROUP // 2], BF16, name="wd_bf3", align_bytes=ALIGN))

@@ -27,8 +27,8 @@ LOGS_AHEAD = 3
 RUN = 4
 ALIGN = 64
 WC_GROUP_BYTES = 2 * 2 * GROUP
-WC_BYTES = 2 * WC_GROUP_BYTES
 WD_PIECE_BYTES = 4 * PACK * GROUP
+WC_BYTES = 2 * WC_GROUP_BYTES
 LINEAR_FROM = 16.0
 LOG_FLOOR = 2.0**-60
 STEPS = (128, 256, 256, 128, 128, 128)
@@ -42,8 +42,8 @@ def tile_list_voxel_radiance_field_kernel(
     nc = tc.nc
     with ExitStack() as ctx:
         keep = ctx.enter_context(tc.tile_pool(name="keep", bufs=1))
-        ring = ctx.enter_context(tc.tile_pool(name="ring", bufs=3))
         stage = ctx.enter_context(tc.tile_pool(name="stage", bufs=1))
+        early = ctx.enter_context(tc.tile_pool(name="early", bufs=1))
         late = ctx.enter_context(tc.tile_pool(name="late", bufs=1))
         turn = ctx.enter_context(tc.tile_pool(name="turn", bufs=1))
         psum = ctx.enter_context(tc.psum_pool(name="psum", bufs=1))
@@ -54,50 +54,52 @@ def tile_list_voxel_radiance_field_kernel(
         nc.sync.dma_start(offsets[:], offs)
         warm = keep.tile([P, 1], F32, name="warm", align_bytes=ALIGN)
         warm_out = keep.tile([P, 1], F32, name="warm_out", align_bytes=ALIGN)
-        tab_s = late.tile([P, T // 4], I32, name="tab_s", offset=WC_BYTES - ALIGN, align_bytes=ALIGN)
+        tab_s = early.tile([P, T // 4], I32, name="tab_s", offset=WC_BYTES - ALIGN, align_bytes=ALIGN)
         wc_s_raw = keep.tile([P, 2, H // 4], I32, name="wc_s_raw", align_bytes=ALIGN)
-        v_s = [keep.tile([P, S // 4], I32, name=f"v_s{a}", align_bytes=ALIGN) for a in range(2)]
+        planes = [keep.tile([P, S // 4], I32, name=f"v_s{a}", align_bytes=ALIGN) for a in range(2)]
 
         nc.gpsimd.memset(wc_s_raw[:], 0)
         nc.gpsimd.memset(warm[:], 0.0)
         nc.vector.memset(tab_s[32:64, :], 0)
         nc.vector.memset(tab_s[64:128, :], 0)
-        for plane in v_s:
+        for plane in planes:
             nc.vector.memset(plane[:], 0)
 
-        wc_raw = [keep.tile([P, 2, GROUP // 2], I32, name="wc_raw0", align_bytes=ALIGN)]
+        wc_raw = [late.tile([P, 2, GROUP // 2], I32, name="wc_raw0", offset=0, align_bytes=ALIGN)]
         wc_src = wc_words.rearrange("a p e -> p a e").bitcast(I32)
         nc.sync.dma_start(tab_s[0:32, :], tab_scales.rearrange("a q t -> (a q) t").bitcast(I32))
         nc.scalar.dma_start(wc_raw[0][:], wc_src[:, :, 0 : GROUP // 2])
-        for q in range(4):
-            nc.sync.dma_start(
-                wc_s_raw[q:P:32, :, :],
-                wc_scales[:, q:16:4, :].rearrange("a r e -> r a e").bitcast(I32),
+        for r, queue in enumerate((nc.sync, nc.sync, nc.scalar, nc.scalar)):
+            queue.dma_start(
+                wc_s_raw[r:P:32, :, :],
+                wc_scales[:, r:16:4, :].rearrange("a r e -> r a e").bitcast(I32),
             )
 
         nc.scalar.activation(warm_out[:], warm[:], ACT.Sigmoid)
 
-        tab_w = [stage.tile([P, T], I32, name="tab_w0", offset=WD_PIECE_BYTES - ALIGN, align_bytes=ALIGN)]
-        nc.sync.dma_start(tab_w[0][:], tab_words[0].rearrange("p t i -> p (t i)").bitcast(I32))
+        tab_w = [
+            stage.tile([P, T], I32, name="tab_w0", offset=WD_PIECE_BYTES - ALIGN, align_bytes=ALIGN),
+            late.tile([P, T], I32, name="tab_w1", offset=0, align_bytes=ALIGN),
+        ]
+        for a in range(2):
+            nc.sync.dma_start(tab_w[a][:], tab_words[a].rearrange("p t i -> p (t i)").bitcast(I32))
 
         picked_s = keep.tile([P, S], U8, name="picked_s", align_bytes=ALIGN)
         nc.vector.tensor_copy(picked_s[:], tab_s[:].bitcast(U8).indirect(offsets[:]))
-
-        def move_scale_rows(a):
-            for q in range(4):
-                nc.scalar.dma_start(v_s[a][q:P:32, :], picked_s[16 * a + q : 16 * (a + 1) : 4, :].bitcast(I32))
-
-        tab_w.append(late.tile([P, T], I32, name="tab_w1", offset=WC_BYTES, align_bytes=ALIGN))
-        move_scale_rows(0)
-        nc.scalar.dma_start(tab_w[1][:], tab_words[1].rearrange("p t i -> p (t i)").bitcast(I32))
-        move_scale_rows(1)
+        for a in range(2):
+            for r in range(4):
+                nc.scalar.dma_start(planes[a][r:P:32, :], picked_s[16 * a + r : 16 * (a + 1) : 4, :].bitcast(I32))
+        v_s = [plane[:].bitcast(U8) for plane in planes]
         gains = keep.tile([P, 2, PACK], F32, name="gains", align_bytes=ALIGN)
         nc.gpsimd.dma_start(gains[:], gain.rearrange("(b p t) -> p b t", b=2, t=PACK))
 
         pairs = [slice(0, 2), slice(2, 4)]
 
-        wc_q = late.tile([P, 2, 2 * H], U8, name="wc_q", offset=0, align_bytes=ALIGN)
-        wc_s = keep.tile([P, 2, H], U8, name="wc_s", align_bytes=ALIGN)
+        wc_q = early.tile([P, 2, 2 * H], U8, name="wc_q", offset=0, align_bytes=ALIGN)
+        wc_s = [
+            keep.tile([P, 2, GROUP], U8, name="wc_s0", align_bytes=ALIGN),
+            keep.tile([P, 2, GROUP], U8, name="wc_s1", align_bytes=ALIGN),
+        ]
 
         def deal_wc_words(b):
             for pair in pairs:
@@ -106,12 +108,16 @@ def tile_list_voxel_radiance_field_kernel(
                     in_=wc_raw[b][:].bitcast(U16).rearrange("p a (m t) -> p a m t", t=PACK)[:, :, :, pair],
                 )
 
+        def deal_wc_scales(b):
+            for pair in pairs:
+                nc.vector.tensor_copy(
+                    out=wc_s[b][:].rearrange("p a (t m) -> p a m t", t=PACK)[:, :, :, pair],
+                    in_=wc_s_raw[:].bitcast(U8).rearrange("p a (b m t) -> p a b m t", b=2, t=PACK)[:, :, b, :, pair],
+                )
+
         deal_wc_words(0)
-        for pair in pairs:
-            nc.vector.tensor_copy(
-                out=wc_s[:].rearrange("p a (b t m) -> p (a b) m t", b=2, t=PACK)[:, :, :, pair],
-                in_=wc_s_raw[:].bitcast(U8).rearrange("p a (b m t) -> p (a b) m t", b=2, t=PACK)[:, :, :, pair],
-            )
+        deal_wc_scales(0)
+        deal_wc_scales(1)
 
         halves = [slice(0, HALF), slice(HALF, S)]
         v_w = [keep.tile([P, S], U32, name=f"v_w{a}", align_bytes=ALIGN) for a in range(2)]
@@ -123,23 +129,21 @@ def tile_list_voxel_radiance_field_kernel(
 
         wd_q = keep.tile([P, 2, H], U32, name="wd_q", align_bytes=ALIGN)
         wd_s = keep.tile([P, 2, H], U8, name="wd_s", align_bytes=ALIGN)
-        wd_places = [
-            (stage, 0), (stage, WD_PIECE_BYTES + WC_GROUP_BYTES), (stage, 2 * WD_PIECE_BYTES + WC_GROUP_BYTES),
-        ]
+
         wc_raw.append(stage.tile([P, 2, GROUP // 2], I32, name="wc_raw1", offset=WD_PIECE_BYTES, align_bytes=ALIGN))
         nc.sync.dma_start(wc_raw[1][:], wc_src[:, :, GROUP // 2 : GROUP])
         wd_raw = []
-        for piece, (pool, place) in enumerate(wd_places):
+        for piece in range(3):
             b, a = divmod(piece, 2)
-            raw = pool.tile([P, PACK, GROUP], F32, name=f"wd_raw{piece}", offset=place, align_bytes=ALIGN)
+            place = piece * WD_PIECE_BYTES + (WC_GROUP_BYTES + 2 * GROUP if piece else 0)
+            raw = stage.tile([P, PACK, GROUP], F32, name=f"wd_raw{piece}", offset=place, align_bytes=ALIGN)
             rows = wd[a * GROUP : (a + 1) * GROUP, b * GROUP : (b + 1) * GROUP]
             nc.sync.dma_start(raw[:], rows.rearrange("(p i) e -> p i e", i=PACK))
             wd_raw.append(raw)
-
         last_raw = []
         for part in range(2):
             raw = late.tile(
-                [P, PACK, GROUP // 2], F32, name=f"wd_last{part}", offset=WC_BYTES + part * WD_PIECE_BYTES // 2, align_bytes=ALIGN
+                [P, PACK, GROUP // 2], F32, name=f"wd_last{part}", offset=part * WD_PIECE_BYTES // 2, align_bytes=ALIGN
             )
             rows = wd[GROUP:, GROUP + part * GROUP // 2 : GROUP + (part + 1) * GROUP // 2]
             nc.sync.dma_start(raw[:], rows.rearrange("(p i) e -> p i e", i=PACK))
@@ -187,12 +191,12 @@ def tile_list_voxel_radiance_field_kernel(
             for t in ts:
                 c0 = b * GROUP + t * P
                 if is_colour:
-                    lhs, lhs_scale = wc_q[:, a, 2 * c0 : 2 * (c0 + P)].bitcast(FP4X4), wc_s[:, a, c0 : c0 + P]
+                    lhs, lhs_scale = wc_q[:, a, 2 * c0 : 2 * (c0 + P)].bitcast(FP4X4), wc_s[b][:, a, t * P : (t + 1) * P]
                 else:
                     lhs, lhs_scale = wd_q[:, a, c0 : c0 + P].bitcast(FP8X4), wd_s[:, a, c0 : c0 + P]
                 nc.tensor.matmul_mx(
                     out=bank[:, (t - ts[0]) * width : (t - ts[0] + 1) * width], lhsT=lhs, lhsT_scale=lhs_scale,
-                    rhs=v_w[a][:, voxels].bitcast(FP8X4), rhs_scale=v_s[a][:].bitcast(U8)[:, voxels],
+                    rhs=v_w[a][:, voxels].bitcast(FP8X4), rhs_scale=v_s[a][:, voxels],
                     start=(a == 0 and t == ts[0]), stop=(a == 1 and t == ts[-1]),
                 )
 
@@ -267,10 +271,10 @@ def tile_list_voxel_radiance_field_kernel(
         wr_s = stage.tile([P, 2, N // 4], I32, name="wr_s", offset=0, align_bytes=ALIGN)
         nc.sync.dma_start(wr_q[:], wr_words.rearrange("a p n i -> p a (n i)").bitcast(I32))
         nc.vector.memset(wr_s[:], 0)
-        for q in range(4):
+        for r in range(4):
             nc.sync.dma_start(
-                wr_s[q:P:32, :, :],
-                wr_scales[:, q:16:4, :].rearrange("a r n -> r a n").bitcast(I32),
+                wr_s[r:P:32, :, :],
+                wr_scales[:, r:16:4, :].rearrange("a r n -> r a n").bitcast(I32),
             )
 
         def all_products(tile, voxels):
@@ -363,7 +367,10 @@ def tile_list_voxel_radiance_field_kernel(
 
         pending = None
         for step, voxels in enumerate(steps):
-            h_bf = ring.tile([P, 2, PACK * (voxels.stop - voxels.start)], BF16, name="h_bf", align_bytes=ALIGN)
+            h_bf = late.tile(
+                [P, 2, PACK * (voxels.stop - voxels.start)], BF16, name=f"h_bf{step}",
+                offset=4 * PACK * voxels.start, align_bytes=ALIGN,
+            )
             hidden(h_bf, 0, voxels)
             if pending is not None:
                 finish(*pending)

@@ -122,8 +122,8 @@ def tile_list_voxel_radiance_field_kernel(
         halves = [slice(0, HALF), slice(HALF, S)]
         v_w = [keep.tile([P, S], U32, name=f"v_w{a}", align_bytes=ALIGN) for a in range(2)]
         quarters = [slice(0, QUARTER), slice(QUARTER, HALF)]
-        for a, pieces in enumerate((halves, quarters + halves[1:])):
-            for piece in pieces:
+        for a in range(2):
+            for piece in quarters + halves[1:]:
                 entries = offsets[:, piece.start // 16 : piece.stop // 16]
                 nc.vector.tensor_copy(v_w[a][:, piece], tab_w[a][:].bitcast(U32).indirect(entries))
 
@@ -286,6 +286,9 @@ def tile_list_voxel_radiance_field_kernel(
             steps.append(slice(first, first + width))
 
         def parts(b, voxels):
+            if steps.index(voxels) == 1 and b == 0:
+                cuts = [voxels.start + c for c in (0, 64, 128, 256)]
+                return [slice(lo, hi) for lo, hi in zip(cuts, cuts[1:])]
             if 2 * steps.index(voxels) + b < HALVED:
                 middle = (voxels.start + voxels.stop) // 2
                 return [slice(voxels.start, middle), slice(middle, voxels.stop)]
@@ -303,8 +306,8 @@ def tile_list_voxel_radiance_field_kernel(
         result = keep.tile([P, N // P, S], F32, name="result")
         out_v = out.rearrange("(n p) j -> p n j", p=P)
 
-        def hidden(h_bf, b, voxels):
-            for part in parts(b, voxels):
+        def hidden(h_bf, b, voxels, which=slice(None)):
+            for part in parts(b, voxels)[which]:
                 local = slice(part.start - voxels.start, part.stop - voxels.start)
                 nc.vector.scalar_tensor_tensor(
                     out=h_bf[:, b, :].rearrange("p (i x) -> p x i", i=RUN)[:, local, :],
@@ -371,11 +374,12 @@ def tile_list_voxel_radiance_field_kernel(
                 [P, 2, PACK * (voxels.stop - voxels.start)], BF16, name=f"h_bf{step}",
                 offset=4 * PACK * voxels.start, align_bytes=ALIGN,
             )
-            hidden(h_bf, 0, voxels)
+            hidden(h_bf, 0, voxels, slice(0, 1))
             if pending is not None:
                 finish(*pending)
                 for later in {1: steps[3:4], 2: steps[4:]}.get(step, []):
                     logarithms(later)
+            hidden(h_bf, 0, voxels, slice(1, None))
             hidden(h_bf, 1, voxels)
             pending = (step, h_bf)
         finish_last(steps[-1], h_bf)

from contextlib import ExitStack

import concourse.mybir as mybir

K, H, N, T, S = 1024, 1024, 384, 4096, 1024
FLOPS = 2 * (2 * K * H * S + H * N * S)

F32 = mybir.dt.float32
BF16 = mybir.dt.bfloat16
I32 = mybir.dt.int32
U32 = mybir.dt.uint32
U16 = mybir.dt.uint16
U8 = mybir.dt.uint8
FP8X4 = mybir.dt.float8_e4m3fn_x4
FP4X4 = mybir.dt.float4_e2m1fn_x4
ACT = mybir.ActivationFunctionType
ALU = mybir.AluOpType

P = 128
PACK = 4
GROUP = P * PACK
HALF = 512
QUARTER = 256
BANKS = 8
VECTOR_GAINS = 2
LOGS_AHEAD = 3
RUN = 4
ALIGN = 64
WC_GROUP_BYTES = 2 * 2 * GROUP
WD_PIECE_BYTES = 4 * PACK * GROUP
WC_BYTES = 2 * WC_GROUP_BYTES
LINEAR_FROM = 16.0
LOG_FLOOR = 2.0**-60
STEPS = (128, 256, 256, 128, 128, 128)
HALVED = 5
LAST_BANKS = N // P


def tile_list_voxel_radiance_field_kernel(
    tc, tab_words, tab_scales, offs, wd, wc_words, wc_scales, gain, wr_words, wr_scales, out
):
    nc = tc.nc
    with ExitStack() as ctx:
        keep = ctx.enter_context(tc.tile_pool(name="keep", bufs=1))
        stage = ctx.enter_context(tc.tile_pool(name="stage", bufs=1))
        early = ctx.enter_context(tc.tile_pool(name="early", bufs=1))
        late = ctx.enter_context(tc.tile_pool(name="late", bufs=1))
        turn = ctx.enter_context(tc.tile_pool(name="turn", bufs=1))
        psum = ctx.enter_context(tc.psum_pool(name="psum", bufs=1))

        banks = [psum.tile([P, HALF], F32, name=f"bank{i}") for i in range(BANKS)]

        offsets = keep.tile([P, S // 16], U16, name="offsets")
        nc.sync.dma_start(offsets[:], offs)
        warm = keep.tile([P, 1], F32, name="warm", align_bytes=ALIGN)
        warm_out = keep.tile([P, 1], F32, name="warm_out", align_bytes=ALIGN)
        tab_s = early.tile([P, T // 4], I32, name="tab_s", offset=WC_BYTES - ALIGN, align_bytes=ALIGN)
        wc_s_raw = keep.tile([P, 2, H // 4], I32, name="wc_s_raw", align_bytes=ALIGN)
        planes = [keep.tile([P, S // 4], I32, name=f"v_s{a}", align_bytes=ALIGN) for a in range(2)]

        nc.gpsimd.memset(wc_s_raw[:], 0)
        nc.gpsimd.memset(warm[:], 0.0)
        nc.vector.memset(tab_s[32:64, :], 0)
        nc.vector.memset(tab_s[64:128, :], 0)
        for plane in planes:
            nc.vector.memset(plane[:], 0)

        wc_raw = [late.tile([P, 2, GROUP // 2], I32, name="wc_raw0", offset=0, align_bytes=ALIGN)]
        wc_src = wc_words.rearrange("a p e -> p a e").bitcast(I32)
        nc.sync.dma_start(tab_s[0:32, :], tab_scales.rearrange("a q t -> (a q) t").bitcast(I32))
        nc.scalar.dma_start(wc_raw[0][:], wc_src[:, :, 0 : GROUP // 2])
        for r, queue in enumerate((nc.sync, nc.sync, nc.scalar, nc.scalar)):
            queue.dma_start(
                wc_s_raw[r:P:32, :, :],
                wc_scales[:, r:16:4, :].rearrange("a r e -> r a e").bitcast(I32),
            )

        nc.scalar.activation(warm_out[:], warm[:], ACT.Sigmoid)

        tab_w = [
            stage.tile([P, T], I32, name="tab_w0", offset=WD_PIECE_BYTES - ALIGN, align_bytes=ALIGN),
            late.tile([P, T], I32, name="tab_w1", offset=0, align_bytes=ALIGN),
        ]
        for a in range(2):
            nc.sync.dma_start(tab_w[a][:], tab_words[a].rearrange("p t i -> p (t i)").bitcast(I32))

        picked_s = keep.tile([P, S], U8, name="picked_s", align_bytes=ALIGN)
        nc.vector.tensor_copy(picked_s[:], tab_s[:].bitcast(U8).indirect(offsets[:]))
        for a in range(2):
            for r in range(4):
                nc.scalar.dma_start(planes[a][r:P:32, :], picked_s[16 * a + r : 16 * (a + 1) : 4, :].bitcast(I32))
        v_s = [plane[:].bitcast(U8) for plane in planes]
        gains = keep.tile([P, 2, PACK], F32, name="gains", align_bytes=ALIGN)
        nc.gpsimd.dma_start(gains[:], gain.rearrange("(b p t) -> p b t", b=2, t=PACK))

        pairs = [slice(0, 2), slice(2, 4)]

        wc_q = early.tile([P, 2, 2 * H], U8, name="wc_q", offset=0, align_bytes=ALIGN)
        wc_s = [
            keep.tile([P, 2, GROUP], U8, name="wc_s0", align_bytes=ALIGN),
            keep.tile([P, 2, GROUP], U8, name="wc_s1", align_bytes=ALIGN),
        ]

        def deal_wc_words(b):
            for pair in pairs:
                nc.vector.tensor_copy(
                    out=wc_q[:].bitcast(U16).rearrange("p a (b t m) -> p a b m t", b=2, t=PACK)[:, :, b, :, pair],
                    in_=wc_raw[b][:].bitcast(U16).rearrange("p a (m t) -> p a m t", t=PACK)[:, :, :, pair],
                )

        def deal_wc_scales(b):
            for pair in pairs:
                nc.vector.tensor_copy(
                    out=wc_s[b][:].rearrange("p a (t m) -> p a m t", t=PACK)[:, :, :, pair],
                    in_=wc_s_raw[:].bitcast(U8).rearrange("p a (b m t) -> p a b m t", b=2, t=PACK)[:, :, b, :, pair],
                )

        deal_wc_words(0)
        deal_wc_scales(0)
        deal_wc_scales(1)

        halves = [slice(0, HALF), slice(HALF, S)]
        v_w = [keep.tile([P, S], U32, name=f"v_w{a}", align_bytes=ALIGN) for a in range(2)]
        quarters = [slice(0, QUARTER), slice(QUARTER, HALF)]
        for a in range(2):
            for piece in quarters + halves[1:]:
                entries = offsets[:, piece.start // 16 : piece.stop // 16]
                nc.vector.tensor_copy(v_w[a][:, piece], tab_w[a][:].bitcast(U32).indirect(entries))

        wd_q = keep.tile([P, 2, H], U32, name="wd_q", align_bytes=ALIGN)
        wd_s = keep.tile([P, 2, H], U8, name="wd_s", align_bytes=ALIGN)

        wc_raw.append(stage.tile([P, 2, GROUP // 2], I32, name="wc_raw1", offset=WD_PIECE_BYTES, align_bytes=ALIGN))
        nc.sync.dma_start(wc_raw[1][:], wc_src[:, :, GROUP // 2 : GROUP])
        wd_raw = []
        for piece in range(3):
            b, a = divmod(piece, 2)
            place = piece * WD_PIECE_BYTES + (WC_GROUP_BYTES + 2 * GROUP if piece else 0)
            raw = stage.tile([P, PACK, GROUP], F32, name=f"wd_raw{piece}", offset=place, align_bytes=ALIGN)
            rows = wd[a * GROUP : (a + 1) * GROUP, b * GROUP : (b + 1) * GROUP]
            nc.sync.dma_start(raw[:], rows.rearrange("(p i) e -> p i e", i=PACK))
            wd_raw.append(raw)
        last_raw = []
        for part in range(2):
            raw = late.tile(
                [P, PACK, GROUP // 2], F32, name=f"wd_last{part}", offset=part * WD_PIECE_BYTES // 2, align_bytes=ALIGN
            )
            rows = wd[GROUP:, GROUP + part * GROUP // 2 : GROUP + (part + 1) * GROUP // 2]
            nc.sync.dma_start(raw[:], rows.rearrange("(p i) e -> p i e", i=PACK))
            last_raw.append(raw)

        def quantise_last(part, grouped):
            for pair in pairs:
                nc.vector.tensor_copy(
                    out=grouped[:].rearrange("p (t m i) -> p m i t", t=PACK, i=PACK)[:, :, :, pair],
                    in_=last_raw[part][:].rearrange("p i (m t) -> p m i t", t=PACK)[:, :, :, pair],
                )
            for t in range(PACK):
                first = GROUP + t * P + part * P // 2
                cols = slice(first, first + P // 2)
                nc.vector.quantize_mx(
                    out=wd_q[:, 1, cols].bitcast(FP8X4), scales=wd_s[:, 1, cols],
                    in_=grouped[:, t * GROUP // 2 : (t + 1) * GROUP // 2],
                )

        def quantise_wd(piece, grouped):
            b, a = divmod(piece, 2)
            cols = slice(b * GROUP, (b + 1) * GROUP)
            for pair in pairs:
                nc.vector.tensor_copy(
                    out=grouped[:].rearrange("p (t m i) -> p m i t", t=PACK, i=PACK)[:, :, :, pair],
                    in_=wd_raw[piece][:].rearrange("p i (m t) -> p m i t", t=PACK)[:, :, :, pair],
                )
            for pair in pairs:
                part = slice(cols.start + pair.start * P, cols.start + pair.stop * P)
                nc.vector.quantize_mx(
                    out=wd_q[:, a, part].bitcast(FP8X4), scales=wd_s[:, a, part],
                    in_=grouped[:, pair.start * GROUP : pair.stop * GROUP],
                )

        wd_bf = [keep.tile([P, PACK * GROUP], BF16, name=f"wd_bf{n}", tag=f"wd_bf{n}", align_bytes=ALIGN) for n in range(3)]
        deal_wc_words(1)
        quantise_wd(0, wd_bf[0])
        quantise_wd(1, wd_bf[1])
        quantise_wd(2, wd_bf[2])
        quantise_last(0, keep.tile([P, PACK * GROUP // 2], BF16, name="wd_bf3", align_bytes=ALIGN))
        quantise_last(1, turn.tile([P, PACK * GROUP // 2], BF16, name="wd_bf4", offset=0, align_bytes=ALIGN))

        def first_stage(bank, is_colour, b, voxels, ts, a):
            width = voxels.stop - voxels.start
            for t in ts:
                c0 = b * GROUP + t * P
                if is_colour:
                    lhs, lhs_scale = wc_q[:, a, 2 * c0 : 2 * (c0 + P)].bitcast(FP4X4), wc_s[b][:, a, t * P : (t + 1) * P]
                else:
                    lhs, lhs_scale = wd_q[:, a, c0 : c0 + P].bitcast(FP8X4), wd_s[:, a, c0 : c0 + P]
                nc.tensor.matmul_mx(
                    out=bank[:, (t - ts[0]) * width : (t - ts[0] + 1) * width], lhsT=lhs, lhsT_scale=lhs_scale,
                    rhs=v_w[a][:, voxels].bitcast(FP8X4), rhs_scale=v_s[a][:, voxels],
                    start=(a == 0 and t == ts[0]), stop=(a == 1 and t == ts[-1]),
                )

        whole = [(b, half, (t,)) for b in range(2) for half in halves for t in range(PACK)]
        colours = [(0, quarter, ts) for quarter in quarters for ts in ((0, 1), (2, 3))] + whole[PACK:]
        last = [(0, halves[1], (t,)) for t in range(VECTOR_GAINS)]
        densities = [d for d in whole[:BANKS] if d not in last]
        held = len(densities)
        densities = densities + [(1, half, (t,)) for t in range(PACK) for half in halves] + last
        turns = [(True, c) for c in colours] + [(False, d) for d in densities]
        dens = keep.tile([P, 2, S // RUN, PACK, RUN], F32, name="dens", align_bytes=ALIGN)
        col = [keep.tile([P, S // RUN, PACK, 2 * RUN], F32, name=f"col{b}", align_bytes=ALIGN) for b in range(2)]
        floor = keep.tile([P, 1], F32, name="floor")
        h_q = keep.tile([P, 2 * S], U32, name="h_q", align_bytes=ALIGN)
        h_s = keep.tile([P, 2 * S], U8, name="h_s", align_bytes=ALIGN)

        def runs(tile, voxels, t):
            return tile[:, voxels.start // RUN : voxels.stop // RUN, t, 0:RUN]

        def in_runs(bank):
            return bank[:].rearrange("p (c i) -> p c i", i=RUN)

        def gain(engine, factors, b, t, voxels=slice(0, S)):
            x = runs(col[b], voxels, t)
            engine.tensor_scalar(out=x, in0=x, scalar1=factors[0], scalar2=factors[1], op0=ALU.mult, op1=factors[2])

        for i, (is_colour, (b, voxels, ts)) in enumerate(turns[:BANKS]):
            first_stage(banks[i], is_colour, b, voxels, ts, 0)
        late_threshold = turn.tile([P, 1], F32, name="late_threshold", offset=0, align_bytes=ALIGN)
        threshold = late_threshold[:]
        nc.vector.memset(threshold, LINEAR_FROM)
        factors = turn.tile([P, 2, PACK], F32, name="factors", offset=ALIGN, align_bytes=ALIGN)
        nc.gpsimd.tensor_scalar(
            out=factors[:], in0=gains[:], scalar1=-1.0 / LINEAR_FROM, scalar2=0.0, op0=ALU.mult, op1=ALU.add,
        )
        for i, (is_colour, (b, voxels, ts)) in enumerate(turns):
            bank = banks[i % BANKS]
            for a in (1,) if i < BANKS else (0, 1):
                first_stage(bank, is_colour, b, voxels, ts, a)
            t = ts[0]
            if is_colour:
                target = col[b][:, voxels.start // RUN : voxels.stop // RUN, t : ts[-1] + 1, 0:RUN]
                nc.scalar.activation(
                    target.rearrange("p c t i -> p t c i"),
                    bank[:].rearrange("p (t c i) -> p t c i", t=len(ts), i=RUN),
                    ACT.Tanh,
                )
                if b == 0 and voxels == quarters[1]:
                    for t in range(ts[0], min(ts[-1] + 1, VECTOR_GAINS)):
                        gain(nc.vector, (gains[:, b, t : t + 1], -1.0 / LINEAR_FROM, ALU.mult), b, t, halves[0])
                if b == 1 and voxels == halves[1]:
                    gain(nc.gpsimd, (factors[:, b, t : t + 1], 0.0, ALU.add), b, t)
            else:
                nc.scalar.activation(runs(dens[:, b], voxels, t), in_runs(bank), ACT.Sigmoid, scale=-1.0)
                if i == len(turns) - 6:
                    nc.vector.tensor_scalar(
                        out=floor[:], in0=dens[:, b, voxels.start // RUN, t, 0:1],
                        scalar1=0.0, scalar2=LOG_FLOOR, op0=ALU.mult, op1=ALU.add,
                    )
                x = runs(col[b], voxels, t)
                nc.vector.scalar_tensor_tensor(
                    out=x, in0=in_runs(bank), scalar=threshold if i < len(colours) + held else LINEAR_FROM, in1=x, op0=ALU.max, op1=ALU.mult,
                )

        for t in range(VECTOR_GAINS, PACK):
            gain(nc.gpsimd, (factors[:, 0, t : t + 1], 0.0, ALU.add), 0, t)
        for t in range(VECTOR_GAINS):
            gain(nc.vector, (gains[:, 0, t : t + 1], -1.0 / LINEAR_FROM, ALU.mult), 0, t, halves[1])


        wr_q = keep.tile([P, 2, N], I32, name="wr_q", tag="wd_bf0", align_bytes=ALIGN)
        wr_s = stage.tile([P, 2, N // 4], I32, name="wr_s", offset=0, align_bytes=ALIGN)
        nc.sync.dma_start(wr_q[:], wr_words.rearrange("a p n i -> p a (n i)").bitcast(I32))
        nc.vector.memset(wr_s[:], 0)
        for r in range(4):
            nc.sync.dma_start(
                wr_s[r:P:32, :, :],
                wr_scales[:, r:16:4, :].rearrange("a r n -> r a n").bitcast(I32),
            )

        def all_products(tile, voxels):
            return tile[:, voxels.start // RUN : voxels.stop // RUN, :, :].rearrange("p c t i -> p (c t) i")

        steps = []
        for width in STEPS:
            first = steps[-1].stop if steps else 0
            steps.append(slice(first, first + width))

        def parts(b, voxels):
            if steps.index(voxels) == 1 and b == 0:
                cuts = [voxels.start + c for c in (0, 64, 128, 256)]
                return [slice(lo, hi) for lo, hi in zip(cuts, cuts[1:])]
            if 2 * steps.index(voxels) + b < HALVED:
                middle = (voxels.start + voxels.stop) // 2
                return [slice(voxels.start, middle), slice(middle, voxels.stop)]
            return [voxels]

        def logarithms(voxels):
            for b in range(2):
                for part in parts(b, voxels):
                    x = all_products(dens[:, b], part)
                    nc.scalar.activation(x, x, ACT.Ln, bias=floor[:])

        for voxels in steps[:LOGS_AHEAD]:
            logarithms(voxels)

        result = keep.tile([P, N // P, S], F32, name="result")
        out_v = out.rearrange("(n p) j -> p n j", p=P)

        def hidden(h_bf, b, voxels, which=slice(None)):
            for part in parts(b, voxels)[which]:
                local = slice(part.start - voxels.start, part.stop - voxels.start)
                nc.vector.scalar_tensor_tensor(
                    out=h_bf[:, b, :].rearrange("p (i x) -> p x i", i=RUN)[:, local, :],
                    in0=all_products(dens[:, b], part),
                    scalar=-LINEAR_FROM,
                    in1=all_products(col[b], part)[:, :, 0:RUN],
                    op0=ALU.max, op1=ALU.mult,
                )

        def h_columns(voxels, b):
            width = voxels.stop - voxels.start
            return slice(2 * voxels.start + b * width, 2 * voxels.start + (b + 1) * width)

        def radiance_pass(dst, n, b, voxels):
            rows = slice(n * P, (n + 1) * P)
            nc.tensor.matmul_mx(
                out=dst,
                lhsT=wr_q[:, b, rows].bitcast(FP8X4),
                lhsT_scale=wr_s[:, b, :].bitcast(U8)[:, rows],
                rhs=h_q[:, h_columns(voxels, b)].bitcast(FP8X4), rhs_scale=h_s[:, h_columns(voxels, b)],
                start=(b == 0), stop=(b == 1),
            )

        def finish(step, h_bf):
            voxels = steps[step]
            width = voxels.stop - voxels.start
            both = slice(2 * voxels.start, 2 * voxels.stop)
            nc.vector.quantize_mx(
                out=h_q[:, both].bitcast(FP8X4), scales=h_s[:, both], in_=h_bf[:].rearrange("p b x -> p (b x)")
            )
            per_bank = HALF // width
            for n0 in range(0, N // P, per_bank):
                count = min(per_bank, N // P - n0)
                bank = banks[LAST_BANKS + (2 * step + n0 // per_bank) % (BANKS - LAST_BANKS)]
                for n in range(n0, n0 + count):
                    for b in range(2):
                        radiance_pass(bank[:, (n - n0) * width : (n - n0 + 1) * width], n, b, voxels)
                nc.scalar.copy(
                    result[:, n0 : n0 + count, voxels].rearrange("p n (c i) -> p n c i", i=RUN),
                    bank[:, 0 : count * width].rearrange("p (n i c) -> p n c i", n=count, i=RUN),
                )
            nc.sync.dma_start(out_v[:, :, voxels], result[:, :, voxels])

        def finish_last(voxels, h_bf):
            width = voxels.stop - voxels.start
            for b in range(2):
                nc.vector.quantize_mx(
                    out=h_q[:, h_columns(voxels, b)].bitcast(FP8X4),
                    scales=h_s[:, h_columns(voxels, b)],
                    in_=h_bf[:, b, :],
                )
                for n in range(LAST_BANKS):
                    radiance_pass(banks[n][:, 0:width], n, b, voxels)
            for n, copy in enumerate((nc.vector.tensor_copy, nc.vector.tensor_copy, nc.scalar.copy)):
                copy(
                    result[:, n, voxels].rearrange("p (c i) -> p c i", i=RUN),
                    banks[n][:, 0:width].rearrange("p (i c) -> p c i", i=RUN),
                )
                nc.sync.dma_start(out_v[:, n, voxels], result[:, n, voxels])

        pending = None
        for step, voxels in enumerate(steps):
            h_bf = late.tile(
                [P, 2, PACK * (voxels.stop - voxels.start)], BF16, name=f"h_bf{step}",
                offset=4 * PACK * voxels.start, align_bytes=ALIGN,
            )
            hidden(h_bf, 0, voxels, slice(0, 1))
            if pending is not None:
                finish(*pending)
                for later in {1: steps[3:4], 2: steps[4:]}.get(step, []):
                    logarithms(later)
            hidden(h_bf, 0, voxels, slice(1, None))
            hidden(h_bf, 1, voxels)
            pending = (step, h_bf)
        finish_last(steps[-1], h_bf)
